import numpy as np
import ml_dtypes


def mxq(x, axis, fmt="e4m3"):
    dtype, down = {"e4m3": (ml_dtypes.float8_e4m3fn, 7), "e5m2": (ml_dtypes.float8_e5m2, 14)}[fmt]
    v = np.moveaxis(np.asarray(x, np.float32).astype(ml_dtypes.bfloat16).astype(np.float64), axis, -1)
    blocks = v.reshape(v.shape[:-1] + (-1, 32))
    amax = np.abs(blocks).max(-1, keepdims=True)
    byte = np.maximum(np.where(amax > 0, np.frexp(amax)[1] - 1 + 127, 0) - down, 1)
    scale = np.exp2(byte - 127.0)
    codes = (blocks / scale).astype(np.float32).astype(dtype).astype(np.float64)
    return np.moveaxis((codes * scale).reshape(v.shape), -1, axis)


WIDE = False


def mx_kscale(k):
    if not WIDE:
        return np.ones(k)
    levels = np.array([10, -10, 5, -5, 0])
    if k % 512:
        return np.exp2(np.random.permutation(np.resize(levels, k // 32))).repeat(32)
    a = np.empty((k // 512, 16))
    for p in range(k // 512):
        a[p, :8] = np.random.permutation(np.resize(levels, 8))
        for g in range(8):
            far = levels[np.abs(levels - a[p, g]) >= 10]
            a[p, g + 8] = far[np.random.randint(len(far))]
    return np.exp2(a.ravel()).repeat(32)


def f64(x):
    return np.asarray(x).astype(np.float64)


def striped(idx):
    return np.tile(idx.reshape(-1, 16).T, (8, 1)).astype(np.uint16)


def unstriped(offs):
    return offs[:16].T.reshape(-1).astype(np.int64)


E2M1 = np.array([0.0, 0.5, 1.0, 1.5, 2.0, 3.0, 4.0, 6.0, -0.0, -0.5, -1.0, -1.5, -2.0, -3.0, -4.0, -6.0])


def pack_weight(w, fmt):
    k, n = w.shape
    w = f64(np.asarray(w, np.float32).astype(ml_dtypes.bfloat16)).reshape(k // 32, 32, n)
    amax = np.abs(w).max(1)
    if fmt == "e4m3":
        byte = np.frexp(amax)[1] - 1 + 127 - 7
    else:
        mant, ex = np.frexp(amax / 6.0)
        byte = np.where(mant > 0.5, ex, ex - 1) + 127
    byte = np.clip(np.where(amax > 0, byte, 1), 1, 254)
    scaled = (w * np.exp2(127.0 - byte)[:, None, :]).reshape(k, n).astype(np.float32)
    by_word = np.ascontiguousarray(scaled.reshape(k // 512, 128, 4, n).transpose(0, 1, 3, 2))
    if fmt == "e4m3":
        words = by_word.astype(ml_dtypes.float8_e4m3fn).view(np.uint8)
    else:
        c = by_word.astype(ml_dtypes.float4_e2m1fn).view(np.uint8) & 0xF
        words = (c[..., 0::2] | (c[..., 1::2] << 4)).reshape(k // 512, 128, 2 * n)
    return np.ascontiguousarray(words), np.ascontiguousarray(byte.astype(np.uint8).reshape(k // 512, 16, n))


def unpack_weight(words, scales, fmt):
    g, _, n = scales.shape
    words = np.ascontiguousarray(words).reshape(g, 128, n, -1)
    if fmt == "e4m3":
        vals = words.view(ml_dtypes.float8_e4m3fn).astype(np.float64)
    else:
        nib = np.empty((g, 128, n, 4), np.uint8)
        nib[..., 0::2] = words & 0xF
        nib[..., 1::2] = words >> 4
        vals = E2M1[nib]
    vals = vals * np.repeat(np.exp2(scales.astype(np.float64) - 127.0), 8, axis=1)[..., None]
    return vals.transpose(0, 1, 3, 2).reshape(g * 512, n)


def gelu(v):
    return 0.5 * v * (1.0 + np.tanh(np.sqrt(2.0 / np.pi) * (v + 0.044715 * v**3)))


K, H, N, T, T2, S = 512, 1024, 384, 2048, 2048, 1024

def setup_inputs():
    n = np.random.standard_normal
    s = mx_kscale(K)[:, None]
    u = mx_kscale(H)[:, None]
    tab_words, tab_scales = pack_weight(n((K, T)) * s, "e4m3")
    xT = (np.round(16 * n((K, T2))) / 16 * s).astype(np.float32)
    w1_words, w1_scales = pack_weight(n((K, H)) / np.sqrt(K) / s * u.T, "e2m1")
    w2 = (n((K, H)) / np.sqrt(2 * K) / s * u.T).astype(np.float32)
    b1 = (0.5 * n(H) * u[:, 0]).astype(np.float32)
    w3_words, w3_scales = pack_weight(n((H, N)) / np.sqrt(H) / u, "e4m3")
    w4 = (n((H, N)) / np.sqrt(H) / u).astype(np.float32)
    return {"tab_words": tab_words, "tab_scales": tab_scales,
            "offs": striped(np.random.permutation(T)[:S]),
            "xT": xT,
            "offs2": striped(np.random.permutation(T2)[:S]),
            "offs3": striped(np.random.permutation(T2)[:S]),
            "w1_words": w1_words, "w1_scales": w1_scales,
            "w2": w2, "b1": b1,
            "w3_words": w3_words, "w3_scales": w3_scales, "w4": w4}

def reference(tab_words, tab_scales, offs, xT, offs2, offs3, w1_words, w1_scales, w2, b1, w3_words, w3_scales, w4):
    v = unpack_weight(tab_words, tab_scales, "e4m3")[:, unstriped(offs)]
    x = f64(xT)[:, unstriped(offs2)] - f64(xT)[:, unstriped(offs3)]
    a = (unpack_weight(w1_words, w1_scales, "e2m1").T @ v) + f64(b1)[:, None]
    b = mxq(f64(w2), 0, "e4m3").T @ mxq(x, 0, "e4m3")
    hi = np.maximum(a, b)
    lo = np.minimum(a, b)
    y3 = unpack_weight(w3_words, w3_scales, "e4m3").T @ mxq(hi, 0, "e4m3")
    y4 = mxq(f64(w4), 0, "e4m3").T @ mxq(lo, 0, "e4m3")
    return y3 * y4

@@ -1,0 +1,272 @@
+from contextlib import ExitStack
+
+import concourse.mybir as mybir
+
+K, H, N, T, S = 512, 1024, 384, 2048, 1024
+FLOPS = 2 * K * H * S * 2 + 2 * H * N * S * 2
+
+F32 = mybir.dt.float32
+BF16 = mybir.dt.bfloat16
+I32 = mybir.dt.int32
+U32 = mybir.dt.uint32
+U16 = mybir.dt.uint16
+U8 = mybir.dt.uint8
+E4M3 = mybir.dt.float8_e4m3fn_x4
+E2M1 = mybir.dt.float4_e2m1fn_x4
+ALU = mybir.AluOpType
+IDENTITY = mybir.ActivationFunctionType.Identity
+
+P = 128
+PACK = 4
+PASS = P * PACK
+G = H // PASS
+HALF = 512
+CHUNK = 256
+NT = N // P
+LIST_ROWS = 16
+
+
+def tile_list_calving_retreat_features_kernel(
+    tc, tab_words, tab_scales, offs, xT, offs2, offs3, w1_words, w1_scales, w2, b1, w3_words, w3_scales, w4, out
+):
+    nc = tc.nc
+    with ExitStack() as ctx:
+        keep = ctx.enter_context(tc.tile_pool(name="keep", bufs=1))
+        ring = ctx.enter_context(tc.tile_pool(name="ring", bufs=2))
+        psum = ctx.enter_context(tc.psum_pool(name="psum", bufs=2))
+
+        idx = keep.tile([P, S // LIST_ROWS], U16, name="idx")
+        idx2 = keep.tile([P, S // LIST_ROWS], U16, name="idx2")
+        idx3 = keep.tile([P, S // LIST_ROWS], U16, name="idx3")
+        tab_w = keep.tile([P, T], I32, name="tab_w", align_bytes=64)
+        tab_s = keep.tile([P, T], U8, name="tab_s", align_bytes=64)
+        w1_raw = keep.tile([P, 2 * H], U8, name="w1_raw", align_bytes=64)
+        w1s_raw = keep.tile([P, H], U8, name="w1s_raw", align_bytes=64)
+        w1_w = keep.tile([P, 2 * H], U8, name="w1_w", align_bytes=64)
+        w1_s = keep.tile([P, H], U8, name="w1_s", align_bytes=64)
+        bias = keep.tile([P, G, PACK], F32, name="bias")
+        w3_w = keep.tile([P, G, N], I32, name="w3_w", align_bytes=64)
+        w3_s = keep.tile([P, G * N], U8, name="w3_s", align_bytes=64)
+        x_plane = [keep.tile([P, T], F32, name=f"x_plane{t}") for t in range(PACK)]
+        w2_raw = [keep.tile([P, PACK, PASS], F32, name=f"w2_raw{g}") for g in range(G)]
+        w4_raw = [keep.tile([P, PACK, N], F32, name=f"w4_raw{g}") for g in range(G)]
+        w2_w = [keep.tile([P, PASS], U32, name=f"w2_w{g}", align_bytes=64) for g in range(G)]
+        w2_s = [keep.tile([P, PASS], U8, name=f"w2_s{g}", align_bytes=64) for g in range(G)]
+        w4_w = keep.tile([P, G * N], U32, name="w4_w", align_bytes=64)
+        w4_s = keep.tile([P, G * N], U8, name="w4_s", align_bytes=64)
+
+        def load_scale_rows(queue, plane, rows):
+            for q in range(4):
+                queue.dma_start(out=plane[32 * q : 32 * q + 4], in_=rows(q))
+
+        x_rows = xT.rearrange("(p t) c -> p t c", t=PACK)
+        w2_rows = w2.rearrange("(p t) r -> p t r", t=PACK)
+
+        nc.vector.memset(tab_s[:].bitcast(I32), 0)
+        nc.vector.memset(w1s_raw[:].bitcast(I32), 0)
+        nc.sync.dma_start(idx[:], offs)
+        nc.sync.dma_start(out=w1_raw[:].bitcast(I32), in_=w1_words[0].bitcast(I32))
+        nc.sync.dma_start(out=tab_w[:], in_=tab_words[0].rearrange("p c i -> p (c i)").bitcast(I32))
+        load_scale_rows(nc.scalar, tab_s[:].bitcast(I32), lambda q: tab_scales[0, 4 * q : 4 * q + 4, :].bitcast(I32))
+        load_scale_rows(nc.scalar, w1s_raw[:].bitcast(I32), lambda q: w1_scales[0, 4 * q : 4 * q + 4, :].bitcast(I32))
+        nc.sync.dma_start(out=w2_raw[0][:], in_=w2_rows[:, :, 0:PASS])
+        nc.sync.dma_start(out=bias[:], in_=b1.rearrange("(g p t) -> p g t", g=G, t=PACK))
+        nc.sync.dma_start(idx3[:], offs3)
+        nc.sync.dma_start(idx2[:], offs2)
+        for t in range(PACK):
+            nc.sync.dma_start(out=x_plane[t][:], in_=x_rows[:, t, :])
+        nc.sync.dma_start(out=w2_raw[1][:], in_=w2_rows[:, :, PASS : 2 * PASS])
+        nc.gpsimd.memset(w3_s[:].bitcast(I32), 0)
+        load_scale_rows(
+            nc.sync,
+            w3_s[:].bitcast(I32).rearrange("p (g n) -> p g n", g=G),
+            lambda q: w3_scales[:, 4 * q : 4 * q + 4, :].bitcast(I32).rearrange("g r n -> r g n"),
+        )
+        nc.sync.dma_start(out=w3_w[:], in_=w3_words.rearrange("g p n i -> p g (n i)").bitcast(I32))
+        for g in range(G):
+            nc.sync.dma_start(
+                out=w4_raw[g][:], in_=w4[g * PASS : (g + 1) * PASS, :].rearrange("(p t) n -> p t n", t=PACK)
+            )
+
+        def offsets(tile, h):
+            cols = HALF // LIST_ROWS
+            return tile[:, h * cols : (h + 1) * cols]
+
+        def gather_table(h):
+            v_w = ring.tile([P, HALF], U32, name="v_w", align_bytes=64)
+            v_s = ring.tile([P, HALF], U8, name="v_s", align_bytes=64)
+            nc.vector.tensor_copy(v_w[:], tab_w[:].bitcast(U32).indirect(offsets(idx, h)))
+            nc.vector.tensor_copy(v_s[:], tab_s[:].indirect(offsets(idx, h)))
+            return v_w, v_s
+
+        def make_a(v):
+            v_w, v_s = v
+            a_bf = ring.tile([P, 2, HALF // CHUNK, G, CHUNK, 2], BF16, name="a_bf")
+            for g in range(G):
+                for t in range(PACK):
+                    col = g * PASS + t * P
+                    bank = psum.tile([P, HALF], F32, name="a_bank")
+                    nc.tensor.matmul_mx(
+                        out=bank[:],
+                        lhsT=w1_w[:, 2 * col : 2 * (col + P)].bitcast(E2M1),
+                        lhsT_scale=w1_s[:, col : col + P],
+                        rhs=v_w[:].bitcast(E4M3),
+                        rhs_scale=v_s[:],
+                        start=True,
+                        stop=True,
+                    )
+                    nc.scalar.activation(
+                        out=a_bf[:, t // 2, :, g, :, t % 2],
+                        in_=bank[:].rearrange("p (c n) -> p c n", n=CHUNK),
+                        func=IDENTITY,
+                        bias=bias[:, g, t : t + 1],
+                    )
+            return a_bf
+
+        def round_w2(g, tag):
+            staged = keep.tile([P, PACK * PASS], BF16, name=f"w2_bf{g}", tag=tag, align_bytes=64)
+            nc.scalar.copy(
+                out=staged[:].rearrange("p (t m j) -> p m j t", t=PACK, j=PACK),
+                in_=w2_raw[g][:].rearrange("p j (m t) -> p m j t", t=PACK),
+            )
+            nc.vector.quantize_mx(out=w2_w[g][:].bitcast(E4M3), scales=w2_s[g][:], in_=staged[:])
+
+        def gather_x(h, tag):
+            before = keep.tile([P, PACK, HALF], F32, name=f"before{h}", tag="before")
+            change = keep.tile([P, PACK, HALF], F32, name=f"change{h}", tag=tag, align_bytes=64)
+            for t in range(PACK):
+                nc.vector.tensor_copy(before[:, t, :], x_plane[t][:].indirect(offsets(idx3, h)))
+                nc.vector.tensor_tensor(
+                    change[:, t, :], x_plane[t][:].indirect(offsets(idx2, h)), before[:, t, :], ALU.subtract
+                )
+            return change
+
+        def quantize_x(change):
+            x_bf = ring.tile([P, HALF * PACK], BF16, name="x_bf", align_bytes=64)
+            x_w = ring.tile([P, HALF], U32, name="x_w", align_bytes=64)
+            x_s = ring.tile([P, HALF], U8, name="x_s", align_bytes=64)
+            nc.scalar.copy(
+                out=x_bf[:].rearrange("p (c i t) -> p c t i", i=4, t=PACK),
+                in_=change[:].rearrange("p t (c i) -> p c t i", i=4),
+            )
+            nc.vector.quantize_mx(out=x_w[:].bitcast(E4M3), scales=x_s[:], in_=x_bf[:])
+            return x_w, x_s
+
+        def make_b(x, c):
+            x_w, x_s = x
+            b_bf = ring.tile([P, G, CHUNK, PACK], BF16, name="b_bf")
+            for g in range(G):
+                for j in range(0, CHUNK, P):
+                    tokens = slice(c * CHUNK + j, c * CHUNK + j + P)
+                    bank = psum.tile([P, PACK, P], F32, name="b_bank")
+                    for t in range(PACK):
+                        nc.tensor.matmul_mx(
+                            out=bank[:, t, :],
+                            lhsT=w2_w[g][:, t * P : (t + 1) * P].bitcast(E4M3),
+                            lhsT_scale=w2_s[g][:, t * P : (t + 1) * P],
+                            rhs=x_w[:, tokens].bitcast(E4M3),
+                            rhs_scale=x_s[:, tokens],
+                            start=True,
+                            stop=True,
+                        )
+                    nc.scalar.copy(out=b_bf[:, g, j : j + P, :], in_=bank[:].rearrange("p t n -> p n t"))
+            return b_bf
+
+        def envelopes(a_bf, b_bf, c):
+            made = []
+            staged = []
+            for name, op in (("hi", ALU.max), ("lo", ALU.min)):
+                env = ring.tile([P, G * CHUNK * PACK], BF16, name=f"{name}_bf", align_bytes=64)
+                nc.vector.tensor_tensor(
+                    env[:].rearrange("p (n u e) -> p n u e", u=2, e=2),
+                    a_bf[:, :, c].rearrange("p u g n e -> p (g n) u e"),
+                    b_bf[:].rearrange("p g n (u e) -> p (g n) u e", u=2),
+                    op,
+                )
+                staged.append((name, env))
+            for name, env in staged:
+                env_w = ring.tile([P, G * CHUNK], U32, name=f"{name}_w", align_bytes=64)
+                env_s = ring.tile([P, G * CHUNK], U8, name=f"{name}_s", align_bytes=64)
+                nc.vector.quantize_mx(out=env_w[:].bitcast(E4M3), scales=env_s[:], in_=env[:])
+                made.append((env_w, env_s))
+            return made
+
+        def round_w4(tag):
+            staged = keep.tile([P, G * N * PACK], BF16, name="w4_bf", tag=tag, align_bytes=64)
+            for g in range(G):
+                nc.vector.tensor_copy(
+                    out=staged[:, g * N * PACK : (g + 1) * N * PACK].rearrange("p (c i t) -> p c t i", i=4, t=PACK),
+                    in_=w4_raw[g][:].rearrange("p t (c i) -> p c t i", i=4),
+                )
+            for lo, hi in ((0, 512), (512, G * N)):
+                nc.vector.quantize_mx(
+                    out=w4_w[:, lo:hi].bitcast(E4M3), scales=w4_s[:, lo:hi], in_=staged[:, lo * PACK : hi * PACK]
+                )
+
+        def project(name, weight, weight_s, env, n):
+            env_w, env_s = env
+            bank = psum.tile([P, CHUNK], F32, name=name)
+            for g in range(G):
+                cols = slice(g * N + n * P, g * N + (n + 1) * P)
+                tokens = slice(g * CHUNK, (g + 1) * CHUNK)
+                nc.tensor.matmul_mx(
+                    out=bank[:],
+                    lhsT=weight[:, cols].bitcast(E4M3),
+                    lhsT_scale=weight_s[:, cols],
+                    rhs=env_w[:, tokens].bitcast(E4M3),
+                    rhs_scale=env_s[:, tokens],
+                    start=(g == 0),
+                    stop=(g == G - 1),
+                )
+            return bank
+
+        w3_flat = w3_w[:].rearrange("p g n -> p (g n)")
+
+        def upper(env):
+            y3 = ring.tile([P, NT, CHUNK], F32, name="y3")
+            for n in range(NT):
+                bank = project("y3_bank", w3_flat, w3_s, env[0], n)
+                nc.scalar.copy(out=y3[:, n, :], in_=bank[:])
+            return y3
+
+        def finish(env, y3, chunk):
+            for n in range(NT):
+                bank = project("y4_bank", w4_w, w4_s, env[1], n)
+                res = ring.tile([P, CHUNK], F32, name="res", bufs=4)
+                nc.vector.tensor_tensor(res[:], bank[:], y3[:, n, :], ALU.mult)
+                nc.sync.dma_start(out=out[n * P : (n + 1) * P, chunk * CHUNK : (chunk + 1) * CHUNK], in_=res[:])
+
+        nc.vector.tensor_copy(
+            out=w1_w[:].bitcast(U16).rearrange("p (g t m) -> p g t m", g=G, t=PACK),
+            in_=w1_raw[:].bitcast(U16).rearrange("p (g m t) -> p g t m", g=G, t=PACK),
+        )
+        v0 = gather_table(0)
+        nc.vector.tensor_copy(
+            out=w1_s[:].rearrange("p (g t m) -> p g t m", g=G, t=PACK),
+            in_=w1s_raw[:].rearrange("p (g m t) -> p g t m", g=G, t=PACK),
+        )
+        round_w2(0, "w2_bf0")
+        a0 = make_a(v0)
+        v1 = gather_table(1)
+        x0 = quantize_x(gather_x(0, "change0"))
+        round_w2(1, "chain")
+        change1 = gather_x(1, "chain")
+        b0 = make_b(x0, 0)
+        b1_ = make_b(x0, 1)
+        env0 = envelopes(a0, b0, 0)
+        y30 = upper(env0)
+        x1 = quantize_x(change1)
+        env1 = envelopes(a0, b1_, 1)
+        round_w4("chain")
+        a1 = make_a(v1)
+        finish(env0, y30, 0)
+        b2 = make_b(x1, 0)
+        y31 = upper(env1)
+        finish(env1, y31, 1)
+        b3 = make_b(x1, 1)
+        env2 = envelopes(a1, b2, 0)
+        y32 = upper(env2)
+        env3 = envelopes(a1, b3, 1)
+        finish(env2, y32, 2)
+        y33 = upper(env3)
+        finish(env3, y33, 3)

@@ -33,6 +33,7 @@ def tile_list_calving_retreat_features_kernel(
     with ExitStack() as ctx:
         keep = ctx.enter_context(tc.tile_pool(name="keep", bufs=1))
         ring = ctx.enter_context(tc.tile_pool(name="ring", bufs=2))
+        reuse = ctx.enter_context(tc.tile_pool(name="reuse", bufs=1))
         psum = ctx.enter_context(tc.psum_pool(name="psum", bufs=2))
 
         idx = keep.tile([P, S // LIST_ROWS], U16, name="idx")
@@ -48,16 +49,18 @@ def tile_list_calving_retreat_features_kernel(
         w3_w = keep.tile([P, G, N], I32, name="w3_w", align_bytes=64)
         w3_s = keep.tile([P, G * N], U8, name="w3_s", align_bytes=64)
         x_plane = [keep.tile([P, T], F32, name=f"x_plane{t}") for t in range(PACK)]
-        w2_raw = [keep.tile([P, PACK, PASS], F32, name=f"w2_raw{g}") for g in range(G)]
+        w2_raw = [keep.tile([P, PACK, PASS], F32, name=f"w2_raw{g}", tag=f"w2_raw{g}") for g in range(G)]
         w4_raw = [keep.tile([P, PACK, N], F32, name=f"w4_raw{g}") for g in range(G)]
-        w2_w = [keep.tile([P, PASS], U32, name=f"w2_w{g}", align_bytes=64) for g in range(G)]
-        w2_s = [keep.tile([P, PASS], U8, name=f"w2_s{g}", align_bytes=64) for g in range(G)]
+        before = [
+            reuse.tile([P, PACK, HALF], F32, name="before0", align_bytes=64, offset=0),
+            keep.tile([P, PACK, HALF], F32, name="before1"),
+        ]
+        w2_s = keep.tile([P, H], U8, name="w2_s", align_bytes=64)
         w4_w = keep.tile([P, G * N], U32, name="w4_w", align_bytes=64)
         w4_s = keep.tile([P, G * N], U8, name="w4_s", align_bytes=64)
 
-        def load_scale_rows(queue, plane, rows):
-            for q in range(4):
-                queue.dma_start(out=plane[32 * q : 32 * q + 4], in_=rows(q))
+        def load_scale_rows(plane, rows, q):
+            nc.sync.dma_start(out=plane[32 * q : 32 * q + 4], in_=rows[4 * q : 4 * q + 4])
 
         x_rows = xT.rearrange("(p t) c -> p t c", t=PACK)
         w2_rows = w2.rearrange("(p t) r -> p t r", t=PACK)
@@ -66,52 +69,55 @@ def tile_list_calving_retreat_features_kernel(
         nc.vector.memset(w1s_raw[:].bitcast(I32), 0)
         nc.sync.dma_start(idx[:], offs)
         nc.sync.dma_start(out=w1_raw[:].bitcast(I32), in_=w1_words[0].bitcast(I32))
+        for q in range(4):
+            load_scale_rows(tab_s[:].bitcast(I32), tab_scales[0].bitcast(I32), q)
+        load_scale_rows(w1s_raw[:].bitcast(I32), w1_scales[0].bitcast(I32), 0)
         nc.sync.dma_start(out=tab_w[:], in_=tab_words[0].rearrange("p c i -> p (c i)").bitcast(I32))
-        load_scale_rows(nc.scalar, tab_s[:].bitcast(I32), lambda q: tab_scales[0, 4 * q : 4 * q + 4, :].bitcast(I32))
-        load_scale_rows(nc.scalar, w1s_raw[:].bitcast(I32), lambda q: w1_scales[0, 4 * q : 4 * q + 4, :].bitcast(I32))
-        nc.sync.dma_start(out=w2_raw[0][:], in_=w2_rows[:, :, 0:PASS])
+        for q in range(1, 4):
+            load_scale_rows(w1s_raw[:].bitcast(I32), w1_scales[0].bitcast(I32), q)
         nc.sync.dma_start(out=bias[:], in_=b1.rearrange("(g p t) -> p g t", g=G, t=PACK))
+        nc.sync.dma_start(out=x_plane[0][:], in_=x_rows[:, 0, :])
         nc.sync.dma_start(idx3[:], offs3)
         nc.sync.dma_start(idx2[:], offs2)
-        for t in range(PACK):
+        nc.sync.dma_start(out=w2_raw[0][:], in_=w2_rows[:, :, 0:PASS])
+        for t in range(1, PACK - 1):
             nc.sync.dma_start(out=x_plane[t][:], in_=x_rows[:, t, :])
         nc.sync.dma_start(out=w2_raw[1][:], in_=w2_rows[:, :, PASS : 2 * PASS])
+        nc.sync.dma_start(out=x_plane[PACK - 1][:], in_=x_rows[:, PACK - 1, :])
         nc.gpsimd.memset(w3_s[:].bitcast(I32), 0)
-        load_scale_rows(
-            nc.sync,
-            w3_s[:].bitcast(I32).rearrange("p (g n) -> p g n", g=G),
-            lambda q: w3_scales[:, 4 * q : 4 * q + 4, :].bitcast(I32).rearrange("g r n -> r g n"),
-        )
+        for q in range(4):
+            load_scale_rows(
+                w3_s[:].bitcast(I32).rearrange("p (g n) -> p g n", g=G),
+                w3_scales.bitcast(I32).rearrange("g r n -> r g n"),
+                q,
+            )
         nc.sync.dma_start(out=w3_w[:], in_=w3_words.rearrange("g p n i -> p g (n i)").bitcast(I32))
         for g in range(G):
             nc.sync.dma_start(
                 out=w4_raw[g][:], in_=w4[g * PASS : (g + 1) * PASS, :].rearrange("(p t) n -> p t n", t=PACK)
             )
 
-        def offsets(tile, h):
-            cols = HALF // LIST_ROWS
-            return tile[:, h * cols : (h + 1) * cols]
+        def offsets(tile, start, count):
+            return tile[:, start // LIST_ROWS : (start + count) // LIST_ROWS]
 
         def gather_table(h):
             v_w = ring.tile([P, HALF], U32, name="v_w", align_bytes=64)
-            v_s = ring.tile([P, HALF], U8, name="v_s", align_bytes=64)
-            nc.vector.tensor_copy(v_w[:], tab_w[:].bitcast(U32).indirect(offsets(idx, h)))
-            nc.vector.tensor_copy(v_s[:], tab_s[:].indirect(offsets(idx, h)))
-            return v_w, v_s
+            nc.vector.tensor_copy(v_w[:], tab_w[:].bitcast(U32).indirect(offsets(idx, h * HALF, HALF)))
+            return v_w, v_s[:, h * HALF : (h + 1) * HALF]
 
-        def make_a(v):
+        def make_a(v, tag):
             v_w, v_s = v
-            a_bf = ring.tile([P, 2, HALF // CHUNK, G, CHUNK, 2], BF16, name="a_bf")
+            a_bf = keep.tile([P, 2, HALF // CHUNK, G, CHUNK, 2], BF16, name="a_bf", tag=tag)
             for g in range(G):
                 for t in range(PACK):
                     col = g * PASS + t * P
-                    bank = psum.tile([P, HALF], F32, name="a_bank")
+                    bank = psum.tile([P, HALF], F32, name="a_bank", tag="ay", bufs=3)
                     nc.tensor.matmul_mx(
                         out=bank[:],
                         lhsT=w1_w[:, 2 * col : 2 * (col + P)].bitcast(E2M1),
                         lhsT_scale=w1_s[:, col : col + P],
                         rhs=v_w[:].bitcast(E4M3),
-                        rhs_scale=v_s[:],
+                        rhs_scale=v_s,
                         start=True,
                         stop=True,
                     )
@@ -123,47 +129,48 @@ def tile_list_calving_retreat_features_kernel(
                     )
             return a_bf
 
-        def round_w2(g, tag):
-            staged = keep.tile([P, PACK * PASS], BF16, name=f"w2_bf{g}", tag=tag, align_bytes=64)
+        def round_w2(staged, g):
             nc.scalar.copy(
-                out=staged[:].rearrange("p (t m j) -> p m j t", t=PACK, j=PACK),
+                out=staged[:, g * PACK * PASS : (g + 1) * PACK * PASS].rearrange("p (t m j) -> p m j t", t=PACK, j=PACK),
                 in_=w2_raw[g][:].rearrange("p j (m t) -> p m j t", t=PACK),
             )
-            nc.vector.quantize_mx(out=w2_w[g][:].bitcast(E4M3), scales=w2_s[g][:], in_=staged[:])
 
-        def gather_x(h, tag):
-            before = keep.tile([P, PACK, HALF], F32, name=f"before{h}", tag="before")
-            change = keep.tile([P, PACK, HALF], F32, name=f"change{h}", tag=tag, align_bytes=64)
-            for t in range(PACK):
-                nc.vector.tensor_copy(before[:, t, :], x_plane[t][:].indirect(offsets(idx3, h)))
-                nc.vector.tensor_tensor(
-                    change[:, t, :], x_plane[t][:].indirect(offsets(idx2, h)), before[:, t, :], ALU.subtract
-                )
-            return change
+        def gather_before(h, t):
+            nc.vector.tensor_copy(before[h][:, t, :], x_plane[t][:].indirect(offsets(idx3, h * HALF, HALF)))
 
-        def quantize_x(change):
-            x_bf = ring.tile([P, HALF * PACK], BF16, name="x_bf", align_bytes=64)
-            x_w = ring.tile([P, HALF], U32, name="x_w", align_bytes=64)
-            x_s = ring.tile([P, HALF], U8, name="x_s", align_bytes=64)
+        def gather_change(change, start, t):
+            width = change.shape[2]
+            h, j = divmod(start, HALF)
+            picked = x_plane[t][:].indirect(offsets(idx2, start, width))
+            nc.vector.tensor_tensor(change[:, t, :], picked, before[h][:, t, j : j + width], ALU.subtract)
+
+        def round_x(change, tag):
+            x_bf = keep.tile([P, change.shape[2] * PACK], BF16, name="x_bf", tag=tag, align_bytes=64)
             nc.scalar.copy(
                 out=x_bf[:].rearrange("p (c i t) -> p c t i", i=4, t=PACK),
-                in_=change[:].rearrange("p t (c i) -> p c t i", i=4),
+                in_=change.rearrange("p t (c i) -> p c t i", i=4),
             )
-            nc.vector.quantize_mx(out=x_w[:].bitcast(E4M3), scales=x_s[:], in_=x_bf[:])
+            return x_bf
+
+        def quantize_x(x_bf, tag):
+            width = x_bf.shape[1] // PACK
+            x_w = keep.tile([P, width], U32, name="x_w", tag=tag, align_bytes=64)
+            x_s = ring.tile([P, width], U8, name="x_s", align_bytes=64, bufs=4)
+            nc.vector.quantize_mx(out=x_w[:].bitcast(E4M3), scales=x_s[:], in_=x_bf)
             return x_w, x_s
 
         def make_b(x, c):
             x_w, x_s = x
-            b_bf = ring.tile([P, G, CHUNK, PACK], BF16, name="b_bf")
+            b_bf = ring.tile([P, G, CHUNK, PACK], BF16, name="b_bf", bufs=3)
             for g in range(G):
                 for j in range(0, CHUNK, P):
                     tokens = slice(c * CHUNK + j, c * CHUNK + j + P)
-                    bank = psum.tile([P, PACK, P], F32, name="b_bank")
+                    bank = psum.tile([P, PACK, P], F32, name="b_bank", bufs=3)
                     for t in range(PACK):
                         nc.tensor.matmul_mx(
                             out=bank[:, t, :],
-                            lhsT=w2_w[g][:, t * P : (t + 1) * P].bitcast(E4M3),
-                            lhsT_scale=w2_s[g][:, t * P : (t + 1) * P],
+                            lhsT=w2_w[:, g * PASS + t * P : g * PASS + (t + 1) * P].bitcast(E4M3),
+                            lhsT_scale=w2_s[:, g * PASS + t * P : g * PASS + (t + 1) * P],
                             rhs=x_w[:, tokens].bitcast(E4M3),
                             rhs_scale=x_s[:, tokens],
                             start=True,
@@ -172,43 +179,65 @@ def tile_list_calving_retreat_features_kernel(
                     nc.scalar.copy(out=b_bf[:, g, j : j + P, :], in_=bank[:].rearrange("p t n -> p n t"))
             return b_bf
 
-        def envelopes(a_bf, b_bf, c):
-            made = []
-            staged = []
-            for name, op in (("hi", ALU.max), ("lo", ALU.min)):
-                env = ring.tile([P, G * CHUNK * PACK], BF16, name=f"{name}_bf", align_bytes=64)
+        def envelope(name, op, a_bf, b_bf, c):
+            env = ring.tile([P, G * CHUNK * PACK], BF16, name=f"{name}_bf", align_bytes=64)
+            nc.vector.tensor_tensor(
+                env[:].rearrange("p (n u e) -> p n u e", u=2, e=2),
+                a_bf[:, :, c].rearrange("p u g n e -> p (g n) u e"),
+                b_bf[:].rearrange("p g n (u e) -> p (g n) u e", u=2),
+                op,
+            )
+            return env
+
+        def narrow_envelope(name, op, a_bf, b_bf, c, j):
+            env = ring.tile([P, G * P * PACK], BF16, name=f"{name}_bf", align_bytes=64)
+            for g in range(G):
                 nc.vector.tensor_tensor(
-                    env[:].rearrange("p (n u e) -> p n u e", u=2, e=2),
-                    a_bf[:, :, c].rearrange("p u g n e -> p (g n) u e"),
-                    b_bf[:].rearrange("p g n (u e) -> p (g n) u e", u=2),
+                    env[:, g * PASS : (g + 1) * PASS].rearrange("p (n u e) -> p n u e", u=2, e=2),
+                    a_bf[:, :, c, g, j : j + P].rearrange("p u n e -> p n u e"),
+                    b_bf[:, g, j : j + P].rearrange("p n (u e) -> p n u e", u=2),
                     op,
                 )
-                staged.append((name, env))
-            for name, env in staged:
-                env_w = ring.tile([P, G * CHUNK], U32, name=f"{name}_w", align_bytes=64)
-                env_s = ring.tile([P, G * CHUNK], U8, name=f"{name}_s", align_bytes=64)
-                nc.vector.quantize_mx(out=env_w[:].bitcast(E4M3), scales=env_s[:], in_=env[:])
-                made.append((env_w, env_s))
-            return made
+            return env
 
-        def round_w4(tag):
-            staged = keep.tile([P, G * N * PACK], BF16, name="w4_bf", tag=tag, align_bytes=64)
-            for g in range(G):
-                nc.vector.tensor_copy(
-                    out=staged[:, g * N * PACK : (g + 1) * N * PACK].rearrange("p (c i t) -> p c t i", i=4, t=PACK),
-                    in_=w4_raw[g][:].rearrange("p t (c i) -> p c t i", i=4),
-                )
-            for lo, hi in ((0, 512), (512, G * N)):
+        def quantize_envelope(name, env):
+            width = env.shape[1] // PACK
+            env_w = ring.tile([P, width], U32, name=f"{name}_w", align_bytes=64, bufs=4)
+            env_s = ring.tile([P, width], U8, name=f"{name}_s", align_bytes=64, bufs=4)
+            nc.vector.quantize_mx(out=env_w[:].bitcast(E4M3), scales=env_s[:], in_=env[:])
+            return env_w, env_s
+
+        def envelopes(a_bf, b_bf, c):
+            hi = envelope("hi", ALU.max, a_bf, b_bf, c)
+            lo = envelope("lo", ALU.min, a_bf, b_bf, c)
+            return quantize_envelope("hi", hi), quantize_envelope("lo", lo)
+
+        def narrow_envelopes(a_bf, b_bf, c, j):
+            hi = narrow_envelope("hi", ALU.max, a_bf, b_bf, c, j)
+            lo = narrow_envelope("lo", ALU.min, a_bf, b_bf, c, j)
+            return quantize_envelope("hi", hi), quantize_envelope("lo", lo)
+
+        def round_w4(copy, staged, g):
+            copy(
+                out=staged[:, g * N * PACK : (g + 1) * N * PACK].rearrange("p (c i t) -> p c t i", i=4, t=PACK),
+                in_=w4_raw[g][:].rearrange("p t (c i) -> p c t i", i=4),
+            )
+
+        def quantize_w4(staged):
+            for first, last in ((0, 256), (256, G * N)):
                 nc.vector.quantize_mx(
-                    out=w4_w[:, lo:hi].bitcast(E4M3), scales=w4_s[:, lo:hi], in_=staged[:, lo * PACK : hi * PACK]
+                    out=w4_w[:, first:last].bitcast(E4M3),
+                    scales=w4_s[:, first:last],
+                    in_=staged[:, first * PACK : last * PACK],
                 )
 
-        def project(name, weight, weight_s, env, n):
+        def project(tag, bufs, weight, weight_s, env, n):
             env_w, env_s = env
-            bank = psum.tile([P, CHUNK], F32, name=name)
+            width = env_w.shape[1] // G
+            bank = psum.tile([P, width], F32, name="y_bank", tag=tag, bufs=bufs)
             for g in range(G):
                 cols = slice(g * N + n * P, g * N + (n + 1) * P)
-                tokens = slice(g * CHUNK, (g + 1) * CHUNK)
+                tokens = slice(g * width, (g + 1) * width)
                 nc.tensor.matmul_mx(
                     out=bank[:],
                     lhsT=weight[:, cols].bitcast(E4M3),
@@ -222,20 +251,23 @@ def tile_list_calving_retreat_features_kernel(
 
         w3_flat = w3_w[:].rearrange("p g n -> p (g n)")
 
-        def upper(env):
-            y3 = ring.tile([P, NT, CHUNK], F32, name="y3")
+        def upper(hi):
+            y3 = ring.tile([P, NT, hi[0].shape[1] // G], F32, name="y3", bufs=4)
             for n in range(NT):
-                bank = project("y3_bank", w3_flat, w3_s, env[0], n)
+                bank = project("ay", 3, w3_flat, w3_s, hi, n)
                 nc.scalar.copy(out=y3[:, n, :], in_=bank[:])
             return y3
 
-        def finish(env, y3, chunk):
-            for n in range(NT):
-                bank = project("y4_bank", w4_w, w4_s, env[1], n)
-                res = ring.tile([P, CHUNK], F32, name="res", bufs=4)
+        def finish(lo, y3, start, banks=(("y4", 2),) * NT, rows=range(NT)):
+            width = y3.shape[2]
+            for n in rows:
+                bank = project(*banks[n], w4_w, w4_s, lo, n)
+                res = ring.tile([P, width], F32, name="res", bufs=8)
                 nc.vector.tensor_tensor(res[:], bank[:], y3[:, n, :], ALU.mult)
-                nc.sync.dma_start(out=out[n * P : (n + 1) * P, chunk * CHUNK : (chunk + 1) * CHUNK], in_=res[:])
+                nc.sync.dma_start(out=out[n * P : (n + 1) * P, start : start + width], in_=res[:])
 
+        v_s = keep.tile([P, S], U8, name="v_s", align_bytes=64)
+        nc.vector.tensor_copy(v_s[:], tab_s[:].indirect(idx[:]))
         nc.vector.tensor_copy(
             out=w1_w[:].bitcast(U16).rearrange("p (g t m) -> p g t m", g=G, t=PACK),
             in_=w1_raw[:].bitcast(U16).rearrange("p (g m t) -> p g t m", g=G, t=PACK),
@@ -245,28 +277,50 @@ def tile_list_calving_retreat_features_kernel(
             out=w1_s[:].rearrange("p (g t m) -> p g t m", g=G, t=PACK),
             in_=w1s_raw[:].rearrange("p (g m t) -> p g t m", g=G, t=PACK),
         )
-        round_w2(0, "w2_bf0")
-        a0 = make_a(v0)
+        a0 = make_a(v0, "a_bf0")
         v1 = gather_table(1)
-        x0 = quantize_x(gather_x(0, "change0"))
-        round_w2(1, "chain")
-        change1 = gather_x(1, "chain")
+        w2_bf = keep.tile([P, PACK * H], BF16, name="w2_bf", align_bytes=64)
+        for g in range(G):
+            round_w2(w2_bf, g)
+        change0 = keep.tile([P, PACK, HALF], F32, name="change0")
+        for t in range(PACK):
+            gather_before(0, t)
+            gather_before(1, t)
+            gather_change(change0, 0, t)
+        x0 = quantize_x(round_x(change0[:, :, :CHUNK], "x_bf00")[:], "x_w00")
+        x1 = quantize_x(round_x(change0[:, :, CHUNK:], "x_bf0")[:], "x_w0")
+        change2 = reuse.tile([P, PACK, CHUNK], F32, name="change2", align_bytes=64, offset=0)
+        gather_change(change2, 2 * CHUNK, 0)
+        w2_w = reuse.tile([P, H], U32, name="w2_w", align_bytes=64, offset=4 * H)
+        nc.vector.quantize_mx(out=w2_w[:].bitcast(E4M3), scales=w2_s[:], in_=w2_bf[:])
+        for t in range(1, PACK):
+            gather_change(change2, 2 * CHUNK, t)
+        change3 = keep.tile([P, PACK, CHUNK], F32, name="change3", tag="x_bf0", align_bytes=64)
+        for t in range(PACK):
+            gather_change(change3, 3 * CHUNK, t)
         b0 = make_b(x0, 0)
-        b1_ = make_b(x0, 1)
-        env0 = envelopes(a0, b0, 0)
-        y30 = upper(env0)
-        x1 = quantize_x(change1)
-        env1 = envelopes(a0, b1_, 1)
-        round_w4("chain")
-        a1 = make_a(v1)
-        finish(env0, y30, 0)
-        b2 = make_b(x1, 0)
-        y31 = upper(env1)
-        finish(env1, y31, 1)
-        b3 = make_b(x1, 1)
-        env2 = envelopes(a1, b2, 0)
-        y32 = upper(env2)
-        env3 = envelopes(a1, b3, 1)
-        finish(env2, y32, 2)
-        y33 = upper(env3)
-        finish(env3, y33, 3)
+        b1_ = make_b(x1, 0)
+        x2 = quantize_x(round_x(change2[:], "x_w00")[:], "x_w2")
+        hi0, lo0 = envelopes(a0, b0, 0)
+        b2 = make_b(x2, 0)
+        x3 = quantize_x(round_x(change3[:], "x_w0")[:], "x_w3")
+        a1 = make_a(v1, "w2_raw1")
+        y30 = upper(hi0)
+        hi1, lo1 = envelopes(a0, b1_, 1)
+        w4_bf = keep.tile([P, G * N * PACK], BF16, name="w4_bf", tag="x_bf0", align_bytes=64)
+        round_w4(nc.vector.tensor_copy, w4_bf, 0)
+        round_w4(nc.vector.tensor_copy, w4_bf, 1)
+        quantize_w4(w4_bf)
+        b3 = make_b(x3, 0)
+        finish(lo0, y30, 0)
+        y31 = upper(hi1)
+        hi2, lo2 = envelopes(a1, b2, 0)
+        y32 = upper(hi2)
+        hi3 = envelope("hi", ALU.max, a1, b3, 1)
+        finish(lo1, y31, CHUNK)
+        y33 = upper(quantize_envelope("hi", hi3))
+        lo3 = envelope("lo", ALU.min, a1, b3, 1)
+        finish(lo2, y32, 2 * CHUNK, (("b_bank", 3),) * NT, range(1))
+        lo3 = quantize_envelope("lo", lo3)
+        finish(lo2, y32, 2 * CHUNK, (("b_bank", 3),) * NT, range(1, NT))
+        finish(lo3, y33, 3 * CHUNK, (("y4", 2), ("y4", 2), ("b_bank", 3)))

@@ -23,6 +23,8 @@ G = H // PASS
 HALF = 512
 CHUNK = 256
 NT = N // P
+W2_PIECE = 256
+A1_EARLY = 6
 LIST_ROWS = 16
 
 
@@ -42,25 +44,34 @@ def tile_list_calving_retreat_features_kernel(
         tab_w = keep.tile([P, T], I32, name="tab_w", align_bytes=64)
         tab_s = keep.tile([P, T], U8, name="tab_s", align_bytes=64)
         w1_raw = keep.tile([P, 2 * H], U8, name="w1_raw", align_bytes=64)
-        w1s_raw = keep.tile([P, H], U8, name="w1s_raw", align_bytes=64)
+        w1s_raw = keep.tile([P, H], U8, name="w1s_raw", tag="w1s_raw", align_bytes=64)
         w1_w = keep.tile([P, 2 * H], U8, name="w1_w", align_bytes=64)
         w1_s = keep.tile([P, H], U8, name="w1_s", align_bytes=64)
         bias = keep.tile([P, G, PACK], F32, name="bias")
         w3_w = keep.tile([P, G, N], I32, name="w3_w", align_bytes=64)
         w3_s = keep.tile([P, G * N], U8, name="w3_s", align_bytes=64)
         x_plane = [keep.tile([P, T], F32, name=f"x_plane{t}") for t in range(PACK)]
-        w2_raw = [keep.tile([P, PACK, PASS], F32, name=f"w2_raw{g}", tag=f"w2_raw{g}") for g in range(G)]
-        w4_raw = [keep.tile([P, PACK, N], F32, name=f"w4_raw{g}") for g in range(G)]
-        before = [
-            reuse.tile([P, PACK, HALF], F32, name="before0", align_bytes=64, offset=0),
-            keep.tile([P, PACK, HALF], F32, name="before1"),
+        w2_raw = [keep.tile([P, PACK, W2_PIECE], F32, name=f"w2_raw{i}", tag=f"w2_raw{i}") for i in range(H // W2_PIECE)]
+        w4_raw = [
+            reuse.tile([P, PACK, N], F32, name="w4_raw0", align_bytes=64, offset=0),
+            keep.tile([P, PACK, N], F32, name="w4_raw1"),
         ]
         w2_s = keep.tile([P, H], U8, name="w2_s", align_bytes=64)
-        w4_w = keep.tile([P, G * N], U32, name="w4_w", align_bytes=64)
         w4_s = keep.tile([P, G * N], U8, name="w4_s", align_bytes=64)
 
-        def load_scale_rows(plane, rows, q):
-            nc.sync.dma_start(out=plane[32 * q : 32 * q + 4], in_=rows[4 * q : 4 * q + 4])
+        def load_scale_rows(plane, rows, q, queue=nc.sync):
+            queue.dma_start(out=plane[q:P:32], in_=rows[q:16:4])
+
+        def load_x(t):
+            nc.sync.dma_start(out=x_plane[t][:], in_=x_rows[:, t, :])
+
+        def load_w2(i):
+            nc.sync.dma_start(out=w2_raw[i][:], in_=w2_rows[:, :, i * W2_PIECE : (i + 1) * W2_PIECE])
+
+        def load_w4(g):
+            nc.sync.dma_start(
+                out=w4_raw[g][:], in_=w4[g * PASS : (g + 1) * PASS, :].rearrange("(p t) n -> p t n", t=PACK)
+            )
 
         x_rows = xT.rearrange("(p t) c -> p t c", t=PACK)
         w2_rows = w2.rearrange("(p t) r -> p t r", t=PACK)
@@ -70,20 +81,19 @@ def tile_list_calving_retreat_features_kernel(
         nc.sync.dma_start(idx[:], offs)
         nc.sync.dma_start(out=w1_raw[:].bitcast(I32), in_=w1_words[0].bitcast(I32))
         for q in range(4):
-            load_scale_rows(tab_s[:].bitcast(I32), tab_scales[0].bitcast(I32), q)
-        load_scale_rows(w1s_raw[:].bitcast(I32), w1_scales[0].bitcast(I32), 0)
+            load_scale_rows(tab_s[:].bitcast(I32), tab_scales[0].bitcast(I32), q, (nc.sync, nc.scalar)[q % 2])
         nc.sync.dma_start(out=tab_w[:], in_=tab_words[0].rearrange("p c i -> p (c i)").bitcast(I32))
-        for q in range(1, 4):
+        for q in range(4):
             load_scale_rows(w1s_raw[:].bitcast(I32), w1_scales[0].bitcast(I32), q)
         nc.sync.dma_start(out=bias[:], in_=b1.rearrange("(g p t) -> p g t", g=G, t=PACK))
-        nc.sync.dma_start(out=x_plane[0][:], in_=x_rows[:, 0, :])
-        nc.sync.dma_start(idx3[:], offs3)
-        nc.sync.dma_start(idx2[:], offs2)
-        nc.sync.dma_start(out=w2_raw[0][:], in_=w2_rows[:, :, 0:PASS])
-        for t in range(1, PACK - 1):
-            nc.sync.dma_start(out=x_plane[t][:], in_=x_rows[:, t, :])
-        nc.sync.dma_start(out=w2_raw[1][:], in_=w2_rows[:, :, PASS : 2 * PASS])
-        nc.sync.dma_start(out=x_plane[PACK - 1][:], in_=x_rows[:, PACK - 1, :])
+        for t in range(PACK):
+            load_w2(t)
+            load_x(t)
+            if t == 0:
+                nc.sync.dma_start(idx3[:], offs3)
+                nc.sync.dma_start(idx2[:], offs2)
+        for g in range(G):
+            load_w4(g)
         nc.gpsimd.memset(w3_s[:].bitcast(I32), 0)
         for q in range(4):
             load_scale_rows(
@@ -92,65 +102,55 @@ def tile_list_calving_retreat_features_kernel(
                 q,
             )
         nc.sync.dma_start(out=w3_w[:], in_=w3_words.rearrange("g p n i -> p g (n i)").bitcast(I32))
-        for g in range(G):
-            nc.sync.dma_start(
-                out=w4_raw[g][:], in_=w4[g * PASS : (g + 1) * PASS, :].rearrange("(p t) n -> p t n", t=PACK)
-            )
 
         def offsets(tile, start, count):
             return tile[:, start // LIST_ROWS : (start + count) // LIST_ROWS]
 
-        def gather_table(h):
-            v_w = ring.tile([P, HALF], U32, name="v_w", align_bytes=64)
+        def gather_words(v_w, h):
             nc.vector.tensor_copy(v_w[:], tab_w[:].bitcast(U32).indirect(offsets(idx, h * HALF, HALF)))
-            return v_w, v_s[:, h * HALF : (h + 1) * HALF]
 
-        def make_a(v, tag):
+        def make_a(v, a_bf, pieces, start=0, width=HALF):
             v_w, v_s = v
-            a_bf = keep.tile([P, 2, HALF // CHUNK, G, CHUNK, 2], BF16, name="a_bf", tag=tag)
-            for g in range(G):
-                for t in range(PACK):
+            for piece in pieces:
+                for g, t in (divmod(piece, PACK),):
                     col = g * PASS + t * P
-                    bank = psum.tile([P, HALF], F32, name="a_bank", tag="ay", bufs=3)
+                    bank = psum.tile([P, width], F32, name="a_bank", tag="ay", bufs=3)
                     nc.tensor.matmul_mx(
                         out=bank[:],
                         lhsT=w1_w[:, 2 * col : 2 * (col + P)].bitcast(E2M1),
                         lhsT_scale=w1_s[:, col : col + P],
-                        rhs=v_w[:].bitcast(E4M3),
-                        rhs_scale=v_s,
+                        rhs=v_w[:, start : start + width].bitcast(E4M3),
+                        rhs_scale=v_s[:, start : start + width],
                         start=True,
                         stop=True,
                     )
                     nc.scalar.activation(
-                        out=a_bf[:, t // 2, :, g, :, t % 2],
-                        in_=bank[:].rearrange("p (c n) -> p c n", n=CHUNK),
+                        out=a_bf[:, t // 2, start // P : (start + width) // P, g, :, t % 2],
+                        in_=bank[:].rearrange("p (c n) -> p c n", n=P),
                         func=IDENTITY,
                         bias=bias[:, g, t : t + 1],
                     )
-            return a_bf
 
-        def round_w2(staged, g):
+        def round_w2(staged, i):
+            g, first = divmod(i * W2_PIECE // PACK, P)
+            by_pass = staged[:].rearrange("p (g t m j) -> p g m j t", g=G, t=PACK, j=PACK)
             nc.scalar.copy(
-                out=staged[:, g * PACK * PASS : (g + 1) * PACK * PASS].rearrange("p (t m j) -> p m j t", t=PACK, j=PACK),
-                in_=w2_raw[g][:].rearrange("p j (m t) -> p m j t", t=PACK),
+                out=by_pass[:, g, first : first + W2_PIECE // PACK],
+                in_=w2_raw[i][:].rearrange("p j (m t) -> p m j t", t=PACK),
             )
 
-        def gather_before(h, t):
-            nc.vector.tensor_copy(before[h][:, t, :], x_plane[t][:].indirect(offsets(idx3, h * HALF, HALF)))
+        def gather_before(before, t, start):
+            nc.vector.tensor_copy(before[:], x_plane[t][:].indirect(offsets(idx3, start, before.shape[1])))
 
-        def gather_change(change, start, t):
-            width = change.shape[2]
-            h, j = divmod(start, HALF)
-            picked = x_plane[t][:].indirect(offsets(idx2, start, width))
-            nc.vector.tensor_tensor(change[:, t, :], picked, before[h][:, t, j : j + width], ALU.subtract)
+        def gather_change(change, before, t, start):
+            picked = x_plane[t][:].indirect(offsets(idx2, start, HALF))
+            nc.vector.tensor_tensor(change[:, t, :], picked, before, ALU.subtract)
 
-        def round_x(change, tag):
-            x_bf = keep.tile([P, change.shape[2] * PACK], BF16, name="x_bf", tag=tag, align_bytes=64)
+        def round_x(x_bf, change):
             nc.scalar.copy(
-                out=x_bf[:].rearrange("p (c i t) -> p c t i", i=4, t=PACK),
+                out=x_bf.rearrange("p (c i t) -> p c t i", i=4, t=PACK),
                 in_=change.rearrange("p t (c i) -> p c t i", i=4),
             )
-            return x_bf
 
         def quantize_x(x_bf, tag):
             width = x_bf.shape[1] // PACK
@@ -159,12 +159,12 @@ def tile_list_calving_retreat_features_kernel(
             nc.vector.quantize_mx(out=x_w[:].bitcast(E4M3), scales=x_s[:], in_=x_bf)
             return x_w, x_s
 
-        def make_b(x, c):
+        def make_b(x, subs):
             x_w, x_s = x
-            b_bf = ring.tile([P, G, CHUNK, PACK], BF16, name="b_bf", bufs=3)
-            for g in range(G):
-                for j in range(0, CHUNK, P):
-                    tokens = slice(c * CHUNK + j, c * CHUNK + j + P)
+            b_bf = ring.tile([P, len(subs), G, P, PACK], BF16, name="b_bf", bufs=4)
+            for i, sub in enumerate(subs):
+                tokens = slice(sub % 2 * P, (sub % 2 + 1) * P)
+                for g in range(G):
                     bank = psum.tile([P, PACK, P], F32, name="b_bank", bufs=3)
                     for t in range(PACK):
                         nc.tensor.matmul_mx(
@@ -176,28 +176,18 @@ def tile_list_calving_retreat_features_kernel(
                             start=True,
                             stop=True,
                         )
-                    nc.scalar.copy(out=b_bf[:, g, j : j + P, :], in_=bank[:].rearrange("p t n -> p n t"))
+                    nc.scalar.copy(out=b_bf[:, i, g], in_=bank[:].rearrange("p t n -> p n t"))
             return b_bf
 
-        def envelope(name, op, a_bf, b_bf, c):
-            env = ring.tile([P, G * CHUNK * PACK], BF16, name=f"{name}_bf", align_bytes=64)
+        def envelope(name, op, a_bf, b_bf, subs):
+            env = ring.tile([P, len(subs) * G * P * PACK], BF16, name=f"{name}_bf", align_bytes=64)
+            first = subs[0] % PACK
             nc.vector.tensor_tensor(
                 env[:].rearrange("p (n u e) -> p n u e", u=2, e=2),
-                a_bf[:, :, c].rearrange("p u g n e -> p (g n) u e"),
-                b_bf[:].rearrange("p g n (u e) -> p (g n) u e", u=2),
+                a_bf[:, :, first : first + len(subs)].rearrange("p u c g n e -> p (c g n) u e"),
+                b_bf[:].rearrange("p c g n (u e) -> p (c g n) u e", u=2),
                 op,
             )
-            return env
-
-        def narrow_envelope(name, op, a_bf, b_bf, c, j):
-            env = ring.tile([P, G * P * PACK], BF16, name=f"{name}_bf", align_bytes=64)
-            for g in range(G):
-                nc.vector.tensor_tensor(
-                    env[:, g * PASS : (g + 1) * PASS].rearrange("p (n u e) -> p n u e", u=2, e=2),
-                    a_bf[:, :, c, g, j : j + P].rearrange("p u n e -> p n u e"),
-                    b_bf[:, g, j : j + P].rearrange("p n (u e) -> p n u e", u=2),
-                    op,
-                )
             return env
 
         def quantize_envelope(name, env):
@@ -207,14 +197,9 @@ def tile_list_calving_retreat_features_kernel(
             nc.vector.quantize_mx(out=env_w[:].bitcast(E4M3), scales=env_s[:], in_=env[:])
             return env_w, env_s
 
-        def envelopes(a_bf, b_bf, c):
-            hi = envelope("hi", ALU.max, a_bf, b_bf, c)
-            lo = envelope("lo", ALU.min, a_bf, b_bf, c)
-            return quantize_envelope("hi", hi), quantize_envelope("lo", lo)
-
-        def narrow_envelopes(a_bf, b_bf, c, j):
-            hi = narrow_envelope("hi", ALU.max, a_bf, b_bf, c, j)
-            lo = narrow_envelope("lo", ALU.min, a_bf, b_bf, c, j)
+        def envelopes(a_bf, b_bf, subs):
+            hi = envelope("hi", ALU.max, a_bf, b_bf, subs)
+            lo = envelope("lo", ALU.min, a_bf, b_bf, subs)
             return quantize_envelope("hi", hi), quantize_envelope("lo", lo)
 
         def round_w4(copy, staged, g):
@@ -231,40 +216,51 @@ def tile_list_calving_retreat_features_kernel(
                     in_=staged[:, first * PACK : last * PACK],
                 )
 
-        def project(tag, bufs, weight, weight_s, env, n):
+        def project(bank, weight, weight_s, env, rows):
             env_w, env_s = env
-            width = env_w.shape[1] // G
-            bank = psum.tile([P, width], F32, name="y_bank", tag=tag, bufs=bufs)
-            for g in range(G):
-                cols = slice(g * N + n * P, g * N + (n + 1) * P)
-                tokens = slice(g * width, (g + 1) * width)
-                nc.tensor.matmul_mx(
-                    out=bank[:],
-                    lhsT=weight[:, cols].bitcast(E4M3),
-                    lhsT_scale=weight_s[:, cols],
-                    rhs=env_w[:, tokens].bitcast(E4M3),
-                    rhs_scale=env_s[:, tokens],
-                    start=(g == 0),
-                    stop=(g == G - 1),
-                )
-            return bank
+            for i, n in enumerate(rows):
+                for j in range(0, bank.shape[2], P):
+                    for g in range(G):
+                        cols = slice(g * N + n * P, g * N + (n + 1) * P)
+                        tokens = slice(j * G + g * P, j * G + (g + 1) * P)
+                        nc.tensor.matmul_mx(
+                            out=bank[:, i, j : j + P],
+                            lhsT=weight[:, cols].bitcast(E4M3),
+                            lhsT_scale=weight_s[:, cols],
+                            rhs=env_w[:, tokens].bitcast(E4M3),
+                            rhs_scale=env_s[:, tokens],
+                            start=(g == 0),
+                            stop=(g == G - 1),
+                        )
 
         w3_flat = w3_w[:].rearrange("p g n -> p (g n)")
+        out_rows = out.rearrange("(n p) j -> p n j", p=P)
+
+        def row_groups(width):
+            per_bank = HALF // width
+            return [range(n, min(n + per_bank, NT)) for n in range(0, NT, per_bank)]
 
         def upper(hi):
-            y3 = ring.tile([P, NT, hi[0].shape[1] // G], F32, name="y3", bufs=4)
-            for n in range(NT):
-                bank = project("ay", 3, w3_flat, w3_s, hi, n)
-                nc.scalar.copy(out=y3[:, n, :], in_=bank[:])
+            width = hi[0].shape[1] // G
+            y3 = ring.tile([P, NT, width], F32, name="y3", bufs=4)
+            for rows in row_groups(width):
+                bank = psum.tile([P, len(rows), width], F32, name="y3_bank", tag="ay", bufs=3)
+                project(bank, w3_flat, w3_s, hi, rows)
+                nc.scalar.copy(out=y3[:, rows[0] : rows[-1] + 1, :], in_=bank[:])
             return y3
 
-        def finish(lo, y3, start, banks=(("y4", 2),) * NT, rows=range(NT)):
+        def finish(lo, y3, subs, tag="y4", bufs=2):
             width = y3.shape[2]
-            for n in rows:
-                bank = project(*banks[n], w4_w, w4_s, lo, n)
-                res = ring.tile([P, width], F32, name="res", bufs=8)
-                nc.vector.tensor_tensor(res[:], bank[:], y3[:, n, :], ALU.mult)
-                nc.sync.dma_start(out=out[n * P : (n + 1) * P, start : start + width], in_=res[:])
+            for rows in row_groups(width):
+                bank = psum.tile([P, len(rows), width], F32, name="y4_bank", tag=tag, bufs=bufs)
+                project(bank, w4_w, w4_s, lo, rows)
+                res = ring.tile([P, len(rows), width], F32, name="res", bufs=8)
+                span = slice(rows[0], rows[-1] + 1)
+                nc.vector.tensor_tensor(res[:], bank[:], y3[:, span, :], ALU.mult)
+                nc.sync.dma_start(out=out_rows[:, span, subs[0] * P : subs[0] * P + width], in_=res[:])
+
+        def placed(shape, dtype, name, offset):
+            return reuse.tile(shape, dtype, name=name, align_bytes=64, offset=offset)
 
         v_s = keep.tile([P, S], U8, name="v_s", align_bytes=64)
         nc.vector.tensor_copy(v_s[:], tab_s[:].indirect(idx[:]))
@@ -272,55 +268,71 @@ def tile_list_calving_retreat_features_kernel(
             out=w1_w[:].bitcast(U16).rearrange("p (g t m) -> p g t m", g=G, t=PACK),
             in_=w1_raw[:].bitcast(U16).rearrange("p (g m t) -> p g t m", g=G, t=PACK),
         )
-        v0 = gather_table(0)
+        v_w0 = keep.tile([P, HALF], U32, name="v_w0", align_bytes=64)
+        gather_words(v_w0, 0)
         nc.vector.tensor_copy(
             out=w1_s[:].rearrange("p (g t m) -> p g t m", g=G, t=PACK),
             in_=w1s_raw[:].rearrange("p (g m t) -> p g t m", g=G, t=PACK),
         )
-        a0 = make_a(v0, "a_bf0")
-        v1 = gather_table(1)
         w2_bf = keep.tile([P, PACK * H], BF16, name="w2_bf", align_bytes=64)
+        round_w2(w2_bf, 0)
+        a0 = keep.tile([P, 2, HALF // P, G, P, 2], BF16, name="a0", tag="w2_raw0")
+        a1 = keep.tile([P, 2, HALF // P, G, P, 2], BF16, name="a1")
+        make_a((v_w0, v_s[:, :HALF]), a0, range(8))
+        v_w1 = keep.tile([P, HALF], U32, name="v_w1", tag="w1s_raw", align_bytes=64)
+        gather_words(v_w1, 1)
+        v1 = (v_w1, v_s[:, HALF:])
+        for i in range(1, H // W2_PIECE):
+            round_w2(w2_bf, i)
+        w4_bf = keep.tile([P, G * N * PACK], BF16, name="w4_bf", align_bytes=64)
         for g in range(G):
-            round_w2(w2_bf, g)
-        change0 = keep.tile([P, PACK, HALF], F32, name="change0")
+            round_w4(nc.scalar.copy, w4_bf, g)
+        change01 = keep.tile([P, PACK, HALF], F32, name="change01", tag="change01", align_bytes=64)
+        before_late = []
         for t in range(PACK):
-            gather_before(0, t)
-            gather_before(1, t)
-            gather_change(change0, 0, t)
-        x0 = quantize_x(round_x(change0[:, :, :CHUNK], "x_bf00")[:], "x_w00")
-        x1 = quantize_x(round_x(change0[:, :, CHUNK:], "x_bf0")[:], "x_w0")
-        change2 = reuse.tile([P, PACK, CHUNK], F32, name="change2", align_bytes=64, offset=0)
-        gather_change(change2, 2 * CHUNK, 0)
-        w2_w = reuse.tile([P, H], U32, name="w2_w", align_bytes=64, offset=4 * H)
+            early = placed([P, HALF], F32, "early", 7168) if t == PACK - 1 else ring.tile([P, HALF], F32, name="early")
+            gather_before(early, t, 0)
+            before_late.append(keep.tile([P, HALF], F32, name=f"before_late{t}"))
+            gather_before(before_late[t], t, HALF)
+            gather_change(change01, early[:], t, 0)
+        change23 = placed([P, PACK, HALF], F32, "change23", 0)
+        w2_w = placed([P, H], U32, "w2_w", 8192)
+        flat23 = change23[:].rearrange("p t c -> p (t c)")
+        x_bf = [flat23[:, first : first + HALF].bitcast(BF16) for first in (3 * CHUNK, 3 * HALF)]
+        for c in range(2):
+            round_x(x_bf[c], change01[:, :, c * CHUNK : (c + 1) * CHUNK])
         nc.vector.quantize_mx(out=w2_w[:].bitcast(E4M3), scales=w2_s[:], in_=w2_bf[:])
-        for t in range(1, PACK):
-            gather_change(change2, 2 * CHUNK, t)
-        change3 = keep.tile([P, PACK, CHUNK], F32, name="change3", tag="x_bf0", align_bytes=64)
+        x0 = quantize_x(x_bf[0], "x_w0")
+        x1 = quantize_x(x_bf[1], "x_w1")
         for t in range(PACK):
-            gather_change(change3, 3 * CHUNK, t)
-        b0 = make_b(x0, 0)
-        b1_ = make_b(x1, 0)
-        x2 = quantize_x(round_x(change2[:], "x_w00")[:], "x_w2")
-        hi0, lo0 = envelopes(a0, b0, 0)
-        b2 = make_b(x2, 0)
-        x3 = quantize_x(round_x(change3[:], "x_w0")[:], "x_w3")
-        a1 = make_a(v1, "w2_raw1")
+            gather_change(change23, before_late[t][:], t, HALF)
+        make_a(v1, a1, range(A1_EARLY))
+        b0 = make_b(x0, (0, 1))
+        x_late = keep.tile([P, 2, CHUNK * PACK], BF16, name="x_late", align_bytes=64)
+        round_x(x_late[:, 0, :], change23[:, :, :CHUNK])
+        b1_ = make_b(x1, (2, 3))
+        x2 = quantize_x(x_late[:, 0, :], "x_w2")
+        hi0, lo0 = envelopes(a0, b0, (0, 1))
+        b2 = make_b(x2, (4, 5))
         y30 = upper(hi0)
-        hi1, lo1 = envelopes(a0, b1_, 1)
-        w4_bf = keep.tile([P, G * N * PACK], BF16, name="w4_bf", tag="x_bf0", align_bytes=64)
-        round_w4(nc.vector.tensor_copy, w4_bf, 0)
-        round_w4(nc.vector.tensor_copy, w4_bf, 1)
+        make_a(v1, a1, range(A1_EARLY, 8), 0, CHUNK)
+        round_x(x_late[:, 1, :], change23[:, :, CHUNK:])
+        x3 = quantize_x(x_late[:, 1, :], "x_w3")
+        hi1, lo1 = envelopes(a0, b1_, (2, 3))
+        w4_w = keep.tile([P, G * N], U32, name="w4_w", tag="change01", align_bytes=64)
         quantize_w4(w4_bf)
-        b3 = make_b(x3, 0)
-        finish(lo0, y30, 0)
+        finish(lo0, y30, (0, 1))
+        make_a(v1, a1, range(A1_EARLY, 8), CHUNK, CHUNK)
+        b3 = make_b(x3, (6,))
         y31 = upper(hi1)
-        hi2, lo2 = envelopes(a1, b2, 0)
+        b4 = make_b(x3, (7,))
+        hi2, lo2 = envelopes(a1, b2, (4, 5))
         y32 = upper(hi2)
-        hi3 = envelope("hi", ALU.max, a1, b3, 1)
-        finish(lo1, y31, CHUNK)
-        y33 = upper(quantize_envelope("hi", hi3))
-        lo3 = envelope("lo", ALU.min, a1, b3, 1)
-        finish(lo2, y32, 2 * CHUNK, (("b_bank", 3),) * NT, range(1))
-        lo3 = quantize_envelope("lo", lo3)
-        finish(lo2, y32, 2 * CHUNK, (("b_bank", 3),) * NT, range(1, NT))
-        finish(lo3, y33, 3 * CHUNK, (("y4", 2), ("y4", 2), ("b_bank", 3)))
+        finish(lo1, y31, (2, 3))
+        hi3, lo3 = envelopes(a1, b3, (6,))
+        y33 = upper(hi3)
+        hi4, lo4 = envelopes(a1, b4, (7,))
+        y34 = upper(hi4)
+        finish(lo2, y32, (4, 5))
+        finish(lo3, y33, (6,), "b_bank", 3)
+        finish(lo4, y34, (7,), "b_bank", 3)

@@ -51,7 +51,9 @@ def tile_list_calving_retreat_features_kernel(
         w3_w = keep.tile([P, G, N], I32, name="w3_w", align_bytes=64)
         w3_s = keep.tile([P, G * N], U8, name="w3_s", align_bytes=64)
         x_plane = [keep.tile([P, T], F32, name=f"x_plane{t}") for t in range(PACK)]
-        w2_raw = [keep.tile([P, PACK, W2_PIECE], F32, name=f"w2_raw{i}", tag=f"w2_raw{i}") for i in range(H // W2_PIECE)]
+        w2_first = [keep.tile([P, PACK, W2_PIECE], F32, name=f"w2_raw{i}", tag=f"w2_raw{i}") for i in range(2)]
+        w2_second = keep.tile([P, PACK, PASS], F32, name="w2_second")
+        w2_raw = [w2_first[0][:], w2_first[1][:], w2_second[:, :, :W2_PIECE], w2_second[:, :, W2_PIECE:]]
         w4_raw = [
             reuse.tile([P, PACK, N], F32, name="w4_raw0", align_bytes=64, offset=0),
             keep.tile([P, PACK, N], F32, name="w4_raw1"),
@@ -66,7 +68,10 @@ def tile_list_calving_retreat_features_kernel(
             nc.sync.dma_start(out=x_plane[t][:], in_=x_rows[:, t, :])
 
         def load_w2(i):
-            nc.sync.dma_start(out=w2_raw[i][:], in_=w2_rows[:, :, i * W2_PIECE : (i + 1) * W2_PIECE])
+            if i < 2:
+                nc.sync.dma_start(out=w2_raw[i], in_=w2_rows[:, :, i * W2_PIECE : (i + 1) * W2_PIECE])
+            elif i == 2:
+                nc.sync.dma_start(out=w2_second[:], in_=w2_rows[:, :, PASS:])
 
         def load_w4(g):
             nc.sync.dma_start(
@@ -131,16 +136,16 @@ def tile_list_calving_retreat_features_kernel(
                         bias=bias[:, g, t : t + 1],
                     )
 
-        def round_w2(staged, i):
+        def round_w2(copy, staged, i):
             g, first = divmod(i * W2_PIECE // PACK, P)
             by_pass = staged[:].rearrange("p (g t m j) -> p g m j t", g=G, t=PACK, j=PACK)
-            nc.scalar.copy(
+            copy(
                 out=by_pass[:, g, first : first + W2_PIECE // PACK],
-                in_=w2_raw[i][:].rearrange("p j (m t) -> p m j t", t=PACK),
+                in_=w2_raw[i].rearrange("p j (m t) -> p m j t", t=PACK),
             )
 
         def gather_before(before, t, start):
-            nc.vector.tensor_copy(before[:], x_plane[t][:].indirect(offsets(idx3, start, before.shape[1])))
+            nc.vector.tensor_copy(before, x_plane[t][:].indirect(offsets(idx3, start, before.shape[1])))
 
         def gather_change(change, before, t, start):
             picked = x_plane[t][:].indirect(offsets(idx2, start, HALF))
@@ -275,7 +280,7 @@ def tile_list_calving_retreat_features_kernel(
             in_=w1s_raw[:].rearrange("p (g m t) -> p g t m", g=G, t=PACK),
         )
         w2_bf = keep.tile([P, PACK * H], BF16, name="w2_bf", align_bytes=64)
-        round_w2(w2_bf, 0)
+        round_w2(nc.scalar.copy, w2_bf, 0)
         a0 = keep.tile([P, 2, HALF // P, G, P, 2], BF16, name="a0", tag="w2_raw0")
         a1 = keep.tile([P, 2, HALF // P, G, P, 2], BF16, name="a1")
         make_a((v_w0, v_s[:, :HALF]), a0, range(8))
@@ -283,7 +288,7 @@ def tile_list_calving_retreat_features_kernel(
         gather_words(v_w1, 1)
         v1 = (v_w1, v_s[:, HALF:])
         for i in range(1, H // W2_PIECE):
-            round_w2(w2_bf, i)
+            round_w2(nc.vector.tensor_copy if i == 2 else nc.scalar.copy, w2_bf, i)
         w4_bf = keep.tile([P, G * N * PACK], BF16, name="w4_bf", align_bytes=64)
         for g in range(G):
             round_w4(nc.scalar.copy, w4_bf, g)
@@ -291,10 +296,12 @@ def tile_list_calving_retreat_features_kernel(
         before_late = []
         for t in range(PACK):
             early = placed([P, HALF], F32, "early", 7168) if t == PACK - 1 else ring.tile([P, HALF], F32, name="early")
-            gather_before(early, t, 0)
+            gather_before(early[:], t, 0)
             before_late.append(keep.tile([P, HALF], F32, name=f"before_late{t}"))
-            gather_before(before_late[t], t, HALF)
+            cut = CHUNK if t == PACK - 1 else HALF
+            gather_before(before_late[t][:, :cut], t, HALF)
             gather_change(change01, early[:], t, 0)
+        gather_before(before_late[PACK - 1][:, CHUNK:], PACK - 1, HALF + CHUNK)
         change23 = placed([P, PACK, HALF], F32, "change23", 0)
         w2_w = placed([P, H], U32, "w2_w", 8192)
         flat23 = change23[:].rearrange("p t c -> p (t c)")

@@ -24,7 +24,7 @@ HALF = 512
 CHUNK = 256
 NT = N // P
 W2_PIECE = 256
-A1_EARLY = 6
+A1_EARLY = 8
 LIST_ROWS = 16
 
 
@@ -35,7 +35,6 @@ def tile_list_calving_retreat_features_kernel(
     with ExitStack() as ctx:
         keep = ctx.enter_context(tc.tile_pool(name="keep", bufs=1))
         ring = ctx.enter_context(tc.tile_pool(name="ring", bufs=2))
-        reuse = ctx.enter_context(tc.tile_pool(name="reuse", bufs=1))
         psum = ctx.enter_context(tc.psum_pool(name="psum", bufs=2))
 
         idx = keep.tile([P, S // LIST_ROWS], U16, name="idx")
@@ -51,11 +50,12 @@ def tile_list_calving_retreat_features_kernel(
         w3_w = keep.tile([P, G, N], I32, name="w3_w", align_bytes=64)
         w3_s = keep.tile([P, G * N], U8, name="w3_s", align_bytes=64)
         x_plane = [keep.tile([P, T], F32, name=f"x_plane{t}") for t in range(PACK)]
-        w2_first = [keep.tile([P, PACK, W2_PIECE], F32, name=f"w2_raw{i}", tag=f"w2_raw{i}") for i in range(2)]
-        w2_second = keep.tile([P, PACK, PASS], F32, name="w2_second")
-        w2_raw = [w2_first[0][:], w2_first[1][:], w2_second[:, :, :W2_PIECE], w2_second[:, :, W2_PIECE:]]
+        change = keep.tile([P, PACK + 4, HALF], F32, name="change", align_bytes=64)
+        change01, change23 = change[:, 4:, :], change[:, 2 : PACK + 2, :]
+        w2_raw = [keep.tile([P, PACK, W2_PIECE], F32, name=f"w2_raw{i}", tag=f"w2_raw{i}")[:] for i in range(3)]
+        w2_raw.append(change[:, :PACK, :W2_PIECE])
         w4_raw = [
-            reuse.tile([P, PACK, N], F32, name="w4_raw0", align_bytes=64, offset=0),
+            keep.tile([P, PACK, N], F32, name="w4_raw0"),
             keep.tile([P, PACK, N], F32, name="w4_raw1"),
         ]
         w2_s = keep.tile([P, H], U8, name="w2_s", align_bytes=64)
@@ -68,10 +68,7 @@ def tile_list_calving_retreat_features_kernel(
             nc.sync.dma_start(out=x_plane[t][:], in_=x_rows[:, t, :])
 
         def load_w2(i):
-            if i < 2:
-                nc.sync.dma_start(out=w2_raw[i], in_=w2_rows[:, :, i * W2_PIECE : (i + 1) * W2_PIECE])
-            elif i == 2:
-                nc.sync.dma_start(out=w2_second[:], in_=w2_rows[:, :, PASS:])
+            nc.sync.dma_start(out=w2_raw[i], in_=w2_rows[:, :, i * W2_PIECE : (i + 1) * W2_PIECE])
 
         def load_w4(g):
             nc.sync.dma_start(
@@ -91,12 +88,15 @@ def tile_list_calving_retreat_features_kernel(
         for q in range(4):
             load_scale_rows(w1s_raw[:].bitcast(I32), w1_scales[0].bitcast(I32), q)
         nc.sync.dma_start(out=bias[:], in_=b1.rearrange("(g p t) -> p g t", g=G, t=PACK))
-        for t in range(PACK):
-            load_w2(t)
+        load_w2(0)
+        load_x(0)
+        nc.sync.dma_start(idx3[:], offs3)
+        nc.sync.dma_start(idx2[:], offs2)
+        load_w2(1)
+        for t in range(1, PACK):
             load_x(t)
-            if t == 0:
-                nc.sync.dma_start(idx3[:], offs3)
-                nc.sync.dma_start(idx2[:], offs2)
+        load_w2(2)
+        load_w2(3)
         for g in range(G):
             load_w4(g)
         nc.gpsimd.memset(w3_s[:].bitcast(I32), 0)
@@ -170,7 +170,7 @@ def tile_list_calving_retreat_features_kernel(
             for i, sub in enumerate(subs):
                 tokens = slice(sub % 2 * P, (sub % 2 + 1) * P)
                 for g in range(G):
-                    bank = psum.tile([P, PACK, P], F32, name="b_bank", bufs=3)
+                    bank = psum.tile([P, PACK, P], F32, name="b_bank", tag="b_bank", bufs=3)
                     for t in range(PACK):
                         nc.tensor.matmul_mx(
                             out=bank[:, t, :],
@@ -245,27 +245,24 @@ def tile_list_calving_retreat_features_kernel(
             per_bank = HALF // width
             return [range(n, min(n + per_bank, NT)) for n in range(0, NT, per_bank)]
 
-        def upper(hi):
-            width = hi[0].shape[1] // G
-            y3 = ring.tile([P, NT, width], F32, name="y3", bufs=4)
+        def upper(hi, y3):
+            width = y3.shape[2]
             for rows in row_groups(width):
                 bank = psum.tile([P, len(rows), width], F32, name="y3_bank", tag="ay", bufs=3)
                 project(bank, w3_flat, w3_s, hi, rows)
                 nc.scalar.copy(out=y3[:, rows[0] : rows[-1] + 1, :], in_=bank[:])
-            return y3
 
-        def finish(lo, y3, subs, tag="y4", bufs=2):
-            width = y3.shape[2]
-            for rows in row_groups(width):
-                bank = psum.tile([P, len(rows), width], F32, name="y4_bank", tag=tag, bufs=bufs)
+        def multiply(bank, y3, rows, c):
+            res = ring.tile([P, len(rows), CHUNK], F32, name="res", bufs=8)
+            span = slice(rows[0], rows[-1] + 1)
+            nc.vector.tensor_tensor(res[:], bank[:], y3[:, span, :], ALU.mult)
+            nc.sync.dma_start(out=out_rows[:, span, c * CHUNK : (c + 1) * CHUNK], in_=res[:])
+
+        def finish(lo, y3, c):
+            for rows in row_groups(CHUNK):
+                bank = psum.tile([P, len(rows), CHUNK], F32, name="y4_bank", bufs=2)
                 project(bank, w4_w, w4_s, lo, rows)
-                res = ring.tile([P, len(rows), width], F32, name="res", bufs=8)
-                span = slice(rows[0], rows[-1] + 1)
-                nc.vector.tensor_tensor(res[:], bank[:], y3[:, span, :], ALU.mult)
-                nc.sync.dma_start(out=out_rows[:, span, subs[0] * P : subs[0] * P + width], in_=res[:])
-
-        def placed(shape, dtype, name, offset):
-            return reuse.tile(shape, dtype, name=name, align_bytes=64, offset=offset)
+                multiply(bank, y3, rows, c)
 
         v_s = keep.tile([P, S], U8, name="v_s", align_bytes=64)
         nc.vector.tensor_copy(v_s[:], tab_s[:].indirect(idx[:]))
@@ -289,57 +286,60 @@ def tile_list_calving_retreat_features_kernel(
         v1 = (v_w1, v_s[:, HALF:])
         for i in range(1, H // W2_PIECE):
             round_w2(nc.vector.tensor_copy if i == 2 else nc.scalar.copy, w2_bf, i)
-        w4_bf = keep.tile([P, G * N * PACK], BF16, name="w4_bf", align_bytes=64)
-        for g in range(G):
-            round_w4(nc.scalar.copy, w4_bf, g)
-        change01 = keep.tile([P, PACK, HALF], F32, name="change01", tag="change01", align_bytes=64)
+        make_a(v1, a1, range(A1_EARLY))
         before_late = []
         for t in range(PACK):
-            early = placed([P, HALF], F32, "early", 7168) if t == PACK - 1 else ring.tile([P, HALF], F32, name="early")
+            early = ring.tile([P, HALF], F32, name="early")
             gather_before(early[:], t, 0)
             before_late.append(keep.tile([P, HALF], F32, name=f"before_late{t}"))
-            cut = CHUNK if t == PACK - 1 else HALF
-            gather_before(before_late[t][:, :cut], t, HALF)
+            gather_before(before_late[t][:], t, HALF)
             gather_change(change01, early[:], t, 0)
-        gather_before(before_late[PACK - 1][:, CHUNK:], PACK - 1, HALF + CHUNK)
-        change23 = placed([P, PACK, HALF], F32, "change23", 0)
-        w2_w = placed([P, H], U32, "w2_w", 8192)
-        flat23 = change23[:].rearrange("p t c -> p (t c)")
-        x_bf = [flat23[:, first : first + HALF].bitcast(BF16) for first in (3 * CHUNK, 3 * HALF)]
+        x_bf = [change[:, c, :].bitcast(BF16) for c in range(2)]
         for c in range(2):
             round_x(x_bf[c], change01[:, :, c * CHUNK : (c + 1) * CHUNK])
+        gather_change(change23, before_late[0][:], 0, HALF)
+        w2_w = keep.tile([P, H], U32, name="w2_w", align_bytes=64)
         nc.vector.quantize_mx(out=w2_w[:].bitcast(E4M3), scales=w2_s[:], in_=w2_bf[:])
+        gather_change(change23, before_late[1][:], 1, HALF)
         x0 = quantize_x(x_bf[0], "x_w0")
         x1 = quantize_x(x_bf[1], "x_w1")
-        for t in range(PACK):
+        for t in (2, 3):
             gather_change(change23, before_late[t][:], t, HALF)
-        make_a(v1, a1, range(A1_EARLY))
+        w4_bf = keep.tile([P, G * N * PACK], BF16, name="w4_bf", align_bytes=64)
+        round_w4(nc.scalar.copy, w4_bf, 0)
         b0 = make_b(x0, (0, 1))
         x_late = keep.tile([P, 2, CHUNK * PACK], BF16, name="x_late", align_bytes=64)
         round_x(x_late[:, 0, :], change23[:, :, :CHUNK])
         b1_ = make_b(x1, (2, 3))
+        round_w4(nc.scalar.copy, w4_bf, 1)
         x2 = quantize_x(x_late[:, 0, :], "x_w2")
         hi0, lo0 = envelopes(a0, b0, (0, 1))
         b2 = make_b(x2, (4, 5))
-        y30 = upper(hi0)
-        make_a(v1, a1, range(A1_EARLY, 8), 0, CHUNK)
+        y3 = [keep.tile([P, NT, CHUNK], F32, name=f"y3_{c}") for c in range(S // CHUNK)]
+        upper(hi0, y3[0])
         round_x(x_late[:, 1, :], change23[:, :, CHUNK:])
         x3 = quantize_x(x_late[:, 1, :], "x_w3")
         hi1, lo1 = envelopes(a0, b1_, (2, 3))
-        w4_w = keep.tile([P, G * N], U32, name="w4_w", tag="change01", align_bytes=64)
+        w4_w = keep.tile([P, G * N], U32, name="w4_w", align_bytes=64)
         quantize_w4(w4_bf)
-        finish(lo0, y30, (0, 1))
-        make_a(v1, a1, range(A1_EARLY, 8), CHUNK, CHUNK)
+        finish(lo0, y3[0], 0)
         b3 = make_b(x3, (6,))
-        y31 = upper(hi1)
+        upper(hi1, y3[1])
         b4 = make_b(x3, (7,))
         hi2, lo2 = envelopes(a1, b2, (4, 5))
-        y32 = upper(hi2)
-        finish(lo1, y31, (2, 3))
-        hi3, lo3 = envelopes(a1, b3, (6,))
-        y33 = upper(hi3)
-        hi4, lo4 = envelopes(a1, b4, (7,))
-        y34 = upper(hi4)
-        finish(lo2, y32, (4, 5))
-        finish(lo3, y33, (6,), "b_bank", 3)
-        finish(lo4, y34, (7,), "b_bank", 3)
+        upper(hi2, y3[2])
+        finish(lo1, y3[1], 1)
+        hi3 = envelope("hi", ALU.max, a1, b3, (6,))
+        lo3 = envelope("lo", ALU.min, a1, b3, (6,))
+        hi4 = envelope("hi", ALU.max, a1, b4, (7,))
+        upper(quantize_envelope("hi", hi3), y3[3][:, :, :P])
+        upper(quantize_envelope("hi", hi4), y3[3][:, :, P:])
+        lo4 = envelope("lo", ALU.min, a1, b4, (7,))
+        lo3 = quantize_envelope("lo", lo3)
+        lo4 = quantize_envelope("lo", lo4)
+        finish(lo2, y3[2], 2)
+        for n in range(NT):
+            bank = psum.tile([P, 1, CHUNK], F32, name="last", tag="b_bank", bufs=3)
+            project(bank[:, :, :P], w4_w, w4_s, lo3, (n,))
+            project(bank[:, :, P:], w4_w, w4_s, lo4, (n,))
+            multiply(bank, y3[3], (n,), 3)

@@ -23,7 +23,6 @@ G = H // PASS
 HALF = 512
 CHUNK = 256
 NT = N // P
-W2_PIECE = 256
 A1_EARLY = 8
 LIST_ROWS = 16
 
@@ -52,8 +51,7 @@ def tile_list_calving_retreat_features_kernel(
         x_plane = [keep.tile([P, T], F32, name=f"x_plane{t}") for t in range(PACK)]
         change = keep.tile([P, PACK + 4, HALF], F32, name="change", align_bytes=64)
         change01, change23 = change[:, 4:, :], change[:, 2 : PACK + 2, :]
-        w2_raw = [keep.tile([P, PACK, W2_PIECE], F32, name=f"w2_raw{i}", tag=f"w2_raw{i}")[:] for i in range(3)]
-        w2_raw.append(change[:, :PACK, :W2_PIECE])
+        w2_raw = [keep.tile([P, PACK, PASS], F32, name="w2_first")[:], change[:, :PACK, :]]
         w4_raw = [
             keep.tile([P, PACK, N], F32, name="w4_raw0"),
             keep.tile([P, PACK, N], F32, name="w4_raw1"),
@@ -68,7 +66,7 @@ def tile_list_calving_retreat_features_kernel(
             nc.sync.dma_start(out=x_plane[t][:], in_=x_rows[:, t, :])
 
         def load_w2(i):
-            nc.sync.dma_start(out=w2_raw[i], in_=w2_rows[:, :, i * W2_PIECE : (i + 1) * W2_PIECE])
+            nc.sync.dma_start(out=w2_raw[i], in_=w2_rows[:, :, i * PASS : (i + 1) * PASS])
 
         def load_w4(g):
             nc.sync.dma_start(
@@ -88,15 +86,14 @@ def tile_list_calving_retreat_features_kernel(
         for q in range(4):
             load_scale_rows(w1s_raw[:].bitcast(I32), w1_scales[0].bitcast(I32), q)
         nc.sync.dma_start(out=bias[:], in_=b1.rearrange("(g p t) -> p g t", g=G, t=PACK))
-        load_w2(0)
         load_x(0)
         nc.sync.dma_start(idx3[:], offs3)
         nc.sync.dma_start(idx2[:], offs2)
+        load_x(1)
+        load_w2(0)
+        load_x(2)
+        load_x(3)
         load_w2(1)
-        for t in range(1, PACK):
-            load_x(t)
-        load_w2(2)
-        load_w2(3)
         for g in range(G):
             load_w4(g)
         nc.gpsimd.memset(w3_s[:].bitcast(I32), 0)
@@ -136,13 +133,16 @@ def tile_list_calving_retreat_features_kernel(
                         bias=bias[:, g, t : t + 1],
                     )
 
-        def round_w2(copy, staged, i):
-            g, first = divmod(i * W2_PIECE // PACK, P)
-            by_pass = staged[:].rearrange("p (g t m j) -> p g m j t", g=G, t=PACK, j=PACK)
+        def round_w2(copy, staged, piece):
+            g, u = divmod(piece, 2)
             copy(
-                out=by_pass[:, g, first : first + W2_PIECE // PACK],
-                in_=w2_raw[i].rearrange("p j (m t) -> p m j t", t=PACK),
+                out=staged[:, piece * H : (piece + 1) * H].rearrange("p (t m j) -> p m j t", t=2, j=PACK),
+                in_=w2_raw[g].rearrange("p j (m t) -> p m j t", t=PACK)[:, :, :, 2 * u : 2 * u + 2],
             )
+
+        def pool_copy(out, in_):
+            order = "p m j t -> p t m j"
+            nc.gpsimd.tensor_scalar(out.rearrange(order), in_.rearrange(order), 1.0, 0.0, ALU.mult, ALU.add)
 
         def gather_before(before, t, start):
             nc.vector.tensor_copy(before, x_plane[t][:].indirect(offsets(idx3, start, before.shape[1])))
@@ -277,23 +277,24 @@ def tile_list_calving_retreat_features_kernel(
             in_=w1s_raw[:].rearrange("p (g m t) -> p g t m", g=G, t=PACK),
         )
         w2_bf = keep.tile([P, PACK * H], BF16, name="w2_bf", align_bytes=64)
-        round_w2(nc.scalar.copy, w2_bf, 0)
-        a0 = keep.tile([P, 2, HALF // P, G, P, 2], BF16, name="a0", tag="w2_raw0")
+        a0 = keep.tile([P, 2, HALF // P, G, P, 2], BF16, name="a0")
         a1 = keep.tile([P, 2, HALF // P, G, P, 2], BF16, name="a1")
         make_a((v_w0, v_s[:, :HALF]), a0, range(8))
         v_w1 = keep.tile([P, HALF], U32, name="v_w1", tag="w1s_raw", align_bytes=64)
         gather_words(v_w1, 1)
         v1 = (v_w1, v_s[:, HALF:])
-        for i in range(1, H // W2_PIECE):
-            round_w2(nc.vector.tensor_copy if i == 2 else nc.scalar.copy, w2_bf, i)
         make_a(v1, a1, range(A1_EARLY))
         before_late = []
         for t in range(PACK):
-            early = ring.tile([P, HALF], F32, name="early")
-            gather_before(early[:], t, 0)
+            if t < PACK - 1:
+                early = w2_bf[:, t * H : (t + 1) * H].bitcast(F32)
+            else:
+                early = keep.tile([P, HALF], F32, name="early")[:]
+            gather_before(early, t, 0)
             before_late.append(keep.tile([P, HALF], F32, name=f"before_late{t}"))
             gather_before(before_late[t][:], t, HALF)
-            gather_change(change01, early[:], t, 0)
+            gather_change(change01, early, t, 0)
+            round_w2(pool_copy if t < PACK - 1 else nc.scalar.copy, w2_bf, t)
         x_bf = [change[:, c, :].bitcast(BF16) for c in range(2)]
         for c in range(2):
             round_x(x_bf[c], change01[:, :, c * CHUNK : (c + 1) * CHUNK])

@@ -42,7 +42,7 @@ def tile_list_calving_retreat_features_kernel(
         tab_w = keep.tile([P, T], I32, name="tab_w", align_bytes=64)
         tab_s = keep.tile([P, T], U8, name="tab_s", align_bytes=64)
         w1_raw = keep.tile([P, 2 * H], U8, name="w1_raw", align_bytes=64)
-        w1s_raw = keep.tile([P, H], U8, name="w1s_raw", tag="w1s_raw", align_bytes=64)
+        w1s_raw = keep.tile([P, H], U8, name="w1s_raw", align_bytes=64)
         w1_w = keep.tile([P, 2 * H], U8, name="w1_w", align_bytes=64)
         w1_s = keep.tile([P, H], U8, name="w1_s", align_bytes=64)
         bias = keep.tile([P, G, PACK], F32, name="bias")
@@ -185,7 +185,7 @@ def tile_list_calving_retreat_features_kernel(
             return b_bf
 
         def envelope(name, op, a_bf, b_bf, subs):
-            env = ring.tile([P, len(subs) * G * P * PACK], BF16, name=f"{name}_bf", align_bytes=64)
+            env = ring.tile([P, len(subs) * G * P * PACK], BF16, name=f"{name}_bf", align_bytes=64, bufs=3)
             first = subs[0] % PACK
             nc.vector.tensor_tensor(
                 env[:].rearrange("p (n u e) -> p n u e", u=2, e=2),
@@ -252,17 +252,21 @@ def tile_list_calving_retreat_features_kernel(
                 project(bank, w3_flat, w3_s, hi, rows)
                 nc.scalar.copy(out=y3[:, rows[0] : rows[-1] + 1, :], in_=bank[:])
 
-        def multiply(bank, y3, rows, c):
-            res = ring.tile([P, len(rows), CHUNK], F32, name="res", bufs=8)
-            span = slice(rows[0], rows[-1] + 1)
-            nc.vector.tensor_tensor(res[:], bank[:], y3[:, span, :], ALU.mult)
-            nc.sync.dma_start(out=out_rows[:, span, c * CHUNK : (c + 1) * CHUNK], in_=res[:])
+        def lower(lo, rows, tag, bufs):
+            bank = psum.tile([P, len(rows), CHUNK], F32, name="y4_bank", tag=tag, bufs=bufs)
+            project(bank, w4_w, w4_s, lo, rows)
+            return bank
 
-        def finish(lo, y3, c):
-            for rows in row_groups(CHUNK):
-                bank = psum.tile([P, len(rows), CHUNK], F32, name="y4_bank", bufs=2)
-                project(bank, w4_w, w4_s, lo, rows)
-                multiply(bank, y3, rows, c)
+        def lower_last_row(los):
+            y4 = ring.tile([P, len(los), CHUNK], F32, name="y4")
+            bank = psum.tile([P, len(los), CHUNK], F32, name="y4_row", tag="ay", bufs=3)
+            for i, lo in enumerate(los):
+                project(bank[:, i : i + 1, :], w4_w, w4_s, lo, (NT - 1,))
+            nc.scalar.copy(out=y4[:], in_=bank[:])
+            return y4[:].rearrange("p c j -> p (c j)")
+
+        def store(res, rows, start):
+            nc.sync.dma_start(out=out_rows[:, rows, start : start + res.shape[2]], in_=res)
 
         v_s = keep.tile([P, S], U8, name="v_s", align_bytes=64)
         nc.vector.tensor_copy(v_s[:], tab_s[:].indirect(idx[:]))
@@ -272,7 +276,7 @@ def tile_list_calving_retreat_features_kernel(
         )
         v_w0 = keep.tile([P, HALF], U32, name="v_w0", align_bytes=64)
         gather_words(v_w0, 0)
-        nc.vector.tensor_copy(
+        nc.gpsimd.tensor_copy(
             out=w1_s[:].rearrange("p (g t m) -> p g t m", g=G, t=PACK),
             in_=w1s_raw[:].rearrange("p (g m t) -> p g t m", g=G, t=PACK),
         )
@@ -280,7 +284,7 @@ def tile_list_calving_retreat_features_kernel(
         a0 = keep.tile([P, 2, HALF // P, G, P, 2], BF16, name="a0")
         a1 = keep.tile([P, 2, HALF // P, G, P, 2], BF16, name="a1")
         make_a((v_w0, v_s[:, :HALF]), a0, range(8))
-        v_w1 = keep.tile([P, HALF], U32, name="v_w1", tag="w1s_raw", align_bytes=64)
+        v_w1 = keep.tile([P, HALF], U32, name="v_w1", align_bytes=64)
         gather_words(v_w1, 1)
         v1 = (v_w1, v_s[:, HALF:])
         make_a(v1, a1, range(A1_EARLY))
@@ -316,31 +320,51 @@ def tile_list_calving_retreat_features_kernel(
         x2 = quantize_x(x_late[:, 0, :], "x_w2")
         hi0, lo0 = envelopes(a0, b0, (0, 1))
         b2 = make_b(x2, (4, 5))
-        y3 = [keep.tile([P, NT, CHUNK], F32, name=f"y3_{c}") for c in range(S // CHUNK)]
-        upper(hi0, y3[0])
+        y3 = keep.tile([P, NT, S], F32, name="y3")
+        upper(hi0, y3[:, :, :CHUNK])
         round_x(x_late[:, 1, :], change23[:, :, CHUNK:])
         x3 = quantize_x(x_late[:, 1, :], "x_w3")
         hi1, lo1 = envelopes(a0, b1_, (2, 3))
         w4_w = keep.tile([P, G * N], U32, name="w4_w", align_bytes=64)
         quantize_w4(w4_bf)
-        finish(lo0, y3[0], 0)
         b3 = make_b(x3, (6,))
-        upper(hi1, y3[1])
+        upper(hi1, y3[:, :, CHUNK:HALF])
         b4 = make_b(x3, (7,))
-        hi2, lo2 = envelopes(a1, b2, (4, 5))
-        upper(hi2, y3[2])
-        finish(lo1, y3[1], 1)
+        banks = [lower(lo, (0, 1), "y4", 2) for lo in (lo0, lo1)]
+        y4_early = lower_last_row((lo0, lo1))
+        hi2_bf = envelope("hi", ALU.max, a1, b2, (4, 5))
+        lo2_bf = envelope("lo", ALU.min, a1, b2, (4, 5))
+        hi2 = quantize_envelope("hi", hi2_bf)
+        lo2 = quantize_envelope("lo", lo2_bf)
+        res = hi2_bf[:].bitcast(F32).rearrange("p (n j) -> p n j", n=2)
+        for c in range(2):
+            cols = slice(c * CHUNK, (c + 1) * CHUNK)
+            nc.vector.tensor_tensor(res[:, :, cols], banks[c][:], y3[:, :2, cols], ALU.mult)
+        store(res, slice(0, 2), 0)
+        res = lo2_bf[:].bitcast(F32)[:, :HALF]
+        nc.gpsimd.tensor_tensor(res, y4_early, y3[:, 2, :HALF], ALU.mult)
+        store(res.unsqueeze(1), slice(2, 3), 0)
+        upper(hi2, y3[:, :, HALF : HALF + CHUNK])
+        y4_late = lower_last_row((lo2,))
         hi3 = envelope("hi", ALU.max, a1, b3, (6,))
         lo3 = envelope("lo", ALU.min, a1, b3, (6,))
         hi4 = envelope("hi", ALU.max, a1, b4, (7,))
-        upper(quantize_envelope("hi", hi3), y3[3][:, :, :P])
-        upper(quantize_envelope("hi", hi4), y3[3][:, :, P:])
-        lo4 = envelope("lo", ALU.min, a1, b4, (7,))
+        upper(quantize_envelope("hi", hi3), y3[:, :, S - CHUNK : S - P])
+        upper(quantize_envelope("hi", hi4), y3[:, :, S - P :])
+        lo4_bf = envelope("lo", ALU.min, a1, b4, (7,))
         lo3 = quantize_envelope("lo", lo3)
-        lo4 = quantize_envelope("lo", lo4)
-        finish(lo2, y3[2], 2)
+        lo4 = quantize_envelope("lo", lo4_bf)
+        cols = slice(HALF, HALF + CHUNK)
+        res = lo4_bf[:].bitcast(F32)[:, :CHUNK]
+        nc.gpsimd.tensor_tensor(res, y4_late, y3[:, 2, cols], ALU.mult)
+        store(res.unsqueeze(1), slice(2, 3), HALF)
+        res = keep.tile([P, 2, CHUNK], F32, name="res2")
+        nc.vector.tensor_tensor(res[:], lower(lo2, (0, 1), "y4", 2)[:], y3[:, :2, cols], ALU.mult)
+        store(res[:], slice(0, 2), HALF)
         for n in range(NT):
             bank = psum.tile([P, 1, CHUNK], F32, name="last", tag="b_bank", bufs=3)
             project(bank[:, :, :P], w4_w, w4_s, lo3, (n,))
             project(bank[:, :, P:], w4_w, w4_s, lo4, (n,))
-            multiply(bank, y3[3], (n,), 3)
+            res = ring.tile([P, 1, CHUNK], F32, name="res", bufs=3)
+            nc.vector.tensor_tensor(res[:], bank[:], y3[:, n : n + 1, S - CHUNK :], ALU.mult)
+            store(res[:], slice(n, n + 1), S - CHUNK)

@@ -166,7 +166,7 @@ def tile_list_calving_retreat_features_kernel(
 
         def make_b(x, subs):
             x_w, x_s = x
-            b_bf = ring.tile([P, len(subs), G, P, PACK], BF16, name="b_bf", bufs=4)
+            b_bf = ring.tile([P, len(subs), G, P, PACK], BF16, name="b_bf", bufs=5)
             for i, sub in enumerate(subs):
                 tokens = slice(sub % 2 * P, (sub % 2 + 1) * P)
                 for g in range(G):
@@ -207,10 +207,10 @@ def tile_list_calving_retreat_features_kernel(
             lo = envelope("lo", ALU.min, a_bf, b_bf, subs)
             return quantize_envelope("hi", hi), quantize_envelope("lo", lo)
 
-        def round_w4(copy, staged, g):
-            copy(
-                out=staged[:, g * N * PACK : (g + 1) * N * PACK].rearrange("p (c i t) -> p c t i", i=4, t=PACK),
-                in_=w4_raw[g][:].rearrange("p t (c i) -> p c t i", i=4),
+        def round_w4(staged, g, first, last):
+            nc.scalar.copy(
+                out=staged[:, (g * N + first) * PACK : (g * N + last) * PACK].rearrange("p (c i t) -> p c t i", i=4, t=PACK),
+                in_=w4_raw[g][:, :, first:last].rearrange("p t (c i) -> p c t i", i=4),
             )
 
         def quantize_w4(staged):
@@ -265,8 +265,8 @@ def tile_list_calving_retreat_features_kernel(
             nc.scalar.copy(out=y4[:], in_=bank[:])
             return y4[:].rearrange("p c j -> p (c j)")
 
-        def store(res, rows, start):
-            nc.sync.dma_start(out=out_rows[:, rows, start : start + res.shape[2]], in_=res)
+        def store(res, rows, start, queue=nc.sync):
+            queue.dma_start(out=out_rows[:, rows, start : start + res.shape[2]], in_=res)
 
         v_s = keep.tile([P, S], U8, name="v_s", align_bytes=64)
         nc.vector.tensor_copy(v_s[:], tab_s[:].indirect(idx[:]))
@@ -311,12 +311,13 @@ def tile_list_calving_retreat_features_kernel(
         for t in (2, 3):
             gather_change(change23, before_late[t][:], t, HALF)
         w4_bf = keep.tile([P, G * N * PACK], BF16, name="w4_bf", align_bytes=64)
-        round_w4(nc.scalar.copy, w4_bf, 0)
+        round_w4(w4_bf, 0, 0, N)
+        round_w4(w4_bf, 1, 0, N // 2)
         b0 = make_b(x0, (0, 1))
         x_late = keep.tile([P, 2, CHUNK * PACK], BF16, name="x_late", align_bytes=64)
         round_x(x_late[:, 0, :], change23[:, :, :CHUNK])
         b1_ = make_b(x1, (2, 3))
-        round_w4(nc.scalar.copy, w4_bf, 1)
+        round_w4(w4_bf, 1, N // 2, N)
         x2 = quantize_x(x_late[:, 0, :], "x_w2")
         hi0, lo0 = envelopes(a0, b0, (0, 1))
         b2 = make_b(x2, (4, 5))
@@ -327,37 +328,37 @@ def tile_list_calving_retreat_features_kernel(
         hi1, lo1 = envelopes(a0, b1_, (2, 3))
         w4_w = keep.tile([P, G * N], U32, name="w4_w", align_bytes=64)
         quantize_w4(w4_bf)
-        b3 = make_b(x3, (6,))
         upper(hi1, y3[:, :, CHUNK:HALF])
-        b4 = make_b(x3, (7,))
-        banks = [lower(lo, (0, 1), "y4", 2) for lo in (lo0, lo1)]
         y4_early = lower_last_row((lo0, lo1))
+        b3 = make_b(x3, (6,))
+        banks = [lower(lo, (0, 1), "y4", 2) for lo in (lo0, lo1)]
+        b4 = make_b(x3, (7,))
         hi2_bf = envelope("hi", ALU.max, a1, b2, (4, 5))
         lo2_bf = envelope("lo", ALU.min, a1, b2, (4, 5))
         hi2 = quantize_envelope("hi", hi2_bf)
         lo2 = quantize_envelope("lo", lo2_bf)
-        res = hi2_bf[:].bitcast(F32).rearrange("p (n j) -> p n j", n=2)
+        res = b2[:].rearrange("p c g n t -> p (c g n t)").bitcast(F32).rearrange("p (n j) -> p n j", n=2)
         for c in range(2):
             cols = slice(c * CHUNK, (c + 1) * CHUNK)
             nc.vector.tensor_tensor(res[:, :, cols], banks[c][:], y3[:, :2, cols], ALU.mult)
         store(res, slice(0, 2), 0)
-        res = lo2_bf[:].bitcast(F32)[:, :HALF]
+        res = hi2_bf[:].bitcast(F32)[:, :HALF]
         nc.gpsimd.tensor_tensor(res, y4_early, y3[:, 2, :HALF], ALU.mult)
         store(res.unsqueeze(1), slice(2, 3), 0)
         upper(hi2, y3[:, :, HALF : HALF + CHUNK])
         y4_late = lower_last_row((lo2,))
         hi3 = envelope("hi", ALU.max, a1, b3, (6,))
-        lo3 = envelope("lo", ALU.min, a1, b3, (6,))
+        lo3_bf = envelope("lo", ALU.min, a1, b3, (6,))
         hi4 = envelope("hi", ALU.max, a1, b4, (7,))
         upper(quantize_envelope("hi", hi3), y3[:, :, S - CHUNK : S - P])
         upper(quantize_envelope("hi", hi4), y3[:, :, S - P :])
         lo4_bf = envelope("lo", ALU.min, a1, b4, (7,))
-        lo3 = quantize_envelope("lo", lo3)
+        lo3 = quantize_envelope("lo", lo3_bf)
         lo4 = quantize_envelope("lo", lo4_bf)
         cols = slice(HALF, HALF + CHUNK)
-        res = lo4_bf[:].bitcast(F32)[:, :CHUNK]
+        res = lo3_bf[:].bitcast(F32)[:, :CHUNK]
         nc.gpsimd.tensor_tensor(res, y4_late, y3[:, 2, cols], ALU.mult)
-        store(res.unsqueeze(1), slice(2, 3), HALF)
+        store(res.unsqueeze(1), slice(2, 3), HALF, nc.scalar)
         res = keep.tile([P, 2, CHUNK], F32, name="res2")
         nc.vector.tensor_tensor(res[:], lower(lo2, (0, 1), "y4", 2)[:], y3[:, :2, cols], ALU.mult)
         store(res[:], slice(0, 2), HALF)

@@ -49,11 +49,11 @@ def tile_list_calving_retreat_features_kernel(
         w3_w = keep.tile([P, G, N], I32, name="w3_w", align_bytes=64)
         w3_s = keep.tile([P, G * N], U8, name="w3_s", align_bytes=64)
         x_plane = [keep.tile([P, T], F32, name=f"x_plane{t}") for t in range(PACK)]
-        change = keep.tile([P, PACK + 4, HALF], F32, name="change", align_bytes=64)
-        change01, change23 = change[:, 4:, :], change[:, 2 : PACK + 2, :]
+        change = keep.tile([P, 2 * PACK + 1, HALF], F32, name="change", align_bytes=64)
+        change01, change23 = change[:, PACK + 1 :, :], change[:, PACK - 1 : 2 * PACK - 1, :]
         w2_raw = [keep.tile([P, PACK, PASS], F32, name="w2_first")[:], change[:, :PACK, :]]
         w4_raw = [
-            keep.tile([P, PACK, N], F32, name="w4_raw0"),
+            keep.tile([P, PACK, N], F32, name="w4_raw0", align_bytes=64),
             keep.tile([P, PACK, N], F32, name="w4_raw1"),
         ]
         w2_s = keep.tile([P, H], U8, name="w2_s", align_bytes=64)
@@ -76,7 +76,7 @@ def tile_list_calving_retreat_features_kernel(
         x_rows = xT.rearrange("(p t) c -> p t c", t=PACK)
         w2_rows = w2.rearrange("(p t) r -> p t r", t=PACK)
 
-        nc.vector.memset(tab_s[:].bitcast(I32), 0)
+        nc.gpsimd.memset(tab_s[:].bitcast(I32), 0)
         nc.vector.memset(w1s_raw[:].bitcast(I32), 0)
         nc.sync.dma_start(idx[:], offs)
         nc.sync.dma_start(out=w1_raw[:].bitcast(I32), in_=w1_words[0].bitcast(I32))
@@ -86,10 +86,10 @@ def tile_list_calving_retreat_features_kernel(
         for q in range(4):
             load_scale_rows(w1s_raw[:].bitcast(I32), w1_scales[0].bitcast(I32), q)
         nc.sync.dma_start(out=bias[:], in_=b1.rearrange("(g p t) -> p g t", g=G, t=PACK))
-        load_x(0)
+        load_x(1)
         nc.sync.dma_start(idx3[:], offs3)
         nc.sync.dma_start(idx2[:], offs2)
-        load_x(1)
+        load_x(0)
         load_w2(0)
         load_x(2)
         load_x(3)
@@ -276,10 +276,12 @@ def tile_list_calving_retreat_features_kernel(
         )
         v_w0 = keep.tile([P, HALF], U32, name="v_w0", align_bytes=64)
         gather_words(v_w0, 0)
-        nc.gpsimd.tensor_copy(
-            out=w1_s[:].rearrange("p (g t m) -> p g t m", g=G, t=PACK),
-            in_=w1s_raw[:].rearrange("p (g m t) -> p g t m", g=G, t=PACK),
-        )
+        for g in range(G):
+            cols = slice(g * PASS, (g + 1) * PASS)
+            nc.gpsimd.tensor_copy(
+                out=w1_s[:, cols].rearrange("p (t m) -> p t m", t=PACK),
+                in_=w1s_raw[:, cols].rearrange("p (m t) -> p t m", t=PACK),
+            )
         w2_bf = keep.tile([P, PACK * H], BF16, name="w2_bf", align_bytes=64)
         a0 = keep.tile([P, 2, HALF // P, G, P, 2], BF16, name="a0")
         a1 = keep.tile([P, 2, HALF // P, G, P, 2], BF16, name="a1")
@@ -288,36 +290,44 @@ def tile_list_calving_retreat_features_kernel(
         gather_words(v_w1, 1)
         v1 = (v_w1, v_s[:, HALF:])
         make_a(v1, a1, range(A1_EARLY))
-        before_late = []
-        for t in range(PACK):
-            if t < PACK - 1:
-                early = w2_bf[:, t * H : (t + 1) * H].bitcast(F32)
+        before_late = {}
+        w4_bf = keep.tile([P, G * N * PACK], BF16, name="w4_bf", align_bytes=64)
+        early = keep.tile([P, HALF], F32, name="early")[:]
+        late = w2_bf[:, :H].bitcast(F32)
+        gather_before(early, 1, 0)
+        gather_before(late, 1, HALF)
+        gather_change(change01, early, 1, 0)
+        gather_change(change23, late, 1, HALF)
+        round_w2(pool_copy, w2_bf, 0)
+        for piece, t in enumerate((0, 2, 3), start=1):
+            if piece < PACK - 1:
+                early = w2_bf[:, piece * H : (piece + 1) * H].bitcast(F32)
             else:
                 early = keep.tile([P, HALF], F32, name="early")[:]
             gather_before(early, t, 0)
-            before_late.append(keep.tile([P, HALF], F32, name=f"before_late{t}"))
-            gather_before(before_late[t][:], t, HALF)
+            if t < PACK - 1:
+                before_late[t] = keep.tile([P, HALF], F32, name=f"before_late{t}")[:]
+            else:
+                before_late[t] = w4_bf[:, N * PACK : N * PACK + 2 * HALF].bitcast(F32)
+            gather_before(before_late[t], t, HALF)
             gather_change(change01, early, t, 0)
-            round_w2(pool_copy if t < PACK - 1 else nc.scalar.copy, w2_bf, t)
-        x_bf = [change[:, c, :].bitcast(BF16) for c in range(2)]
+            round_w2(pool_copy if piece < PACK - 1 else nc.scalar.copy, w2_bf, piece)
+        round_w4(w4_bf, 0, 0, N)
+        x_bf = [w4_raw[0][:].rearrange("p t n -> p (t n)")[:, c * HALF : (c + 1) * HALF].bitcast(BF16) for c in range(2)]
         for c in range(2):
             round_x(x_bf[c], change01[:, :, c * CHUNK : (c + 1) * CHUNK])
-        gather_change(change23, before_late[0][:], 0, HALF)
+        gather_change(change23, before_late[0], 0, HALF)
         w2_w = keep.tile([P, H], U32, name="w2_w", align_bytes=64)
         nc.vector.quantize_mx(out=w2_w[:].bitcast(E4M3), scales=w2_s[:], in_=w2_bf[:])
-        gather_change(change23, before_late[1][:], 1, HALF)
         x0 = quantize_x(x_bf[0], "x_w0")
         x1 = quantize_x(x_bf[1], "x_w1")
         for t in (2, 3):
-            gather_change(change23, before_late[t][:], t, HALF)
-        w4_bf = keep.tile([P, G * N * PACK], BF16, name="w4_bf", align_bytes=64)
-        round_w4(w4_bf, 0, 0, N)
-        round_w4(w4_bf, 1, 0, N // 2)
+            gather_change(change23, before_late[t], t, HALF)
         b0 = make_b(x0, (0, 1))
         x_late = keep.tile([P, 2, CHUNK * PACK], BF16, name="x_late", align_bytes=64)
         round_x(x_late[:, 0, :], change23[:, :, :CHUNK])
         b1_ = make_b(x1, (2, 3))
-        round_w4(w4_bf, 1, N // 2, N)
+        round_w4(w4_bf, 1, 0, N)
         x2 = quantize_x(x_late[:, 0, :], "x_w2")
         hi0, lo0 = envelopes(a0, b0, (0, 1))
         b2 = make_b(x2, (4, 5))

@@ -49,12 +49,12 @@ def tile_list_calving_retreat_features_kernel(
         w3_w = keep.tile([P, G, N], I32, name="w3_w", align_bytes=64)
         w3_s = keep.tile([P, G * N], U8, name="w3_s", align_bytes=64)
         x_plane = [keep.tile([P, T], F32, name=f"x_plane{t}") for t in range(PACK)]
-        change = keep.tile([P, 2 * PACK + 1, HALF], F32, name="change", align_bytes=64)
-        change01, change23 = change[:, PACK + 1 :, :], change[:, PACK - 1 : 2 * PACK - 1, :]
-        w2_raw = [keep.tile([P, PACK, PASS], F32, name="w2_first")[:], change[:, :PACK, :]]
+        change = keep.tile([P, 2 * PACK, HALF], F32, name="change", align_bytes=64)
+        change01, change23 = change[:, PACK:, :], change[:, 2 : PACK + 2, :]
+        w2_raw = [keep.tile([P, PACK, PASS], F32, name=f"w2_raw{g}")[:] for g in range(G)]
         w4_raw = [
-            keep.tile([P, PACK, N], F32, name="w4_raw0", align_bytes=64),
-            keep.tile([P, PACK, N], F32, name="w4_raw1"),
+            change[:, :NT, :].rearrange("p r c -> p (r c)").rearrange("p (t n) -> p t n", t=PACK),
+            keep.tile([P, PACK, N], F32, name="w4_raw1")[:],
         ]
         w2_s = keep.tile([P, H], U8, name="w2_s", align_bytes=64)
         w4_s = keep.tile([P, G * N], U8, name="w4_s", align_bytes=64)
@@ -65,12 +65,12 @@ def tile_list_calving_retreat_features_kernel(
         def load_x(t):
             nc.sync.dma_start(out=x_plane[t][:], in_=x_rows[:, t, :])
 
-        def load_w2(i):
-            nc.sync.dma_start(out=w2_raw[i], in_=w2_rows[:, :, i * PASS : (i + 1) * PASS])
+        def load_w2(g, first=0, last=PASS):
+            nc.sync.dma_start(out=w2_raw[g][:, :, first:last], in_=w2_rows[:, :, g * PASS + first : g * PASS + last])
 
         def load_w4(g):
             nc.sync.dma_start(
-                out=w4_raw[g][:], in_=w4[g * PASS : (g + 1) * PASS, :].rearrange("(p t) n -> p t n", t=PACK)
+                out=w4_raw[g], in_=w4[g * PASS : (g + 1) * PASS, :].rearrange("(p t) n -> p t n", t=PACK)
             )
 
         x_rows = xT.rearrange("(p t) c -> p t c", t=PACK)
@@ -89,11 +89,13 @@ def tile_list_calving_retreat_features_kernel(
         load_x(1)
         nc.sync.dma_start(idx3[:], offs3)
         nc.sync.dma_start(idx2[:], offs2)
+        load_w2(0, 0, PASS // 2)
         load_x(0)
-        load_w2(0)
+        load_w2(0, PASS // 2, PASS)
         load_x(2)
+        load_w2(1, 0, PASS // 2)
         load_x(3)
-        load_w2(1)
+        load_w2(1, PASS // 2, PASS)
         for g in range(G):
             load_w4(g)
         nc.gpsimd.memset(w3_s[:].bitcast(I32), 0)
@@ -133,11 +135,11 @@ def tile_list_calving_retreat_features_kernel(
                         bias=bias[:, g, t : t + 1],
                     )
 
-        def round_w2(copy, staged, piece):
-            g, u = divmod(piece, 2)
+        def round_w2(copy, staged, g, planes, columns):
+            half = staged[:, g * PACK * PASS : (g + 1) * PACK * PASS]
             copy(
-                out=staged[:, piece * H : (piece + 1) * H].rearrange("p (t m j) -> p m j t", t=2, j=PACK),
-                in_=w2_raw[g].rearrange("p j (m t) -> p m j t", t=PACK)[:, :, :, 2 * u : 2 * u + 2],
+                out=half.rearrange("p (t m j) -> p m j t", t=PACK, j=PACK)[:, columns, :, planes],
+                in_=w2_raw[g].rearrange("p j (m t) -> p m j t", t=PACK)[:, columns, :, planes],
             )
 
         def pool_copy(out, in_):
@@ -258,12 +260,12 @@ def tile_list_calving_retreat_features_kernel(
             return bank
 
         def lower_last_row(los):
-            y4 = ring.tile([P, len(los), CHUNK], F32, name="y4")
+            y4 = ring.tile([P, CHUNK], F32, name="y4")
             bank = psum.tile([P, len(los), CHUNK], F32, name="y4_row", tag="ay", bufs=3)
             for i, lo in enumerate(los):
                 project(bank[:, i : i + 1, :], w4_w, w4_s, lo, (NT - 1,))
-            nc.scalar.copy(out=y4[:], in_=bank[:])
-            return y4[:].rearrange("p c j -> p (c j)")
+            nc.scalar.copy(out=y4[:], in_=bank[:, 0, :])
+            return y4[:], bank
 
         def store(res, rows, start, queue=nc.sync):
             queue.dma_start(out=out_rows[:, rows, start : start + res.shape[2]], in_=res)
@@ -282,7 +284,7 @@ def tile_list_calving_retreat_features_kernel(
                 out=w1_s[:, cols].rearrange("p (t m) -> p t m", t=PACK),
                 in_=w1s_raw[:, cols].rearrange("p (m t) -> p t m", t=PACK),
             )
-        w2_bf = keep.tile([P, PACK * H], BF16, name="w2_bf", align_bytes=64)
+        w2_bf = keep.tile([P, PACK * H + H - CHUNK], BF16, name="w2_bf", align_bytes=64)
         a0 = keep.tile([P, 2, HALF // P, G, P, 2], BF16, name="a0")
         a1 = keep.tile([P, 2, HALF // P, G, P, 2], BF16, name="a1")
         make_a((v_w0, v_s[:, :HALF]), a0, range(8))
@@ -293,15 +295,17 @@ def tile_list_calving_retreat_features_kernel(
         before_late = {}
         w4_bf = keep.tile([P, G * N * PACK], BF16, name="w4_bf", align_bytes=64)
         early = keep.tile([P, HALF], F32, name="early")[:]
-        late = w2_bf[:, :H].bitcast(F32)
+        late = w2_bf[:, H : 2 * H].bitcast(F32)
+        low, high = slice(0, P // 2), slice(P // 2, P)
+        round_w2(pool_copy, w2_bf, 0, slice(0, 2), low)
         gather_before(early, 1, 0)
         gather_before(late, 1, HALF)
         gather_change(change01, early, 1, 0)
         gather_change(change23, late, 1, HALF)
-        round_w2(pool_copy, w2_bf, 0)
-        for piece, t in enumerate((0, 2, 3), start=1):
-            if piece < PACK - 1:
-                early = w2_bf[:, piece * H : (piece + 1) * H].bitcast(F32)
+        round_w2(pool_copy, w2_bf, 0, slice(2, PACK), slice(0, P))
+        for t, start, columns in ((0, 2 * H, low), (2, PACK * H - CHUNK, high), (3, None, None)):
+            if columns:
+                early = w2_bf[:, start : start + H].bitcast(F32)
             else:
                 early = keep.tile([P, HALF], F32, name="early")[:]
             gather_before(early, t, 0)
@@ -311,15 +315,17 @@ def tile_list_calving_retreat_features_kernel(
                 before_late[t] = w4_bf[:, N * PACK : N * PACK + 2 * HALF].bitcast(F32)
             gather_before(before_late[t], t, HALF)
             gather_change(change01, early, t, 0)
-            round_w2(pool_copy if piece < PACK - 1 else nc.scalar.copy, w2_bf, piece)
+            if columns:
+                round_w2(pool_copy, w2_bf, 1, slice(0, PACK), columns)
+        round_w2(nc.scalar.copy, w2_bf, 0, slice(0, 2), high)
         round_w4(w4_bf, 0, 0, N)
-        x_bf = [w4_raw[0][:].rearrange("p t n -> p (t n)")[:, c * HALF : (c + 1) * HALF].bitcast(BF16) for c in range(2)]
+        x_bf = [change[:, 2 - c, :].bitcast(BF16) for c in range(2)]
         for c in range(2):
             round_x(x_bf[c], change01[:, :, c * CHUNK : (c + 1) * CHUNK])
-        gather_change(change23, before_late[0], 0, HALF)
         w2_w = keep.tile([P, H], U32, name="w2_w", align_bytes=64)
-        nc.vector.quantize_mx(out=w2_w[:].bitcast(E4M3), scales=w2_s[:], in_=w2_bf[:])
+        nc.vector.quantize_mx(out=w2_w[:].bitcast(E4M3), scales=w2_s[:], in_=w2_bf[:, : PACK * H])
         x0 = quantize_x(x_bf[0], "x_w0")
+        gather_change(change23, before_late[0], 0, HALF)
         x1 = quantize_x(x_bf[1], "x_w1")
         for t in (2, 3):
             gather_change(change23, before_late[t], t, HALF)
@@ -339,7 +345,7 @@ def tile_list_calving_retreat_features_kernel(
         w4_w = keep.tile([P, G * N], U32, name="w4_w", align_bytes=64)
         quantize_w4(w4_bf)
         upper(hi1, y3[:, :, CHUNK:HALF])
-        y4_early = lower_last_row((lo0, lo1))
+        y4_early, row_bank = lower_last_row((lo0, lo1))
         b3 = make_b(x3, (6,))
         banks = [lower(lo, (0, 1), "y4", 2) for lo in (lo0, lo1)]
         b4 = make_b(x3, (7,))
@@ -353,10 +359,11 @@ def tile_list_calving_retreat_features_kernel(
             nc.vector.tensor_tensor(res[:, :, cols], banks[c][:], y3[:, :2, cols], ALU.mult)
         store(res, slice(0, 2), 0)
         res = hi2_bf[:].bitcast(F32)[:, :HALF]
-        nc.gpsimd.tensor_tensor(res, y4_early, y3[:, 2, :HALF], ALU.mult)
+        nc.gpsimd.tensor_tensor(res[:, :CHUNK], y4_early, y3[:, 2, :CHUNK], ALU.mult)
+        nc.vector.tensor_tensor(res[:, CHUNK:], row_bank[:, 1, :], y3[:, 2, CHUNK:HALF], ALU.mult)
         store(res.unsqueeze(1), slice(2, 3), 0)
         upper(hi2, y3[:, :, HALF : HALF + CHUNK])
-        y4_late = lower_last_row((lo2,))
+        y4_late, late_bank = lower_last_row((lo2,))
         hi3 = envelope("hi", ALU.max, a1, b3, (6,))
         lo3_bf = envelope("lo", ALU.min, a1, b3, (6,))
         hi4 = envelope("hi", ALU.max, a1, b4, (7,))

@@ -49,11 +49,12 @@ def tile_list_calving_retreat_features_kernel(
         w3_w = keep.tile([P, G, N], I32, name="w3_w", align_bytes=64)
         w3_s = keep.tile([P, G * N], U8, name="w3_s", align_bytes=64)
         x_plane = [keep.tile([P, T], F32, name=f"x_plane{t}") for t in range(PACK)]
-        change = keep.tile([P, 2 * PACK, HALF], F32, name="change", align_bytes=64)
-        change01, change23 = change[:, PACK:, :], change[:, 2 : PACK + 2, :]
+        change = keep.tile([P, PACK * HALF + HALF + CHUNK], F32, name="change", align_bytes=64)
+        change01 = change[:, HALF + CHUNK :].rearrange("p (t c) -> p t c", t=PACK)
+        change23 = change[:, : PACK * HALF].rearrange("p (t c) -> p t c", t=PACK)
         w2_raw = [keep.tile([P, PACK, PASS], F32, name=f"w2_raw{g}")[:] for g in range(G)]
         w4_raw = [
-            change[:, :NT, :].rearrange("p r c -> p (r c)").rearrange("p (t n) -> p t n", t=PACK),
+            keep.tile([P, PACK, N], F32, name="w4_raw0", align_bytes=64)[:],
             keep.tile([P, PACK, N], F32, name="w4_raw1")[:],
         ]
         w2_s = keep.tile([P, H], U8, name="w2_s", align_bytes=64)
@@ -82,15 +83,15 @@ def tile_list_calving_retreat_features_kernel(
         nc.sync.dma_start(out=w1_raw[:].bitcast(I32), in_=w1_words[0].bitcast(I32))
         for q in range(4):
             load_scale_rows(tab_s[:].bitcast(I32), tab_scales[0].bitcast(I32), q, (nc.sync, nc.scalar)[q % 2])
+        nc.sync.dma_start(idx3[:], offs3)
         nc.sync.dma_start(out=tab_w[:], in_=tab_words[0].rearrange("p c i -> p (c i)").bitcast(I32))
         for q in range(4):
             load_scale_rows(w1s_raw[:].bitcast(I32), w1_scales[0].bitcast(I32), q)
         nc.sync.dma_start(out=bias[:], in_=b1.rearrange("(g p t) -> p g t", g=G, t=PACK))
-        load_x(1)
-        nc.sync.dma_start(idx3[:], offs3)
+        load_x(0)
         nc.sync.dma_start(idx2[:], offs2)
         load_w2(0, 0, PASS // 2)
-        load_x(0)
+        load_x(1)
         load_w2(0, PASS // 2, PASS)
         load_x(2)
         load_w2(1, 0, PASS // 2)
@@ -259,13 +260,14 @@ def tile_list_calving_retreat_features_kernel(
             project(bank, w4_w, w4_s, lo, rows)
             return bank
 
-        def lower_last_row(los):
-            y4 = ring.tile([P, CHUNK], F32, name="y4")
+        def lower_last_row(los, copied):
+            y4 = ring.tile([P, copied], F32, name="y4")
             bank = psum.tile([P, len(los), CHUNK], F32, name="y4_row", tag="ay", bufs=3)
             for i, lo in enumerate(los):
                 project(bank[:, i : i + 1, :], w4_w, w4_s, lo, (NT - 1,))
-            nc.scalar.copy(out=y4[:], in_=bank[:, 0, :])
-            return y4[:], bank
+            row = bank[:].rearrange("p c j -> p (c j)")
+            nc.scalar.copy(out=y4[:], in_=row[:, :copied])
+            return y4[:], row[:, copied:]
 
         def store(res, rows, start, queue=nc.sync):
             queue.dma_start(out=out_rows[:, rows, start : start + res.shape[2]], in_=res)
@@ -298,12 +300,12 @@ def tile_list_calving_retreat_features_kernel(
         late = w2_bf[:, H : 2 * H].bitcast(F32)
         low, high = slice(0, P // 2), slice(P // 2, P)
         round_w2(pool_copy, w2_bf, 0, slice(0, 2), low)
-        gather_before(early, 1, 0)
-        gather_before(late, 1, HALF)
-        gather_change(change01, early, 1, 0)
-        gather_change(change23, late, 1, HALF)
+        gather_before(early, 0, 0)
+        gather_before(late, 0, HALF)
+        gather_change(change01, early, 0, 0)
+        gather_change(change23, late, 0, HALF)
         round_w2(pool_copy, w2_bf, 0, slice(2, PACK), slice(0, P))
-        for t, start, columns in ((0, 2 * H, low), (2, PACK * H - CHUNK, high), (3, None, None)):
+        for t, start, columns in ((1, 2 * H, low), (2, PACK * H - CHUNK, high), (3, None, None)):
             if columns:
                 early = w2_bf[:, start : start + H].bitcast(F32)
             else:
@@ -319,13 +321,13 @@ def tile_list_calving_retreat_features_kernel(
                 round_w2(pool_copy, w2_bf, 1, slice(0, PACK), columns)
         round_w2(nc.scalar.copy, w2_bf, 0, slice(0, 2), high)
         round_w4(w4_bf, 0, 0, N)
-        x_bf = [change[:, 2 - c, :].bitcast(BF16) for c in range(2)]
+        x_bf = [w4_raw[0].rearrange("p t n -> p (t n)")[:, c * HALF : (c + 1) * HALF].bitcast(BF16) for c in range(2)]
         for c in range(2):
             round_x(x_bf[c], change01[:, :, c * CHUNK : (c + 1) * CHUNK])
         w2_w = keep.tile([P, H], U32, name="w2_w", align_bytes=64)
         nc.vector.quantize_mx(out=w2_w[:].bitcast(E4M3), scales=w2_s[:], in_=w2_bf[:, : PACK * H])
         x0 = quantize_x(x_bf[0], "x_w0")
-        gather_change(change23, before_late[0], 0, HALF)
+        gather_change(change23, before_late[1], 1, HALF)
         x1 = quantize_x(x_bf[1], "x_w1")
         for t in (2, 3):
             gather_change(change23, before_late[t], t, HALF)
@@ -345,7 +347,7 @@ def tile_list_calving_retreat_features_kernel(
         w4_w = keep.tile([P, G * N], U32, name="w4_w", align_bytes=64)
         quantize_w4(w4_bf)
         upper(hi1, y3[:, :, CHUNK:HALF])
-        y4_early, row_bank = lower_last_row((lo0, lo1))
+        y4_early, row_bank = lower_last_row((lo0, lo1), HALF - P)
         b3 = make_b(x3, (6,))
         banks = [lower(lo, (0, 1), "y4", 2) for lo in (lo0, lo1)]
         b4 = make_b(x3, (7,))
@@ -359,11 +361,11 @@ def tile_list_calving_retreat_features_kernel(
             nc.vector.tensor_tensor(res[:, :, cols], banks[c][:], y3[:, :2, cols], ALU.mult)
         store(res, slice(0, 2), 0)
         res = hi2_bf[:].bitcast(F32)[:, :HALF]
-        nc.gpsimd.tensor_tensor(res[:, :CHUNK], y4_early, y3[:, 2, :CHUNK], ALU.mult)
-        nc.vector.tensor_tensor(res[:, CHUNK:], row_bank[:, 1, :], y3[:, 2, CHUNK:HALF], ALU.mult)
+        nc.gpsimd.tensor_tensor(res[:, : HALF - P], y4_early, y3[:, 2, : HALF - P], ALU.mult)
+        nc.vector.tensor_tensor(res[:, HALF - P :], row_bank, y3[:, 2, HALF - P : HALF], ALU.mult)
         store(res.unsqueeze(1), slice(2, 3), 0)
         upper(hi2, y3[:, :, HALF : HALF + CHUNK])
-        y4_late, late_bank = lower_last_row((lo2,))
+        y4_late, late_bank = lower_last_row((lo2,), CHUNK)
         hi3 = envelope("hi", ALU.max, a1, b3, (6,))
         lo3_bf = envelope("lo", ALU.min, a1, b3, (6,))
         hi4 = envelope("hi", ALU.max, a1, b4, (7,))

@@ -24,6 +24,7 @@ HALF = 512
 CHUNK = 256
 NT = N // P
 A1_EARLY = 8
+CUTS = (32, 112)
 LIST_ROWS = 16
 
 
@@ -49,12 +50,17 @@ def tile_list_calving_retreat_features_kernel(
         w3_w = keep.tile([P, G, N], I32, name="w3_w", align_bytes=64)
         w3_s = keep.tile([P, G * N], U8, name="w3_s", align_bytes=64)
         x_plane = [keep.tile([P, T], F32, name=f"x_plane{t}") for t in range(PACK)]
-        change = keep.tile([P, PACK * HALF + HALF + CHUNK], F32, name="change", align_bytes=64)
-        change01 = change[:, HALF + CHUNK :].rearrange("p (t c) -> p t c", t=PACK)
-        change23 = change[:, : PACK * HALF].rearrange("p (t c) -> p t c", t=PACK)
-        w2_raw = [keep.tile([P, PACK, PASS], F32, name=f"w2_raw{g}")[:] for g in range(G)]
+        change = keep.tile([P, 2 * PACK * HALF], F32, name="change", align_bytes=64)
+        change01 = change[:, 2 * HALF : (2 + PACK) * HALF].rearrange("p (t c) -> p t c", t=PACK)
+        change23 = change[:, PACK * HALF :].rearrange("p (t c) -> p t c", t=PACK)
+        w2_raw = [
+            keep.tile([P, PACK, PASS], F32, name="w2_raw0")[:],
+            change[:, : PACK * PASS].rearrange("p (j c) -> p j c", j=PACK),
+        ]
+        w4_stage = keep.tile([P, 2 * PACK * N], F32, name="w4_stage", align_bytes=64)
+        w4_bf = w4_stage[:, : PACK * N].bitcast(BF16)
         w4_raw = [
-            keep.tile([P, PACK, N], F32, name="w4_raw0", align_bytes=64)[:],
+            w4_stage[:, PACK * N :].rearrange("p (t n) -> p t n", t=PACK),
             keep.tile([P, PACK, N], F32, name="w4_raw1")[:],
         ]
         w2_s = keep.tile([P, H], U8, name="w2_s", align_bytes=64)
@@ -88,14 +94,14 @@ def tile_list_calving_retreat_features_kernel(
         for q in range(4):
             load_scale_rows(w1s_raw[:].bitcast(I32), w1_scales[0].bitcast(I32), q)
         nc.sync.dma_start(out=bias[:], in_=b1.rearrange("(g p t) -> p g t", g=G, t=PACK))
-        load_x(0)
+        load_x(3)
         nc.sync.dma_start(idx2[:], offs2)
         load_w2(0, 0, PASS // 2)
-        load_x(1)
-        load_w2(0, PASS // 2, PASS)
         load_x(2)
+        load_w2(0, PASS // 2, PASS)
+        load_x(1)
         load_w2(1, 0, PASS // 2)
-        load_x(3)
+        load_x(0)
         load_w2(1, PASS // 2, PASS)
         for g in range(G):
             load_w4(g)
@@ -144,7 +150,7 @@ def tile_list_calving_retreat_features_kernel(
             )
 
         def pool_copy(out, in_):
-            order = "p m j t -> p t m j"
+            order = "p m j t -> p m t j"
             nc.gpsimd.tensor_scalar(out.rearrange(order), in_.rearrange(order), 1.0, 0.0, ALU.mult, ALU.add)
 
         def gather_before(before, t, start):
@@ -286,7 +292,7 @@ def tile_list_calving_retreat_features_kernel(
                 out=w1_s[:, cols].rearrange("p (t m) -> p t m", t=PACK),
                 in_=w1s_raw[:, cols].rearrange("p (m t) -> p t m", t=PACK),
             )
-        w2_bf = keep.tile([P, PACK * H + H - CHUNK], BF16, name="w2_bf", align_bytes=64)
+        w2_bf = keep.tile([P, PACK * H], BF16, name="w2_bf", align_bytes=64)
         a0 = keep.tile([P, 2, HALF // P, G, P, 2], BF16, name="a0")
         a1 = keep.tile([P, 2, HALF // P, G, P, 2], BF16, name="a1")
         make_a((v_w0, v_s[:, :HALF]), a0, range(8))
@@ -294,55 +300,66 @@ def tile_list_calving_retreat_features_kernel(
         gather_words(v_w1, 1)
         v1 = (v_w1, v_s[:, HALF:])
         make_a(v1, a1, range(A1_EARLY))
-        before_late = {}
-        w4_bf = keep.tile([P, G * N * PACK], BF16, name="w4_bf", align_bytes=64)
-        early = keep.tile([P, HALF], F32, name="early")[:]
-        late = w2_bf[:, H : 2 * H].bitcast(F32)
-        low, high = slice(0, P // 2), slice(P // 2, P)
-        round_w2(pool_copy, w2_bf, 0, slice(0, 2), low)
-        gather_before(early, 0, 0)
-        gather_before(late, 0, HALF)
-        gather_change(change01, early, 0, 0)
-        gather_change(change23, late, 0, HALF)
-        round_w2(pool_copy, w2_bf, 0, slice(2, PACK), slice(0, P))
-        for t, start, columns in ((1, 2 * H, low), (2, PACK * H - CHUNK, high), (3, None, None)):
-            if columns:
-                early = w2_bf[:, start : start + H].bitcast(F32)
-            else:
-                early = keep.tile([P, HALF], F32, name="early")[:]
+        planes = slice(0, PACK)
+
+        def before_at(word):
+            return w2_bf[:, PACK * word : PACK * word + S].bitcast(F32)
+
+        round_w2(pool_copy, w2_bf, 0, planes, slice(0, CUTS[0]))
+        for t, word in ((3, PASS - P + CUTS[0]), (2, H - CHUNK)):
+            early = keep.tile([P, HALF], F32, name=f"early{t}")[:]
+            late = before_at(word)
             gather_before(early, t, 0)
-            if t < PACK - 1:
-                before_late[t] = keep.tile([P, HALF], F32, name=f"before_late{t}")[:]
-            else:
-                before_late[t] = w4_bf[:, N * PACK : N * PACK + 2 * HALF].bitcast(F32)
-            gather_before(before_late[t], t, HALF)
+            gather_before(late, t, HALF)
             gather_change(change01, early, t, 0)
-            if columns:
-                round_w2(pool_copy, w2_bf, 1, slice(0, PACK), columns)
-        round_w2(nc.scalar.copy, w2_bf, 0, slice(0, 2), high)
+            gather_change(change23, late, t, HALF)
+            if t == 3:
+                round_w2(pool_copy, w2_bf, 0, planes, slice(CUTS[0], CUTS[1]))
+        round_w2(pool_copy, w2_bf, 1, planes, slice(0, P // 2))
+        round_w2(pool_copy, w2_bf, 1, planes, slice(P // 2, P))
+        before1 = keep.tile([P, S], F32, name="before1")[:]
+        gather_before(before1, 1, 0)
+        early = keep.tile([P, HALF], F32, name="early0")[:]
+        gather_before(early, 0, 0)
+        gather_change(change01, before1[:, :HALF], 1, 0)
+        gather_change(change01, early, 0, 0)
+        round_w2(nc.scalar.copy, w2_bf, 0, planes, slice(CUTS[1], P))
         round_w4(w4_bf, 0, 0, N)
-        x_bf = [w4_raw[0].rearrange("p t n -> p (t n)")[:, c * HALF : (c + 1) * HALF].bitcast(BF16) for c in range(2)]
+        x_at = PACK * N - CHUNK
+        x_bf = [w4_stage[:, x_at + c * HALF : x_at + (c + 1) * HALF].bitcast(BF16) for c in range(2)]
         for c in range(2):
             round_x(x_bf[c], change01[:, :, c * CHUNK : (c + 1) * CHUNK])
         w2_w = keep.tile([P, H], U32, name="w2_w", align_bytes=64)
         nc.vector.quantize_mx(out=w2_w[:].bitcast(E4M3), scales=w2_s[:], in_=w2_bf[:, : PACK * H])
         x0 = quantize_x(x_bf[0], "x_w0")
-        gather_change(change23, before_late[1], 1, HALF)
+        late = change[:, 2 * HALF - CHUNK : 2 * HALF + CHUNK]
+        gather_before(late, 0, HALF)
+        nc.gpsimd.tensor_scalar(
+            w4_bf[:, (G * N - P) * PACK :].rearrange("p (c t) -> p c t", t=PACK),
+            w4_raw[1][:, :, N - P :].rearrange("p t c -> p c t"),
+            1.0,
+            0.0,
+            ALU.mult,
+            ALU.add,
+        )
         x1 = quantize_x(x_bf[1], "x_w1")
-        for t in (2, 3):
-            gather_change(change23, before_late[t], t, HALF)
+        gather_change(change23, before1[:, HALF:], 1, HALF)
+        gather_change(change23, late, 0, HALF)
         b0 = make_b(x0, (0, 1))
-        x_late = keep.tile([P, 2, CHUNK * PACK], BF16, name="x_late", align_bytes=64)
-        round_x(x_late[:, 0, :], change23[:, :, :CHUNK])
+        x_late = [
+            w4_bf[:, N * PACK : (N + CHUNK) * PACK],
+            keep.tile([P, CHUNK * PACK], BF16, name="x_late", align_bytes=64)[:],
+        ]
+        round_x(x_late[0], change23[:, :, :CHUNK])
         b1_ = make_b(x1, (2, 3))
-        round_w4(w4_bf, 1, 0, N)
-        x2 = quantize_x(x_late[:, 0, :], "x_w2")
+        x2 = quantize_x(x_late[0], "x_w2")
+        round_w4(w4_bf, 1, 0, N - P)
         hi0, lo0 = envelopes(a0, b0, (0, 1))
         b2 = make_b(x2, (4, 5))
         y3 = keep.tile([P, NT, S], F32, name="y3")
         upper(hi0, y3[:, :, :CHUNK])
-        round_x(x_late[:, 1, :], change23[:, :, CHUNK:])
-        x3 = quantize_x(x_late[:, 1, :], "x_w3")
+        round_x(x_late[1], change23[:, :, CHUNK:])
+        x3 = quantize_x(x_late[1], "x_w3")
         hi1, lo1 = envelopes(a0, b1_, (2, 3))
         w4_w = keep.tile([P, G * N], U32, name="w4_w", align_bytes=64)
         quantize_w4(w4_bf)

@@ -350,15 +350,15 @@ def tile_list_calving_retreat_features_kernel(
             w4_bf[:, N * PACK : (N + CHUNK) * PACK],
             keep.tile([P, CHUNK * PACK], BF16, name="x_late", align_bytes=64)[:],
         ]
-        round_x(x_late[0], change23[:, :, :CHUNK])
         b1_ = make_b(x1, (2, 3))
-        x2 = quantize_x(x_late[0], "x_w2")
-        round_w4(w4_bf, 1, 0, N - P)
+        round_x(x_late[0], change23[:, :, :CHUNK])
+        round_x(x_late[1], change23[:, :, CHUNK:])
         hi0, lo0 = envelopes(a0, b0, (0, 1))
+        x2 = quantize_x(x_late[0], "x_w2")
         b2 = make_b(x2, (4, 5))
+        round_w4(w4_bf, 1, 0, N - P)
         y3 = keep.tile([P, NT, S], F32, name="y3")
         upper(hi0, y3[:, :, :CHUNK])
-        round_x(x_late[1], change23[:, :, CHUNK:])
         x3 = quantize_x(x_late[1], "x_w3")
         hi1, lo1 = envelopes(a0, b1_, (2, 3))
         w4_w = keep.tile([P, G * N], U32, name="w4_w", align_bytes=64)
@@ -382,7 +382,10 @@ def tile_list_calving_retreat_features_kernel(
         nc.vector.tensor_tensor(res[:, HALF - P :], row_bank, y3[:, 2, HALF - P : HALF], ALU.mult)
         store(res.unsqueeze(1), slice(2, 3), 0)
         upper(hi2, y3[:, :, HALF : HALF + CHUNK])
-        y4_late, late_bank = lower_last_row((lo2,), CHUNK)
+        y4_late = ring.tile([P, NT, P], F32, name="y4")
+        bank = psum.tile([P, NT, P], F32, name="y4_bank", tag="ay", bufs=3)
+        project(bank, w4_w, w4_s, lo2, range(NT))
+        nc.scalar.copy(out=y4_late[:], in_=bank[:])
         hi3 = envelope("hi", ALU.max, a1, b3, (6,))
         lo3_bf = envelope("lo", ALU.min, a1, b3, (6,))
         hi4 = envelope("hi", ALU.max, a1, b4, (7,))
@@ -391,17 +394,23 @@ def tile_list_calving_retreat_features_kernel(
         lo4_bf = envelope("lo", ALU.min, a1, b4, (7,))
         lo3 = quantize_envelope("lo", lo3_bf)
         lo4 = quantize_envelope("lo", lo4_bf)
-        cols = slice(HALF, HALF + CHUNK)
-        res = lo3_bf[:].bitcast(F32)[:, :CHUNK]
-        nc.gpsimd.tensor_tensor(res, y4_late, y3[:, 2, cols], ALU.mult)
-        store(res.unsqueeze(1), slice(2, 3), HALF, nc.scalar)
-        res = keep.tile([P, 2, CHUNK], F32, name="res2")
-        nc.vector.tensor_tensor(res[:], lower(lo2, (0, 1), "y4", 2)[:], y3[:, :2, cols], ALU.mult)
-        store(res[:], slice(0, 2), HALF)
-        for n in range(NT):
-            bank = psum.tile([P, 1, CHUNK], F32, name="last", tag="b_bank", bufs=3)
-            project(bank[:, :, :P], w4_w, w4_s, lo3, (n,))
-            project(bank[:, :, P:], w4_w, w4_s, lo4, (n,))
-            res = ring.tile([P, 1, CHUNK], F32, name="res", bufs=3)
-            nc.vector.tensor_tensor(res[:], bank[:], y3[:, n : n + 1, S - CHUNK :], ALU.mult)
-            store(res[:], slice(n, n + 1), S - CHUNK)
+        res = lo3_bf[:].bitcast(F32)[:, : NT * P].rearrange("p (n j) -> p n j", n=NT)
+        nc.gpsimd.tensor_tensor(res, y4_late[:], y3[:, :, HALF : HALF + P], ALU.mult)
+        store(res, slice(0, NT), HALF, nc.scalar)
+        bank = psum.tile([P, NT, P], F32, name="y4_bank", tag="y4", bufs=2)
+        project(bank, w4_w, w4_s, (lo2[0][:, G * P :], lo2[1][:, G * P :]), range(NT))
+        res = keep.tile([P, NT, P], F32, name="res2")
+        nc.vector.tensor_tensor(res[:], bank[:], y3[:, :, HALF + P : HALF + CHUNK], ALU.mult)
+        store(res[:], slice(0, NT), HALF + P)
+        for lo, start, rows, tag, bufs in (
+            (lo3, S - CHUNK, range(NT), "y4", 2),
+            (lo4, S - P, range(0, 1), "b_bank", 3),
+            (lo4, S - P, range(1, 2), "b_bank", 3),
+            (lo4, S - P, range(2, 3), "b_bank", 3),
+        ):
+            bank = psum.tile([P, len(rows), P], F32, name="last", tag=tag, bufs=bufs)
+            project(bank, w4_w, w4_s, lo, rows)
+            res = ring.tile([P, len(rows), P], F32, name="res", bufs=4)
+            tiles = slice(rows[0], rows[-1] + 1)
+            nc.vector.tensor_tensor(res[:], bank[:], y3[:, tiles, start : start + P], ALU.mult)
+            store(res[:], tiles, start)

@@ -204,6 +204,11 @@ def tile_list_calving_retreat_features_kernel(
             )
             return env
 
+        def plain_envelope(name, op, a_flat, b_bf):
+            env = ring.tile([P, G * P * PACK], BF16, name=f"{name}_bf", align_bytes=64, bufs=3)
+            nc.vector.tensor_tensor(env[:], a_flat, b_bf[:].rearrange("p c g n t -> p (c g n t)"), op)
+            return env
+
         def quantize_envelope(name, env):
             width = env.shape[1] // PACK
             env_w = ring.tile([P, width], U32, name=f"{name}_w", align_bytes=64, bufs=4)
@@ -346,9 +351,10 @@ def tile_list_calving_retreat_features_kernel(
         gather_change(change23, before1[:, HALF:], 1, HALF)
         gather_change(change23, late, 0, HALF)
         b0 = make_b(x0, (0, 1))
+        woven = keep.tile([P, 2 * G * P * PACK], BF16, name="woven", align_bytes=64)
         x_late = [
             w4_bf[:, N * PACK : (N + CHUNK) * PACK],
-            keep.tile([P, CHUNK * PACK], BF16, name="x_late", align_bytes=64)[:],
+            woven[:, : CHUNK * PACK],
         ]
         b1_ = make_b(x1, (2, 3))
         round_x(x_late[0], change23[:, :, :CHUNK])
@@ -360,6 +366,10 @@ def tile_list_calving_retreat_features_kernel(
         y3 = keep.tile([P, NT, S], F32, name="y3")
         upper(hi0, y3[:, :, :CHUNK])
         x3 = quantize_x(x_late[1], "x_w3")
+        nc.scalar.copy(
+            out=woven[:].bitcast(U32).rearrange("p (n u) -> p n u", u=2),
+            in_=a1[:, :, 2:].rearrange("p u c g n e -> p u (c g n e)").bitcast(U32).rearrange("p u n -> p n u"),
+        )
         hi1, lo1 = envelopes(a0, b1_, (2, 3))
         w4_w = keep.tile([P, G * N], U32, name="w4_w", align_bytes=64)
         quantize_w4(w4_bf)
@@ -386,12 +396,12 @@ def tile_list_calving_retreat_features_kernel(
         bank = psum.tile([P, NT, P], F32, name="y4_bank", tag="ay", bufs=3)
         project(bank, w4_w, w4_s, lo2, range(NT))
         nc.scalar.copy(out=y4_late[:], in_=bank[:])
-        hi3 = envelope("hi", ALU.max, a1, b3, (6,))
-        lo3_bf = envelope("lo", ALU.min, a1, b3, (6,))
-        hi4 = envelope("hi", ALU.max, a1, b4, (7,))
+        hi3 = plain_envelope("hi", ALU.max, woven[:, : G * P * PACK], b3)
+        lo3_bf = plain_envelope("lo", ALU.min, woven[:, : G * P * PACK], b3)
+        hi4 = plain_envelope("hi", ALU.max, woven[:, G * P * PACK :], b4)
         upper(quantize_envelope("hi", hi3), y3[:, :, S - CHUNK : S - P])
         upper(quantize_envelope("hi", hi4), y3[:, :, S - P :])
-        lo4_bf = envelope("lo", ALU.min, a1, b4, (7,))
+        lo4_bf = plain_envelope("lo", ALU.min, woven[:, G * P * PACK :], b4)
         lo3 = quantize_envelope("lo", lo3_bf)
         lo4 = quantize_envelope("lo", lo4_bf)
         res = lo3_bf[:].bitcast(F32)[:, : NT * P].rearrange("p (n j) -> p n j", n=NT)

@@ -1,6 +1,7 @@
 from contextlib import ExitStack
 
 import concourse.mybir as mybir
+from concourse.masks import make_identity
 
 K, H, N, T, S = 512, 1024, 384, 2048, 1024
 FLOPS = 2 * K * H * S * 2 + 2 * H * N * S * 2
@@ -20,10 +21,10 @@ P = 128
 PACK = 4
 PASS = P * PACK
 G = H // PASS
+BLOCKS = H // P
 HALF = 512
 CHUNK = 256
 NT = N // P
-A1_EARLY = 8
 CUTS = (32, 112)
 LIST_ROWS = 16
 
@@ -35,18 +36,20 @@ def tile_list_calving_retreat_features_kernel(
     with ExitStack() as ctx:
         keep = ctx.enter_context(tc.tile_pool(name="keep", bufs=1))
         ring = ctx.enter_context(tc.tile_pool(name="ring", bufs=2))
-        psum = ctx.enter_context(tc.psum_pool(name="psum", bufs=2))
+        psum = ctx.enter_context(tc.psum_pool(name="psum", bufs=1))
+        banks = [psum.tile([P, HALF], F32, name=f"bank{i}") for i in range(8)]
 
         idx = keep.tile([P, S // LIST_ROWS], U16, name="idx")
         idx2 = keep.tile([P, S // LIST_ROWS], U16, name="idx2")
         idx3 = keep.tile([P, S // LIST_ROWS], U16, name="idx3")
         tab_w = keep.tile([P, T], I32, name="tab_w", align_bytes=64)
         tab_s = keep.tile([P, T], U8, name="tab_s", align_bytes=64)
-        w1_raw = keep.tile([P, 2 * H], U8, name="w1_raw", align_bytes=64)
-        w1s_raw = keep.tile([P, H], U8, name="w1s_raw", align_bytes=64)
         w1_w = keep.tile([P, 2 * H], U8, name="w1_w", align_bytes=64)
         w1_s = keep.tile([P, H], U8, name="w1_s", align_bytes=64)
-        bias = keep.tile([P, G, PACK], F32, name="bias")
+        bias_rows = keep.tile([P, P], F32, name="bias_rows")
+        bias = keep.tile([P, BLOCKS], F32, name="bias")
+        ident_f32 = keep.tile([P, P], F32, name="ident_f32")
+        ident_bf = keep.tile([P, P], BF16, name="ident_bf")
         w3_w = keep.tile([P, G, N], I32, name="w3_w", align_bytes=64)
         w3_s = keep.tile([P, G * N], U8, name="w3_s", align_bytes=64)
         x_plane = [keep.tile([P, T], F32, name=f"x_plane{t}") for t in range(PACK)]
@@ -57,10 +60,9 @@ def tile_list_calving_retreat_features_kernel(
             keep.tile([P, PACK, PASS], F32, name="w2_raw0")[:],
             change[:, : PACK * PASS].rearrange("p (j c) -> p j c", j=PACK),
         ]
-        w4_stage = keep.tile([P, 2 * PACK * N], F32, name="w4_stage", align_bytes=64)
-        w4_bf = w4_stage[:, : PACK * N].bitcast(BF16)
+        w4_stage = keep.tile([P, PACK * N], F32, name="w4_stage", align_bytes=64)
         w4_raw = [
-            w4_stage[:, PACK * N :].rearrange("p (t n) -> p t n", t=PACK),
+            w4_stage[:].rearrange("p (t n) -> p t n", t=PACK),
             keep.tile([P, PACK, N], F32, name="w4_raw1")[:],
         ]
         w2_s = keep.tile([P, H], U8, name="w2_s", align_bytes=64)
@@ -72,7 +74,7 @@ def tile_list_calving_retreat_features_kernel(
         def load_x(t):
             nc.sync.dma_start(out=x_plane[t][:], in_=x_rows[:, t, :])
 
-        def load_w2(g, first=0, last=PASS):
+        def load_w2(g, first, last):
             nc.sync.dma_start(out=w2_raw[g][:, :, first:last], in_=w2_rows[:, :, g * PASS + first : g * PASS + last])
 
         def load_w4(g):
@@ -84,16 +86,19 @@ def tile_list_calving_retreat_features_kernel(
         w2_rows = w2.rearrange("(p t) r -> p t r", t=PACK)
 
         nc.gpsimd.memset(tab_s[:].bitcast(I32), 0)
-        nc.vector.memset(w1s_raw[:].bitcast(I32), 0)
+        nc.vector.memset(bias_rows[:], 0.0)
+        nc.vector.memset(w1_s[:].bitcast(I32), 0)
+        make_identity(nc, ident_f32[:])
+        make_identity(nc, ident_bf[:])
         nc.sync.dma_start(idx[:], offs)
-        nc.sync.dma_start(out=w1_raw[:].bitcast(I32), in_=w1_words[0].bitcast(I32))
+        nc.sync.dma_start(out=w1_w[:].bitcast(I32), in_=w1_words[0].bitcast(I32))
+        nc.sync.dma_start(out=bias_rows[:BLOCKS, :], in_=b1.rearrange("(j q) -> j q", q=P))
         for q in range(4):
             load_scale_rows(tab_s[:].bitcast(I32), tab_scales[0].bitcast(I32), q, (nc.sync, nc.scalar)[q % 2])
-        nc.sync.dma_start(idx3[:], offs3)
         nc.sync.dma_start(out=tab_w[:], in_=tab_words[0].rearrange("p c i -> p (c i)").bitcast(I32))
+        nc.sync.dma_start(idx3[:], offs3)
         for q in range(4):
-            load_scale_rows(w1s_raw[:].bitcast(I32), w1_scales[0].bitcast(I32), q)
-        nc.sync.dma_start(out=bias[:], in_=b1.rearrange("(g p t) -> p g t", g=G, t=PACK))
+            load_scale_rows(w1_s[:].bitcast(I32), w1_scales[0].bitcast(I32), q)
         load_x(3)
         nc.sync.dma_start(idx2[:], offs2)
         load_w2(0, 0, PASS // 2)
@@ -117,41 +122,49 @@ def tile_list_calving_retreat_features_kernel(
         def offsets(tile, start, count):
             return tile[:, start // LIST_ROWS : (start + count) // LIST_ROWS]
 
-        def gather_words(v_w, h):
-            nc.vector.tensor_copy(v_w[:], tab_w[:].bitcast(U32).indirect(offsets(idx, h * HALF, HALF)))
+        def make_a(h, j):
+            bank = banks[(h * BLOCKS + j) % 3]
+            nc.tensor.matmul_mx(
+                out=bank[:],
+                lhsT=w1_w[:, 2 * j * P : 2 * (j + 1) * P].bitcast(E2M1),
+                lhsT_scale=w1_s[:, j * P : (j + 1) * P],
+                rhs=v_w[h][:].bitcast(E4M3),
+                rhs_scale=v_s[:, h * HALF : (h + 1) * HALF],
+                start=True,
+                stop=True,
+            )
+            nc.scalar.activation(out=a_rows[h][:, j, :], in_=bank[:], func=IDENTITY, bias=bias[:, j : j + 1])
 
-        def make_a(v, a_bf, pieces, start=0, width=HALF):
-            v_w, v_s = v
-            for piece in pieces:
-                for g, t in (divmod(piece, PACK),):
-                    col = g * PASS + t * P
-                    bank = psum.tile([P, width], F32, name="a_bank", tag="ay", bufs=3)
-                    nc.tensor.matmul_mx(
-                        out=bank[:],
-                        lhsT=w1_w[:, 2 * col : 2 * (col + P)].bitcast(E2M1),
-                        lhsT_scale=w1_s[:, col : col + P],
-                        rhs=v_w[:, start : start + width].bitcast(E4M3),
-                        rhs_scale=v_s[:, start : start + width],
-                        start=True,
-                        stop=True,
-                    )
-                    nc.scalar.activation(
-                        out=a_bf[:, t // 2, start // P : (start + width) // P, g, :, t % 2],
-                        in_=bank[:].rearrange("p (c n) -> p c n", n=P),
-                        func=IDENTITY,
-                        bias=bias[:, g, t : t + 1],
-                    )
+        def turn_a(s, bank):
+            h, i = divmod(s, HALF // P)
+            values = bank[:].bitcast(BF16)
+            for j in range(BLOCKS):
+                nc.tensor.transpose(values[:, j * P : (j + 1) * P], a_rows[h][:, j, i * P : (i + 1) * P], ident_bf[:])
+            nc.scalar.copy(
+                out=a_turned[s][:].rearrange("n (u m) -> n u m", u=2),
+                in_=bank[:].rearrange("n (m u) -> n u m", u=2),
+            )
 
-        def round_w2(copy, staged, g, planes, columns):
+        def weave_a(s):
+            bank = banks[6 + s % 2]
+            for i in range(2 * G):
+                cols = slice(i * P, (i + 1) * P)
+                nc.tensor.transpose(bank[:, cols], a_turned[s][:, cols], ident_f32[:])
+            return bank[:].bitcast(BF16).rearrange("p (u g n e) -> p g n u e", u=2, g=G, e=2)
+
+        def round_w2(copy, staged, g, columns):
             half = staged[:, g * PACK * PASS : (g + 1) * PACK * PASS]
             copy(
-                out=half.rearrange("p (t m j) -> p m j t", t=PACK, j=PACK)[:, columns, :, planes],
-                in_=w2_raw[g].rearrange("p j (m t) -> p m j t", t=PACK)[:, columns, :, planes],
+                out=half.rearrange("p (t m j) -> p m j t", t=PACK, j=PACK)[:, columns],
+                in_=w2_raw[g].rearrange("p j (m t) -> p m j t", t=PACK)[:, columns],
             )
+
+        def pool_round(out, in_):
+            nc.gpsimd.tensor_scalar(out, in_, 1.0, 0.0, ALU.mult, ALU.add)
 
         def pool_copy(out, in_):
             order = "p m j t -> p m t j"
-            nc.gpsimd.tensor_scalar(out.rearrange(order), in_.rearrange(order), 1.0, 0.0, ALU.mult, ALU.add)
+            pool_round(out.rearrange(order), in_.rearrange(order))
 
         def gather_before(before, t, start):
             nc.vector.tensor_copy(before, x_plane[t][:].indirect(offsets(idx3, start, before.shape[1])))
@@ -160,267 +173,238 @@ def tile_list_calving_retreat_features_kernel(
             picked = x_plane[t][:].indirect(offsets(idx2, start, HALF))
             nc.vector.tensor_tensor(change[:, t, :], picked, before, ALU.subtract)
 
-        def round_x(x_bf, change):
+        def round_rows(rounded, rows):
             nc.scalar.copy(
-                out=x_bf.rearrange("p (c i t) -> p c t i", i=4, t=PACK),
-                in_=change.rearrange("p t (c i) -> p c t i", i=4),
+                out=rounded.rearrange("p (c i t) -> p c t i", i=4, t=PACK),
+                in_=rows.rearrange("p t (c i) -> p c t i", i=4),
             )
 
+        def pool_round_rows(rounded, rows):
+            pool_round(rounded.rearrange("p (c t) -> p c t", t=PACK), rows.rearrange("p t c -> p c t"))
+
         def quantize_x(x_bf, tag):
-            width = x_bf.shape[1] // PACK
-            x_w = keep.tile([P, width], U32, name="x_w", tag=tag, align_bytes=64)
-            x_s = ring.tile([P, width], U8, name="x_s", align_bytes=64, bufs=4)
+            x_w = keep.tile([P, CHUNK], U32, name="x_w", tag=f"x_w{tag}", align_bytes=64)
+            x_s = keep.tile([P, CHUNK], U8, name="x_s", tag=f"x_s{tag}", align_bytes=64)
             nc.vector.quantize_mx(out=x_w[:].bitcast(E4M3), scales=x_s[:], in_=x_bf)
             return x_w, x_s
 
-        def make_b(x, subs):
+        def make_b(x, i, bank_pair, tag="b_bf", bufs=4):
             x_w, x_s = x
-            b_bf = ring.tile([P, len(subs), G, P, PACK], BF16, name="b_bf", bufs=5)
-            for i, sub in enumerate(subs):
-                tokens = slice(sub % 2 * P, (sub % 2 + 1) * P)
-                for g in range(G):
-                    bank = psum.tile([P, PACK, P], F32, name="b_bank", tag="b_bank", bufs=3)
-                    for t in range(PACK):
-                        nc.tensor.matmul_mx(
-                            out=bank[:, t, :],
-                            lhsT=w2_w[:, g * PASS + t * P : g * PASS + (t + 1) * P].bitcast(E4M3),
-                            lhsT_scale=w2_s[:, g * PASS + t * P : g * PASS + (t + 1) * P],
-                            rhs=x_w[:, tokens].bitcast(E4M3),
-                            rhs_scale=x_s[:, tokens],
-                            start=True,
-                            stop=True,
-                        )
-                    nc.scalar.copy(out=b_bf[:, i, g], in_=bank[:].rearrange("p t n -> p n t"))
+            tokens = slice(i * P, (i + 1) * P)
+            b_bf = ring.tile([P, G, P, PACK], BF16, name="b_bf", tag=tag, bufs=bufs, align_bytes=64)
+            for g in range(G):
+                bank = banks[bank_pair[g]][:].rearrange("p (t n) -> p t n", t=PACK)
+                for t in range(PACK):
+                    cols = slice(g * PASS + t * P, g * PASS + (t + 1) * P)
+                    nc.tensor.matmul_mx(
+                        out=bank[:, t, :],
+                        lhsT=w2_w[:, cols].bitcast(E4M3),
+                        lhsT_scale=w2_s[:, cols],
+                        rhs=x_w[:, tokens].bitcast(E4M3),
+                        rhs_scale=x_s[:, tokens],
+                        start=True,
+                        stop=True,
+                    )
+                nc.scalar.copy(out=b_bf[:, g], in_=bank.rearrange("p t n -> p n t"))
             return b_bf
 
-        def envelope(name, op, a_bf, b_bf, subs):
-            env = ring.tile([P, len(subs) * G * P * PACK], BF16, name=f"{name}_bf", align_bytes=64, bufs=3)
-            first = subs[0] % PACK
+        def envelope_tile(name, width):
+            return ring.tile([P, G, width, PACK], BF16, name=f"{name}_bf", tag=f"{name}{width}", align_bytes=64)[:]
+
+        def envelope(env, i, op, a_woven, b_bf):
             nc.vector.tensor_tensor(
-                env[:].rearrange("p (n u e) -> p n u e", u=2, e=2),
-                a_bf[:, :, first : first + len(subs)].rearrange("p u c g n e -> p (c g n) u e"),
-                b_bf[:].rearrange("p c g n (u e) -> p (c g n) u e", u=2),
+                env[:, :, i * P : (i + 1) * P, :].rearrange("p g n (u e) -> p g n u e", u=2),
+                a_woven,
+                b_bf[:].rearrange("p g n (u e) -> p g n u e", u=2),
                 op,
             )
-            return env
-
-        def plain_envelope(name, op, a_flat, b_bf):
-            env = ring.tile([P, G * P * PACK], BF16, name=f"{name}_bf", align_bytes=64, bufs=3)
-            nc.vector.tensor_tensor(env[:], a_flat, b_bf[:].rearrange("p c g n t -> p (c g n t)"), op)
-            return env
 
         def quantize_envelope(name, env):
-            width = env.shape[1] // PACK
-            env_w = ring.tile([P, width], U32, name=f"{name}_w", align_bytes=64, bufs=4)
-            env_s = ring.tile([P, width], U8, name=f"{name}_s", align_bytes=64, bufs=4)
-            nc.vector.quantize_mx(out=env_w[:].bitcast(E4M3), scales=env_s[:], in_=env[:])
+            width = G * env.shape[2]
+            env_w = ring.tile([P, width], U32, name=f"{name}_w", align_bytes=64, bufs=3)
+            env_s = ring.tile([P, width], U8, name=f"{name}_s", align_bytes=64, bufs=3)
+            nc.vector.quantize_mx(
+                out=env_w[:].bitcast(E4M3), scales=env_s[:], in_=env.rearrange("p g n t -> p (g n t)")
+            )
             return env_w, env_s
 
-        def envelopes(a_bf, b_bf, subs):
-            hi = envelope("hi", ALU.max, a_bf, b_bf, subs)
-            lo = envelope("lo", ALU.min, a_bf, b_bf, subs)
-            return quantize_envelope("hi", hi), quantize_envelope("lo", lo)
+        def envelopes(c, lo):
+            hi = envelope_tile("hi", CHUNK)
+            for i in range(2):
+                a_woven = weave_a(2 * c + i)
+                envelope(hi, i, ALU.max, a_woven, b[2 * c + i])
+                envelope(lo, i, ALU.min, a_woven, b[2 * c + i])
+            return hi, lo
 
-        def round_w4(staged, g, first, last):
-            nc.scalar.copy(
-                out=staged[:, (g * N + first) * PACK : (g * N + last) * PACK].rearrange("p (c i t) -> p c t i", i=4, t=PACK),
-                in_=w4_raw[g][:, :, first:last].rearrange("p t (c i) -> p c t i", i=4),
-            )
-
-        def quantize_w4(staged):
-            for first, last in ((0, 256), (256, G * N)):
-                nc.vector.quantize_mx(
-                    out=w4_w[:, first:last].bitcast(E4M3),
-                    scales=w4_s[:, first:last],
-                    in_=staged[:, first * PACK : last * PACK],
-                )
-
-        def project(bank, weight, weight_s, env, rows):
+        def project(target, weight, weight_s, env, row, first=0):
             env_w, env_s = env
-            for i, n in enumerate(rows):
-                for j in range(0, bank.shape[2], P):
-                    for g in range(G):
-                        cols = slice(g * N + n * P, g * N + (n + 1) * P)
-                        tokens = slice(j * G + g * P, j * G + (g + 1) * P)
-                        nc.tensor.matmul_mx(
-                            out=bank[:, i, j : j + P],
-                            lhsT=weight[:, cols].bitcast(E4M3),
-                            lhsT_scale=weight_s[:, cols],
-                            rhs=env_w[:, tokens].bitcast(E4M3),
-                            rhs_scale=env_s[:, tokens],
-                            start=(g == 0),
-                            stop=(g == G - 1),
-                        )
+            width = env_w.shape[1] // G
+            for g in range(G):
+                cols = slice(g * N + row * P, g * N + (row + 1) * P)
+                tokens = slice(g * width + first, g * width + first + target.shape[1])
+                nc.tensor.matmul_mx(
+                    out=target,
+                    lhsT=weight[:, cols].bitcast(E4M3),
+                    lhsT_scale=weight_s[:, cols],
+                    rhs=env_w[:, tokens].bitcast(E4M3),
+                    rhs_scale=env_s[:, tokens],
+                    start=(g == 0),
+                    stop=(g == G - 1),
+                )
 
         w3_flat = w3_w[:].rearrange("p g n -> p (g n)")
         out_rows = out.rearrange("(n p) j -> p n j", p=P)
 
-        def row_groups(width):
-            per_bank = HALF // width
-            return [range(n, min(n + per_bank, NT)) for n in range(0, NT, per_bank)]
+        def rows_of(bank, count, width):
+            return banks[bank][:, : count * width].rearrange("p (n j) -> p n j", n=count)
 
-        def upper(hi, y3):
-            width = y3.shape[2]
-            for rows in row_groups(width):
-                bank = psum.tile([P, len(rows), width], F32, name="y3_bank", tag="ay", bufs=3)
-                project(bank, w3_flat, w3_s, hi, rows)
-                nc.scalar.copy(out=y3[:, rows[0] : rows[-1] + 1, :], in_=bank[:])
+        def projections(hi, lo, bank_ids, pool_rows):
+            y = ring.tile([P, 2, NT, CHUNK], F32, name="y", bufs=3)
+            upper, mixed, lower = [rows_of(bank, 2, CHUNK) for bank in bank_ids]
+            for row in range(2):
+                project(upper[:, row, :], w3_flat, w3_s, hi, row)
+            nc.scalar.copy(out=y[:, 0, :2, :], in_=upper)
+            project(mixed[:, 0, :], w3_flat, w3_s, hi, 2)
+            project(mixed[:, 1, :], w4_w, w4_s, lo, 2)
+            kept = pool_rows - 1
+            nc.scalar.copy(out=y[:, :kept, 2, :], in_=mixed[:, :kept, :])
+            for row in range(2):
+                project(lower[:, row, :], w4_w, w4_s, lo, row)
+            nc.scalar.copy(out=y[:, 1, :2, :], in_=lower)
+            return y, mixed[:, 1, :]
 
-        def lower(lo, rows, tag, bufs):
-            bank = psum.tile([P, len(rows), CHUNK], F32, name="y4_bank", tag=tag, bufs=bufs)
-            project(bank, w4_w, w4_s, lo, rows)
-            return bank
+        def pool_product(env, y, rows, start, queue=nc.sync):
+            res = as_result(env)[:, : rows * CHUNK].rearrange("p (n j) -> p n j", n=rows)
+            nc.gpsimd.tensor_tensor(res, y[:, 0, :rows, :], y[:, 1, :rows, :], ALU.mult)
+            store(res, slice(0, rows), start, queue)
 
-        def lower_last_row(los, copied):
-            y4 = ring.tile([P, copied], F32, name="y4")
-            bank = psum.tile([P, len(los), CHUNK], F32, name="y4_row", tag="ay", bufs=3)
-            for i, lo in enumerate(los):
-                project(bank[:, i : i + 1, :], w4_w, w4_s, lo, (NT - 1,))
-            row = bank[:].rearrange("p c j -> p (c j)")
-            nc.scalar.copy(out=y4[:], in_=row[:, :copied])
-            return y4[:], row[:, copied:]
+        def last_row_product(y, sums, start):
+            res = ring.tile([P, 1, CHUNK], F32, name="res_row")
+            nc.vector.tensor_tensor(res[:, 0, :], sums, y[:, 0, 2, :], ALU.mult)
+            store(res[:], slice(2, 3), start)
+
+        def as_result(env):
+            return env.rearrange("p g n t -> p (g n t)").bitcast(F32)
 
         def store(res, rows, start, queue=nc.sync):
             queue.dma_start(out=out_rows[:, rows, start : start + res.shape[2]], in_=res)
 
+        nc.tensor.transpose(banks[7][:, :P], bias_rows[:], ident_f32[:])
+        nc.scalar.copy(out=bias[:], in_=banks[7][:, :BLOCKS])
         v_s = keep.tile([P, S], U8, name="v_s", align_bytes=64)
         nc.vector.tensor_copy(v_s[:], tab_s[:].indirect(idx[:]))
-        nc.vector.tensor_copy(
-            out=w1_w[:].bitcast(U16).rearrange("p (g t m) -> p g t m", g=G, t=PACK),
-            in_=w1_raw[:].bitcast(U16).rearrange("p (g m t) -> p g t m", g=G, t=PACK),
-        )
-        v_w0 = keep.tile([P, HALF], U32, name="v_w0", align_bytes=64)
-        gather_words(v_w0, 0)
-        for g in range(G):
-            cols = slice(g * PASS, (g + 1) * PASS)
-            nc.gpsimd.tensor_copy(
-                out=w1_s[:, cols].rearrange("p (t m) -> p t m", t=PACK),
-                in_=w1s_raw[:, cols].rearrange("p (m t) -> p t m", t=PACK),
-            )
+        v_w = [keep.tile([P, HALF], U32, name=f"v_w{h}", align_bytes=64) for h in range(2)]
+        a_rows = [keep.tile([P, BLOCKS, HALF], BF16, name=f"a_rows{h}") for h in range(2)]
+        a_turned = [keep.tile([P, H // 2], F32, name=f"a_turned{s}") for s in range(S // P)]
+        for h in range(2):
+            nc.vector.tensor_copy(v_w[h][:], tab_w[:].bitcast(U32).indirect(offsets(idx, h * HALF, HALF)))
+        for j in range(BLOCKS):
+            make_a(0, j)
+        for j in range(BLOCKS):
+            make_a(1, j)
+            if j % 2:
+                turn_a(j // 2, banks[3 + j // 2])
+        for s, bank in zip(range(4, 8), (7, 3, 4, 5)):
+            turn_a(s, banks[bank])
+
         w2_bf = keep.tile([P, PACK * H], BF16, name="w2_bf", align_bytes=64)
-        a0 = keep.tile([P, 2, HALF // P, G, P, 2], BF16, name="a0")
-        a1 = keep.tile([P, 2, HALF // P, G, P, 2], BF16, name="a1")
-        make_a((v_w0, v_s[:, :HALF]), a0, range(8))
-        v_w1 = keep.tile([P, HALF], U32, name="v_w1", align_bytes=64)
-        gather_words(v_w1, 1)
-        v1 = (v_w1, v_s[:, HALF:])
-        make_a(v1, a1, range(A1_EARLY))
-        planes = slice(0, PACK)
 
         def before_at(word):
             return w2_bf[:, PACK * word : PACK * word + S].bitcast(F32)
 
-        round_w2(pool_copy, w2_bf, 0, planes, slice(0, CUTS[0]))
+        round_w2(pool_copy, w2_bf, 0, slice(0, CUTS[0]))
         for t, word in ((3, PASS - P + CUTS[0]), (2, H - CHUNK)):
-            early = keep.tile([P, HALF], F32, name=f"early{t}")[:]
+            early = ring.tile([P, HALF], F32, name="early")[:]
             late = before_at(word)
             gather_before(early, t, 0)
             gather_before(late, t, HALF)
             gather_change(change01, early, t, 0)
             gather_change(change23, late, t, HALF)
             if t == 3:
-                round_w2(pool_copy, w2_bf, 0, planes, slice(CUTS[0], CUTS[1]))
-        round_w2(pool_copy, w2_bf, 1, planes, slice(0, P // 2))
-        round_w2(pool_copy, w2_bf, 1, planes, slice(P // 2, P))
-        before1 = keep.tile([P, S], F32, name="before1")[:]
+                round_w2(pool_copy, w2_bf, 0, slice(CUTS[0], CUTS[1]))
+        round_w2(pool_copy, w2_bf, 1, slice(0, P // 2))
+        round_w2(pool_copy, w2_bf, 1, slice(P // 2, P))
+        before1 = keep.tile([P, S], F32, name="before1", align_bytes=64)[:]
         gather_before(before1, 1, 0)
-        early = keep.tile([P, HALF], F32, name="early0")[:]
+        early = ring.tile([P, HALF], F32, name="early")[:]
         gather_before(early, 0, 0)
         gather_change(change01, before1[:, :HALF], 1, 0)
         gather_change(change01, early, 0, 0)
-        round_w2(nc.scalar.copy, w2_bf, 0, planes, slice(CUTS[1], P))
-        round_w4(w4_bf, 0, 0, N)
-        x_at = PACK * N - CHUNK
-        x_bf = [w4_stage[:, x_at + c * HALF : x_at + (c + 1) * HALF].bitcast(BF16) for c in range(2)]
+        round_w2(nc.scalar.copy, w2_bf, 0, slice(CUTS[1], P))
+        w4_first = keep.tile([P, N * PACK], BF16, name="w4_first", align_bytes=64)[:]
+        round_rows(w4_first, w4_raw[0])
+        x_bf = [w4_stage[:, c * HALF : (c + 1) * HALF].bitcast(BF16) for c in range(2)]
         for c in range(2):
-            round_x(x_bf[c], change01[:, :, c * CHUNK : (c + 1) * CHUNK])
+            round_rows(x_bf[c], change01[:, :, c * CHUNK : (c + 1) * CHUNK])
         w2_w = keep.tile([P, H], U32, name="w2_w", align_bytes=64)
-        nc.vector.quantize_mx(out=w2_w[:].bitcast(E4M3), scales=w2_s[:], in_=w2_bf[:, : PACK * H])
-        x0 = quantize_x(x_bf[0], "x_w0")
-        late = change[:, 2 * HALF - CHUNK : 2 * HALF + CHUNK]
+        nc.vector.quantize_mx(out=w2_w[:].bitcast(E4M3), scales=w2_s[:], in_=w2_bf[:])
+        late = before1[:, :HALF]
         gather_before(late, 0, HALF)
-        nc.gpsimd.tensor_scalar(
-            w4_bf[:, (G * N - P) * PACK :].rearrange("p (c t) -> p c t", t=PACK),
-            w4_raw[1][:, :, N - P :].rearrange("p t c -> p c t"),
-            1.0,
-            0.0,
-            ALU.mult,
-            ALU.add,
-        )
-        x1 = quantize_x(x_bf[1], "x_w1")
+        w4_tail = w2_bf[:, : P * PACK]
+        pool_round_rows(w4_tail, w4_raw[1][:, :, CHUNK:])
+        x0 = quantize_x(x_bf[0], 0)
+        x1 = quantize_x(x_bf[1], 1)
         gather_change(change23, before1[:, HALF:], 1, HALF)
         gather_change(change23, late, 0, HALF)
-        b0 = make_b(x0, (0, 1))
-        woven = keep.tile([P, 2 * G * P * PACK], BF16, name="woven", align_bytes=64)
-        x_late = [
-            w4_bf[:, N * PACK : (N + CHUNK) * PACK],
-            woven[:, : CHUNK * PACK],
-        ]
-        b1_ = make_b(x1, (2, 3))
-        round_x(x_late[0], change23[:, :, :CHUNK])
-        round_x(x_late[1], change23[:, :, CHUNK:])
-        hi0, lo0 = envelopes(a0, b0, (0, 1))
-        x2 = quantize_x(x_late[0], "x_w2")
-        b2 = make_b(x2, (4, 5))
-        round_w4(w4_bf, 1, 0, N - P)
-        y3 = keep.tile([P, NT, S], F32, name="y3")
-        upper(hi0, y3[:, :, :CHUNK])
-        x3 = quantize_x(x_late[1], "x_w3")
-        nc.scalar.copy(
-            out=woven[:].bitcast(U32).rearrange("p (n u) -> p n u", u=2),
-            in_=a1[:, :, 2:].rearrange("p u c g n e -> p u (c g n e)").bitcast(U32).rearrange("p u n -> p n u"),
-        )
-        hi1, lo1 = envelopes(a0, b1_, (2, 3))
-        w4_w = keep.tile([P, G * N], U32, name="w4_w", align_bytes=64)
-        quantize_w4(w4_bf)
-        upper(hi1, y3[:, :, CHUNK:HALF])
-        y4_early, row_bank = lower_last_row((lo0, lo1), HALF - P)
-        b3 = make_b(x3, (6,))
-        banks = [lower(lo, (0, 1), "y4", 2) for lo in (lo0, lo1)]
-        b4 = make_b(x3, (7,))
-        hi2_bf = envelope("hi", ALU.max, a1, b2, (4, 5))
-        lo2_bf = envelope("lo", ALU.min, a1, b2, (4, 5))
-        hi2 = quantize_envelope("hi", hi2_bf)
-        lo2 = quantize_envelope("lo", lo2_bf)
-        res = b2[:].rearrange("p c g n t -> p (c g n t)").bitcast(F32).rearrange("p (n j) -> p n j", n=2)
-        for c in range(2):
-            cols = slice(c * CHUNK, (c + 1) * CHUNK)
-            nc.vector.tensor_tensor(res[:, :, cols], banks[c][:], y3[:, :2, cols], ALU.mult)
-        store(res, slice(0, 2), 0)
-        res = hi2_bf[:].bitcast(F32)[:, :HALF]
-        nc.gpsimd.tensor_tensor(res[:, : HALF - P], y4_early, y3[:, 2, : HALF - P], ALU.mult)
-        nc.vector.tensor_tensor(res[:, HALF - P :], row_bank, y3[:, 2, HALF - P : HALF], ALU.mult)
-        store(res.unsqueeze(1), slice(2, 3), 0)
-        upper(hi2, y3[:, :, HALF : HALF + CHUNK])
-        y4_late = ring.tile([P, NT, P], F32, name="y4")
-        bank = psum.tile([P, NT, P], F32, name="y4_bank", tag="ay", bufs=3)
-        project(bank, w4_w, w4_s, lo2, range(NT))
-        nc.scalar.copy(out=y4_late[:], in_=bank[:])
-        hi3 = plain_envelope("hi", ALU.max, woven[:, : G * P * PACK], b3)
-        lo3_bf = plain_envelope("lo", ALU.min, woven[:, : G * P * PACK], b3)
-        hi4 = plain_envelope("hi", ALU.max, woven[:, G * P * PACK :], b4)
-        upper(quantize_envelope("hi", hi3), y3[:, :, S - CHUNK : S - P])
-        upper(quantize_envelope("hi", hi4), y3[:, :, S - P :])
-        lo4_bf = plain_envelope("lo", ALU.min, woven[:, G * P * PACK :], b4)
-        lo3 = quantize_envelope("lo", lo3_bf)
-        lo4 = quantize_envelope("lo", lo4_bf)
-        res = lo3_bf[:].bitcast(F32)[:, : NT * P].rearrange("p (n j) -> p n j", n=NT)
-        nc.gpsimd.tensor_tensor(res, y4_late[:], y3[:, :, HALF : HALF + P], ALU.mult)
-        store(res, slice(0, NT), HALF, nc.scalar)
-        bank = psum.tile([P, NT, P], F32, name="y4_bank", tag="y4", bufs=2)
-        project(bank, w4_w, w4_s, (lo2[0][:, G * P :], lo2[1][:, G * P :]), range(NT))
-        res = keep.tile([P, NT, P], F32, name="res2")
-        nc.vector.tensor_tensor(res[:], bank[:], y3[:, :, HALF + P : HALF + CHUNK], ALU.mult)
-        store(res[:], slice(0, NT), HALF + P)
-        for lo, start, rows, tag, bufs in (
-            (lo3, S - CHUNK, range(NT), "y4", 2),
-            (lo4, S - P, range(0, 1), "b_bank", 3),
-            (lo4, S - P, range(1, 2), "b_bank", 3),
-            (lo4, S - P, range(2, 3), "b_bank", 3),
-        ):
-            bank = psum.tile([P, len(rows), P], F32, name="last", tag=tag, bufs=bufs)
-            project(bank, w4_w, w4_s, lo, rows)
+        b = [make_b(x0, 0, (0, 1)), make_b(x0, 1, (2, 3), "b_then_w4", 1), make_b(x1, 0, (4, 5))]
+        stage = keep.tile([P, (G + 1) * CHUNK * PACK], BF16, name="stage", align_bytes=64)
+        first_lo = stage[:, : G * CHUNK * PACK].rearrange("p (g n t) -> p g n t", g=G, t=PACK)
+        x2_bf = stage[:, G * CHUNK * PACK :]
+        x3_bf = stage[:, G * CHUNK * PACK - HALF : G * CHUNK * PACK + HALF]
+        round_rows(x2_bf, change23[:, :, :CHUNK])
+        w4_head = late.bitcast(BF16)
+        pool_round_rows(w4_head, w4_raw[1][:, :, :CHUNK])
+        b.append(make_b(x1, 1, (0, 1)))
+
+        hi_bf, lo_bf = envelopes(0, first_lo)
+        hi0 = quantize_envelope("hi", hi_bf)
+        w4_w = ring.tile([P, G * N], U32, name="w4_w", tag="b_then_w4", bufs=1, align_bytes=64)
+        for staged, first in ((w4_first, 0), (w4_tail, N + CHUNK), (w4_head, N)):
+            cols = slice(first, first + staged.shape[1] // PACK)
+            nc.vector.quantize_mx(out=w4_w[:, cols].bitcast(E4M3), scales=w4_s[:, cols], in_=staged)
+        x2 = quantize_x(x2_bf, 0)
+        lo0 = quantize_envelope("lo", lo_bf)
+        pool_round_rows(x3_bf, change23[:, :, CHUNK:])
+        b.extend([make_b(x2, 0, (2, 3)), make_b(x2, 1, (4, 5))])
+        y0 = projections(hi0, lo0, (0, 1, 2), NT)[0]
+
+        hi_bf, lo_bf = envelopes(1, envelope_tile("lo", CHUNK))
+        x3 = quantize_x(x3_bf, 1)
+        hi1, lo1 = quantize_envelope("hi", hi_bf), quantize_envelope("lo", lo_bf)
+        pool_product(lo_bf, y0, NT, 0)
+        b.append(make_b(x3, 0, (3, 4)))
+        y1, row1 = projections(hi1, lo1, (5, 0, 1), 2)
+        b.append(make_b(x3, 1, (5, 2)))
+
+        hi_bf, lo_bf = envelopes(2, envelope_tile("lo", CHUNK))
+        hi2, lo2 = quantize_envelope("hi", hi_bf), quantize_envelope("lo", lo_bf)
+        pool_product(lo_bf, y1, 2, CHUNK)
+        y2, row2 = projections(hi2, lo2, (3, 4, 1), 2)
+
+        hi_bf = envelope_tile("hi", CHUNK)
+        lo_bf = [envelope_tile("lo", P) for i in range(2)]
+        a_woven = [weave_a(6 + i) for i in range(2)]
+        last_row_product(y1, row1, CHUNK)
+        for i in range(2):
+            envelope(hi_bf, i, ALU.max, a_woven[i], b[6 + i])
+        envelope(lo_bf[0], 0, ALU.min, a_woven[0], b[6])
+        hi3 = quantize_envelope("hi", hi_bf)
+        envelope(lo_bf[1], 0, ALU.min, a_woven[1], b[7])
+        y3 = []
+        for i, bank in enumerate((5, 2)):
+            sums = rows_of(bank, NT, P)
+            for row in range(NT):
+                project(sums[:, row, :], w3_flat, w3_s, hi3, row, i * P)
+            y3.append(ring.tile([P, NT, P], F32, name="y3"))
+            nc.scalar.copy(out=y3[i][:], in_=sums)
+        lo3 = [quantize_envelope("lo", env) for env in lo_bf]
+        pool_product(lo_bf[1], y2, 2, HALF, nc.scalar)
+        last_row_product(y2, row2, HALF)
+        for i, rows, bank in ((0, range(NT), 6), (1, range(0, 1), 0), (1, range(1, 2), 3), (1, range(2, 3), 7)):
+            sums = rows_of(bank, len(rows), P)
+            for n, row in enumerate(rows):
+                project(sums[:, n, :], w4_w, w4_s, lo3[i], row)
             res = ring.tile([P, len(rows), P], F32, name="res", bufs=4)
             tiles = slice(rows[0], rows[-1] + 1)
-            nc.vector.tensor_tensor(res[:], bank[:], y3[:, tiles, start : start + P], ALU.mult)
-            store(res[:], tiles, start)
+            nc.vector.tensor_tensor(res[:], sums, y3[i][:, tiles, :], ALU.mult)
+            store(res[:], tiles, S - CHUNK + i * P)

@@ -53,18 +53,15 @@ def tile_list_calving_retreat_features_kernel(
         w3_w = keep.tile([P, G, N], I32, name="w3_w", align_bytes=64)
         w3_s = keep.tile([P, G * N], U8, name="w3_s", align_bytes=64)
         x_plane = [keep.tile([P, T], F32, name=f"x_plane{t}") for t in range(PACK)]
-        change = keep.tile([P, 2 * PACK * HALF], F32, name="change", align_bytes=64)
+        change = keep.tile([P, (2 + PACK) * HALF], F32, name="change", align_bytes=64)
         change01 = change[:, 2 * HALF : (2 + PACK) * HALF].rearrange("p (t c) -> p t c", t=PACK)
-        change23 = change[:, PACK * HALF :].rearrange("p (t c) -> p t c", t=PACK)
+        change_late = keep.tile([P, PACK * HALF], F32, name="change_late", align_bytes=64)
+        change23 = change_late[:].rearrange("p (t c) -> p t c", t=PACK)
         w2_raw = [
             keep.tile([P, PACK, PASS], F32, name="w2_raw0")[:],
             change[:, : PACK * PASS].rearrange("p (j c) -> p j c", j=PACK),
         ]
-        w4_stage = keep.tile([P, PACK * N], F32, name="w4_stage", align_bytes=64)
-        w4_raw = [
-            w4_stage[:].rearrange("p (t n) -> p t n", t=PACK),
-            keep.tile([P, PACK, N], F32, name="w4_raw1")[:],
-        ]
+        w4_raw = [keep.tile([P, PACK, N], F32, name=f"w4_raw{g}")[:] for g in range(G)]
         w2_s = keep.tile([P, H], U8, name="w2_s", align_bytes=64)
         w4_s = keep.tile([P, G * N], U8, name="w4_s", align_bytes=64)
 
@@ -231,9 +228,10 @@ def tile_list_calving_retreat_features_kernel(
         def envelopes(c, lo):
             hi = envelope_tile("hi", CHUNK)
             for i in range(2):
-                a_woven = weave_a(2 * c + i)
-                envelope(hi, i, ALU.max, a_woven, b[2 * c + i])
-                envelope(lo, i, ALU.min, a_woven, b[2 * c + i])
+                s = 2 * c + i
+                envelope(hi, i, ALU.max, a_woven[s], b[s])
+                envelope(lo, i, ALU.min, a_woven[s], b[s])
+                a_woven.append(weave_a(s + 2))
             return hi, lo
 
         def project(target, weight, weight_s, env, row, first=0):
@@ -307,6 +305,8 @@ def tile_list_calving_retreat_features_kernel(
         for s, bank in zip(range(4, 8), (7, 3, 4, 5)):
             turn_a(s, banks[bank])
 
+        a_woven = [weave_a(s) for s in range(2)]
+
         w2_bf = keep.tile([P, PACK * H], BF16, name="w2_bf", align_bytes=64)
 
         def before_at(word):
@@ -331,9 +331,9 @@ def tile_list_calving_retreat_features_kernel(
         gather_change(change01, before1[:, :HALF], 1, 0)
         gather_change(change01, early, 0, 0)
         round_w2(nc.scalar.copy, w2_bf, 0, slice(CUTS[1], P))
+        x_bf = [change_late[:, t * HALF : (t + 1) * HALF].bitcast(BF16) for t in (1, 0)]
         w4_first = keep.tile([P, N * PACK], BF16, name="w4_first", align_bytes=64)[:]
         round_rows(w4_first, w4_raw[0])
-        x_bf = [w4_stage[:, c * HALF : (c + 1) * HALF].bitcast(BF16) for c in range(2)]
         for c in range(2):
             round_rows(x_bf[c], change01[:, :, c * CHUNK : (c + 1) * CHUNK])
         w2_w = keep.tile([P, H], U32, name="w2_w", align_bytes=64)
@@ -343,8 +343,8 @@ def tile_list_calving_retreat_features_kernel(
         w4_tail = w2_bf[:, : P * PACK]
         pool_round_rows(w4_tail, w4_raw[1][:, :, CHUNK:])
         x0 = quantize_x(x_bf[0], 0)
-        x1 = quantize_x(x_bf[1], 1)
         gather_change(change23, before1[:, HALF:], 1, HALF)
+        x1 = quantize_x(x_bf[1], 1)
         gather_change(change23, late, 0, HALF)
         b = [make_b(x0, 0, (0, 1)), make_b(x0, 1, (2, 3), "b_then_w4", 1), make_b(x1, 0, (4, 5))]
         stage = keep.tile([P, (G + 1) * CHUNK * PACK], BF16, name="stage", align_bytes=64)
@@ -383,13 +383,12 @@ def tile_list_calving_retreat_features_kernel(
 
         hi_bf = envelope_tile("hi", CHUNK)
         lo_bf = [envelope_tile("lo", P) for i in range(2)]
-        a_woven = [weave_a(6 + i) for i in range(2)]
         last_row_product(y1, row1, CHUNK)
         for i in range(2):
-            envelope(hi_bf, i, ALU.max, a_woven[i], b[6 + i])
-        envelope(lo_bf[0], 0, ALU.min, a_woven[0], b[6])
+            envelope(hi_bf, i, ALU.max, a_woven[6 + i], b[6 + i])
+        envelope(lo_bf[0], 0, ALU.min, a_woven[6], b[6])
         hi3 = quantize_envelope("hi", hi_bf)
-        envelope(lo_bf[1], 0, ALU.min, a_woven[1], b[7])
+        envelope(lo_bf[1], 0, ALU.min, a_woven[7], b[7])
         y3 = []
         for i, bank in enumerate((5, 2)):
             sums = rows_of(bank, NT, P)

@@ -89,11 +89,11 @@ def tile_list_calving_retreat_features_kernel(
         make_identity(nc, ident_bf[:])
         nc.sync.dma_start(idx[:], offs)
         nc.sync.dma_start(out=w1_w[:].bitcast(I32), in_=w1_words[0].bitcast(I32))
-        nc.sync.dma_start(out=bias_rows[:BLOCKS, :], in_=b1.rearrange("(j q) -> j q", q=P))
         for q in range(4):
             load_scale_rows(tab_s[:].bitcast(I32), tab_scales[0].bitcast(I32), q, (nc.sync, nc.scalar)[q % 2])
-        nc.sync.dma_start(out=tab_w[:], in_=tab_words[0].rearrange("p c i -> p (c i)").bitcast(I32))
         nc.sync.dma_start(idx3[:], offs3)
+        nc.sync.dma_start(out=tab_w[:], in_=tab_words[0].rearrange("p c i -> p (c i)").bitcast(I32))
+        nc.sync.dma_start(out=bias_rows[:BLOCKS, :], in_=b1.rearrange("(j q) -> j q", q=P))
         for q in range(4):
             load_scale_rows(w1_s[:].bitcast(I32), w1_scales[0].bitcast(I32), q)
         load_x(3)
@@ -120,7 +120,7 @@ def tile_list_calving_retreat_features_kernel(
             return tile[:, start // LIST_ROWS : (start + count) // LIST_ROWS]
 
         def make_a(h, j):
-            bank = banks[(h * BLOCKS + j) % 3]
+            bank = banks[j % (BLOCKS // (h + 1))]
             nc.tensor.matmul_mx(
                 out=bank[:],
                 lhsT=w1_w[:, 2 * j * P : 2 * (j + 1) * P].bitcast(E2M1),
@@ -179,10 +179,12 @@ def tile_list_calving_retreat_features_kernel(
         def pool_round_rows(rounded, rows):
             pool_round(rounded.rearrange("p (c t) -> p c t", t=PACK), rows.rearrange("p t c -> p c t"))
 
-        def quantize_x(x_bf, tag):
-            x_w = keep.tile([P, CHUNK], U32, name="x_w", tag=f"x_w{tag}", align_bytes=64)
+        def x_codes(tag):
+            return keep.tile([P, CHUNK], U32, name="x_w", tag=f"x_w{tag}", align_bytes=64)[:]
+
+        def quantize_x(x_bf, tag, x_w):
             x_s = keep.tile([P, CHUNK], U8, name="x_s", tag=f"x_s{tag}", align_bytes=64)
-            nc.vector.quantize_mx(out=x_w[:].bitcast(E4M3), scales=x_s[:], in_=x_bf)
+            nc.vector.quantize_mx(out=x_w.bitcast(E4M3), scales=x_s[:], in_=x_bf)
             return x_w, x_s
 
         def make_b(x, i, bank_pair, tag="b_bf", bufs=4):
@@ -264,22 +266,23 @@ def tile_list_calving_retreat_features_kernel(
             nc.scalar.copy(out=y[:, 0, :2, :], in_=upper)
             project(mixed[:, 0, :], w3_flat, w3_s, hi, 2)
             project(mixed[:, 1, :], w4_w, w4_s, lo, 2)
-            kept = pool_rows - 1
+            kept = 2 if pool_rows == NT else 1
             nc.scalar.copy(out=y[:, :kept, 2, :], in_=mixed[:, :kept, :])
             for row in range(2):
                 project(lower[:, row, :], w4_w, w4_s, lo, row)
-            nc.scalar.copy(out=y[:, 1, :2, :], in_=lower)
-            return y, mixed[:, 1, :]
+            kept = min(pool_rows, 2)
+            nc.scalar.copy(out=y[:, 1, :kept, :], in_=lower[:, :kept, :])
+            return y, (lower[:, 0, :], lower[:, 1, :], mixed[:, 1, :])
 
         def pool_product(env, y, rows, start, queue=nc.sync):
             res = as_result(env)[:, : rows * CHUNK].rearrange("p (n j) -> p n j", n=rows)
             nc.gpsimd.tensor_tensor(res, y[:, 0, :rows, :], y[:, 1, :rows, :], ALU.mult)
             store(res, slice(0, rows), start, queue)
 
-        def last_row_product(y, sums, start):
-            res = ring.tile([P, 1, CHUNK], F32, name="res_row")
-            nc.vector.tensor_tensor(res[:, 0, :], sums, y[:, 0, 2, :], ALU.mult)
-            store(res[:], slice(2, 3), start)
+        def row_product(y, sums, row, start):
+            res = ring.tile([P, 1, CHUNK], F32, name="res_row", bufs=3)
+            nc.vector.tensor_tensor(res[:, 0, :], sums[row], y[:, 0, row, :], ALU.mult)
+            store(res[:], slice(row, row + 1), start)
 
         def as_result(env):
             return env.rearrange("p g n t -> p (g n t)").bitcast(F32)
@@ -287,13 +290,13 @@ def tile_list_calving_retreat_features_kernel(
         def store(res, rows, start, queue=nc.sync):
             queue.dma_start(out=out_rows[:, rows, start : start + res.shape[2]], in_=res)
 
-        nc.tensor.transpose(banks[7][:, :P], bias_rows[:], ident_f32[:])
-        nc.scalar.copy(out=bias[:], in_=banks[7][:, :BLOCKS])
+        nc.tensor.transpose(banks[0][:, :P], bias_rows[:], ident_f32[:])
+        nc.scalar.copy(out=bias[:], in_=banks[0][:, :BLOCKS])
         v_s = keep.tile([P, S], U8, name="v_s", align_bytes=64)
         nc.vector.tensor_copy(v_s[:], tab_s[:].indirect(idx[:]))
         v_w = [keep.tile([P, HALF], U32, name=f"v_w{h}", align_bytes=64) for h in range(2)]
         a_rows = [keep.tile([P, BLOCKS, HALF], BF16, name=f"a_rows{h}") for h in range(2)]
-        a_turned = [keep.tile([P, H // 2], F32, name=f"a_turned{s}") for s in range(S // P)]
+        a_turned = [keep.tile([P, H // 2], F32, name=f"a_turned{s}", align_bytes=64) for s in range(S // P)]
         for h in range(2):
             nc.vector.tensor_copy(v_w[h][:], tab_w[:].bitcast(U32).indirect(offsets(idx, h * HALF, HALF)))
         for j in range(BLOCKS):
@@ -301,9 +304,9 @@ def tile_list_calving_retreat_features_kernel(
         for j in range(BLOCKS):
             make_a(1, j)
             if j % 2:
-                turn_a(j // 2, banks[3 + j // 2])
-        for s, bank in zip(range(4, 8), (7, 3, 4, 5)):
-            turn_a(s, banks[bank])
+                turn_a(j // 2, banks[4 + j // 2])
+        for s in range(4, 8):
+            turn_a(s, banks[s])
 
         a_woven = [weave_a(s) for s in range(2)]
 
@@ -342,48 +345,49 @@ def tile_list_calving_retreat_features_kernel(
         gather_before(late, 0, HALF)
         w4_tail = w2_bf[:, : P * PACK]
         pool_round_rows(w4_tail, w4_raw[1][:, :, CHUNK:])
-        x0 = quantize_x(x_bf[0], 0)
+        x0 = quantize_x(x_bf[0], 0, x_codes(0))
         gather_change(change23, before1[:, HALF:], 1, HALF)
-        x1 = quantize_x(x_bf[1], 1)
+        x1 = quantize_x(x_bf[1], 1, x_codes(1))
         gather_change(change23, late, 0, HALF)
-        b = [make_b(x0, 0, (0, 1)), make_b(x0, 1, (2, 3), "b_then_w4", 1), make_b(x1, 0, (4, 5))]
+        b = [make_b(x0, 0, (0, 1)), make_b(x0, 1, (2, 3), "b_then_codes", 1)]
         stage = keep.tile([P, (G + 1) * CHUNK * PACK], BF16, name="stage", align_bytes=64)
         first_lo = stage[:, : G * CHUNK * PACK].rearrange("p (g n t) -> p g n t", g=G, t=PACK)
         x2_bf = stage[:, G * CHUNK * PACK :]
         x3_bf = stage[:, G * CHUNK * PACK - HALF : G * CHUNK * PACK + HALF]
-        round_rows(x2_bf, change23[:, :, :CHUNK])
-        w4_head = late.bitcast(BF16)
-        pool_round_rows(w4_head, w4_raw[1][:, :, :CHUNK])
-        b.append(make_b(x1, 1, (0, 1)))
+        pool_round_rows(x2_bf, change23[:, :, :CHUNK])
+        w4_head = a_turned[2][:].bitcast(BF16)
+        b.extend([make_b(x1, 0, (4, 5)), make_b(x1, 1, (0, 1))])
 
         hi_bf, lo_bf = envelopes(0, first_lo)
+        round_rows(w4_head, w4_raw[1][:, :, :CHUNK])
+        codes = ring.tile([P, G * N + CHUNK], U32, name="codes", tag="b_then_codes", bufs=1, align_bytes=64)
+        w4_w = codes[:, : G * N]
+        x2 = quantize_x(x2_bf, 0, codes[:, G * N :])
         hi0 = quantize_envelope("hi", hi_bf)
-        w4_w = ring.tile([P, G * N], U32, name="w4_w", tag="b_then_w4", bufs=1, align_bytes=64)
         for staged, first in ((w4_first, 0), (w4_tail, N + CHUNK), (w4_head, N)):
             cols = slice(first, first + staged.shape[1] // PACK)
             nc.vector.quantize_mx(out=w4_w[:, cols].bitcast(E4M3), scales=w4_s[:, cols], in_=staged)
-        x2 = quantize_x(x2_bf, 0)
         lo0 = quantize_envelope("lo", lo_bf)
         pool_round_rows(x3_bf, change23[:, :, CHUNK:])
         b.extend([make_b(x2, 0, (2, 3)), make_b(x2, 1, (4, 5))])
         y0 = projections(hi0, lo0, (0, 1, 2), NT)[0]
 
         hi_bf, lo_bf = envelopes(1, envelope_tile("lo", CHUNK))
-        x3 = quantize_x(x3_bf, 1)
+        x3 = quantize_x(x3_bf, 1, x_codes(1))
         hi1, lo1 = quantize_envelope("hi", hi_bf), quantize_envelope("lo", lo_bf)
         pool_product(lo_bf, y0, NT, 0)
         b.append(make_b(x3, 0, (3, 4)))
-        y1, row1 = projections(hi1, lo1, (5, 0, 1), 2)
+        y1, sums1 = projections(hi1, lo1, (5, 0, 1), 2)
         b.append(make_b(x3, 1, (5, 2)))
 
         hi_bf, lo_bf = envelopes(2, envelope_tile("lo", CHUNK))
         hi2, lo2 = quantize_envelope("hi", hi_bf), quantize_envelope("lo", lo_bf)
         pool_product(lo_bf, y1, 2, CHUNK)
-        y2, row2 = projections(hi2, lo2, (3, 4, 1), 2)
+        y2, sums2 = projections(hi2, lo2, (3, 4, 1), 1)
 
         hi_bf = envelope_tile("hi", CHUNK)
         lo_bf = [envelope_tile("lo", P) for i in range(2)]
-        last_row_product(y1, row1, CHUNK)
+        row_product(y1, sums1, 2, CHUNK)
         for i in range(2):
             envelope(hi_bf, i, ALU.max, a_woven[6 + i], b[6 + i])
         envelope(lo_bf[0], 0, ALU.min, a_woven[6], b[6])
@@ -397,8 +401,9 @@ def tile_list_calving_retreat_features_kernel(
             y3.append(ring.tile([P, NT, P], F32, name="y3"))
             nc.scalar.copy(out=y3[i][:], in_=sums)
         lo3 = [quantize_envelope("lo", env) for env in lo_bf]
-        pool_product(lo_bf[1], y2, 2, HALF, nc.scalar)
-        last_row_product(y2, row2, HALF)
+        pool_product(lo_bf[1], y2, 1, HALF, nc.scalar)
+        for row in (1, 2):
+            row_product(y2, sums2, row, HALF)
         for i, rows, bank in ((0, range(NT), 6), (1, range(0, 1), 0), (1, range(1, 2), 3), (1, range(2, 3), 7)):
             sums = rows_of(bank, len(rows), P)
             for n, row in enumerate(rows):

@@ -68,8 +68,8 @@ def tile_list_calving_retreat_features_kernel(
         def load_scale_rows(plane, rows, q, queue=nc.sync):
             queue.dma_start(out=plane[q:P:32], in_=rows[q:16:4])
 
-        def load_x(t):
-            nc.sync.dma_start(out=x_plane[t][:], in_=x_rows[:, t, :])
+        def load_x(t, first=0, last=T):
+            nc.sync.dma_start(out=x_plane[t][:, first:last], in_=x_rows[:, t, first:last])
 
         def load_w2(g, first, last):
             nc.sync.dma_start(out=w2_raw[g][:, :, first:last], in_=w2_rows[:, :, g * PASS + first : g * PASS + last])
@@ -94,9 +94,10 @@ def tile_list_calving_retreat_features_kernel(
         nc.sync.dma_start(idx3[:], offs3)
         nc.sync.dma_start(out=tab_w[:], in_=tab_words[0].rearrange("p c i -> p (c i)").bitcast(I32))
         nc.sync.dma_start(out=bias_rows[:BLOCKS, :], in_=b1.rearrange("(j q) -> j q", q=P))
+        load_x(3, 0, T // 2)
         for q in range(4):
             load_scale_rows(w1_s[:].bitcast(I32), w1_scales[0].bitcast(I32), q)
-        load_x(3)
+        load_x(3, T // 2, T)
         nc.sync.dma_start(idx2[:], offs2)
         load_w2(0, 0, PASS // 2)
         load_x(2)

@@ -27,6 +27,7 @@ CHUNK = 256
 NT = N // P
 CUTS = (32, 112)
 LIST_ROWS = 16
+RUN_TILES = 4
 
 
 def tile_list_calving_retreat_features_kernel(
@@ -145,10 +146,11 @@ def tile_list_calving_retreat_features_kernel(
 
         def weave_a(s):
             bank = banks[6 + s % 2]
+            order = "(g n u)" if s < RUN_TILES else "(u g n)"
+            words = bank[:].rearrange(f"p {order} -> p u g n", g=G, u=2)
             for i in range(2 * G):
-                cols = slice(i * P, (i + 1) * P)
-                nc.tensor.transpose(bank[:, cols], a_turned[s][:, cols], ident_f32[:])
-            return bank[:].bitcast(BF16).rearrange("p (u g n e) -> p g n u e", u=2, g=G, e=2)
+                nc.tensor.transpose(words[:, i // G, i % G, :], a_turned[s][:, i * P : (i + 1) * P], ident_f32[:])
+            return bank[:].bitcast(BF16).rearrange(f"p {order[:-1]} e) -> p g n u e", u=2, g=G, e=2)
 
         def round_w2(copy, staged, g, columns):
             half = staged[:, g * PACK * PASS : (g + 1) * PACK * PASS]
@@ -370,8 +372,9 @@ def tile_list_calving_retreat_features_kernel(
             nc.vector.quantize_mx(out=w4_w[:, cols].bitcast(E4M3), scales=w4_s[:, cols], in_=staged)
         lo0 = quantize_envelope("lo", lo_bf)
         pool_round_rows(x3_bf, change23[:, :, CHUNK:])
-        b.extend([make_b(x2, 0, (2, 3)), make_b(x2, 1, (4, 5))])
-        y0 = projections(hi0, lo0, (0, 1, 2), NT)[0]
+        b.append(make_b(x2, 0, (2, 3)))
+        y0 = projections(hi0, lo0, (0, 1, 4), NT)[0]
+        b.append(make_b(x2, 1, (0, 1)))
 
         hi_bf, lo_bf = envelopes(1, envelope_tile("lo", CHUNK))
         x3 = quantize_x(x3_bf, 1, x_codes(1))

from contextlib import ExitStack

import concourse.mybir as mybir
from concourse.masks import make_identity

K, H, N, T, S = 512, 1024, 384, 2048, 1024
FLOPS = 2 * K * H * S * 2 + 2 * H * N * S * 2

F32 = mybir.dt.float32
BF16 = mybir.dt.bfloat16
I32 = mybir.dt.int32
U32 = mybir.dt.uint32
U16 = mybir.dt.uint16
U8 = mybir.dt.uint8
E4M3 = mybir.dt.float8_e4m3fn_x4
E2M1 = mybir.dt.float4_e2m1fn_x4
ALU = mybir.AluOpType
IDENTITY = mybir.ActivationFunctionType.Identity

P = 128
PACK = 4
PASS = P * PACK
G = H // PASS
BLOCKS = H // P
HALF = 512
CHUNK = 256
NT = N // P
CUTS = (32, 112)
LIST_ROWS = 16
RUN_TILES = 4


def tile_list_calving_retreat_features_kernel(
    tc, tab_words, tab_scales, offs, xT, offs2, offs3, w1_words, w1_scales, w2, b1, w3_words, w3_scales, w4, out
):
    nc = tc.nc
    with ExitStack() as ctx:
        keep = ctx.enter_context(tc.tile_pool(name="keep", bufs=1))
        ring = ctx.enter_context(tc.tile_pool(name="ring", bufs=2))
        psum = ctx.enter_context(tc.psum_pool(name="psum", bufs=1))
        banks = [psum.tile([P, HALF], F32, name=f"bank{i}") for i in range(8)]

        idx = keep.tile([P, S // LIST_ROWS], U16, name="idx")
        idx2 = keep.tile([P, S // LIST_ROWS], U16, name="idx2")
        idx3 = keep.tile([P, S // LIST_ROWS], U16, name="idx3")
        tab_w = keep.tile([P, T], I32, name="tab_w", align_bytes=64)
        tab_s = keep.tile([P, T], U8, name="tab_s", align_bytes=64)
        w1_w = keep.tile([P, 2 * H], U8, name="w1_w", align_bytes=64)
        w1_s = keep.tile([P, H], U8, name="w1_s", align_bytes=64)
        bias_rows = keep.tile([P, P], F32, name="bias_rows")
        bias = keep.tile([P, BLOCKS], F32, name="bias")
        ident_f32 = keep.tile([P, P], F32, name="ident_f32")
        ident_bf = keep.tile([P, P], BF16, name="ident_bf")
        w3_w = keep.tile([P, G, N], I32, name="w3_w", align_bytes=64)
        w3_s = keep.tile([P, G * N], U8, name="w3_s", align_bytes=64)
        x_plane = [keep.tile([P, T], F32, name=f"x_plane{t}") for t in range(PACK)]
        change = keep.tile([P, (2 + PACK) * HALF], F32, name="change", align_bytes=64)
        change01 = change[:, 2 * HALF : (2 + PACK) * HALF].rearrange("p (t c) -> p t c", t=PACK)
        change_late = keep.tile([P, PACK * HALF], F32, name="change_late", align_bytes=64)
        change23 = change_late[:].rearrange("p (t c) -> p t c", t=PACK)
        w2_raw = [
            keep.tile([P, PACK, PASS], F32, name="w2_raw0")[:],
            change[:, : PACK * PASS].rearrange("p (j c) -> p j c", j=PACK),
        ]
        w4_raw = [keep.tile([P, PACK, N], F32, name=f"w4_raw{g}")[:] for g in range(G)]
        w2_s = keep.tile([P, H], U8, name="w2_s", align_bytes=64)
        w4_s = keep.tile([P, G * N], U8, name="w4_s", align_bytes=64)

        def load_scale_rows(plane, rows, q, queue=nc.sync):
            queue.dma_start(out=plane[q:P:32], in_=rows[q:16:4])

        def load_x(t, first=0, last=T):
            nc.sync.dma_start(out=x_plane[t][:, first:last], in_=x_rows[:, t, first:last])

        def load_w2(g, first, last):
            nc.sync.dma_start(out=w2_raw[g][:, :, first:last], in_=w2_rows[:, :, g * PASS + first : g * PASS + last])

        def load_w4(g):
            nc.sync.dma_start(
                out=w4_raw[g], in_=w4[g * PASS : (g + 1) * PASS, :].rearrange("(p t) n -> p t n", t=PACK)
            )

        x_rows = xT.rearrange("(p t) c -> p t c", t=PACK)
        w2_rows = w2.rearrange("(p t) r -> p t r", t=PACK)

        nc.gpsimd.memset(tab_s[:].bitcast(I32), 0)
        nc.vector.memset(bias_rows[:], 0.0)
        nc.vector.memset(w1_s[:].bitcast(I32), 0)
        make_identity(nc, ident_f32[:])
        make_identity(nc, ident_bf[:])
        nc.sync.dma_start(idx[:], offs)
        nc.sync.dma_start(out=w1_w[:].bitcast(I32), in_=w1_words[0].bitcast(I32))
        for q in range(4):
            load_scale_rows(tab_s[:].bitcast(I32), tab_scales[0].bitcast(I32), q, (nc.sync, nc.scalar)[q % 2])
        nc.sync.dma_start(idx3[:], offs3)
        nc.sync.dma_start(out=tab_w[:], in_=tab_words[0].rearrange("p c i -> p (c i)").bitcast(I32))
        nc.sync.dma_start(out=bias_rows[:BLOCKS, :], in_=b1.rearrange("(j q) -> j q", q=P))
        load_x(3, 0, T // 2)
        for q in range(4):
            load_scale_rows(w1_s[:].bitcast(I32), w1_scales[0].bitcast(I32), q)
        load_x(3, T // 2, T)
        nc.sync.dma_start(idx2[:], offs2)
        load_w2(0, 0, PASS // 2)
        load_x(2)
        load_w2(0, PASS // 2, PASS)
        load_x(1)
        load_w2(1, 0, PASS // 2)
        load_x(0)
        load_w2(1, PASS // 2, PASS)
        for g in range(G):
            load_w4(g)
        nc.gpsimd.memset(w3_s[:].bitcast(I32), 0)
        for q in range(4):
            load_scale_rows(
                w3_s[:].bitcast(I32).rearrange("p (g n) -> p g n", g=G),
                w3_scales.bitcast(I32).rearrange("g r n -> r g n"),
                q,
            )
        nc.sync.dma_start(out=w3_w[:], in_=w3_words.rearrange("g p n i -> p g (n i)").bitcast(I32))

        def offsets(tile, start, count):
            return tile[:, start // LIST_ROWS : (start + count) // LIST_ROWS]

        def make_a(h, j):
            bank = banks[j % (BLOCKS // (h + 1))]
            nc.tensor.matmul_mx(
                out=bank[:],
                lhsT=w1_w[:, 2 * j * P : 2 * (j + 1) * P].bitcast(E2M1),
                lhsT_scale=w1_s[:, j * P : (j + 1) * P],
                rhs=v_w[h][:].bitcast(E4M3),
                rhs_scale=v_s[:, h * HALF : (h + 1) * HALF],
                start=True,
                stop=True,
            )
            nc.scalar.activation(out=a_rows[h][:, j, :], in_=bank[:], func=IDENTITY, bias=bias[:, j : j + 1])

        def turn_a(s, bank):
            h, i = divmod(s, HALF // P)
            values = bank[:].bitcast(BF16)
            for j in range(BLOCKS):
                nc.tensor.transpose(values[:, j * P : (j + 1) * P], a_rows[h][:, j, i * P : (i + 1) * P], ident_bf[:])
            nc.scalar.copy(
                out=a_turned[s][:].rearrange("n (u m) -> n u m", u=2),
                in_=bank[:].rearrange("n (m u) -> n u m", u=2),
            )

        def weave_a(s):
            bank = banks[6 + s % 2]
            order = "(g n u)" if s < RUN_TILES else "(u g n)"
            words = bank[:].rearrange(f"p {order} -> p u g n", g=G, u=2)
            for i in range(2 * G):
                nc.tensor.transpose(words[:, i // G, i % G, :], a_turned[s][:, i * P : (i + 1) * P], ident_f32[:])
            return bank[:].bitcast(BF16).rearrange(f"p {order[:-1]} e) -> p g n u e", u=2, g=G, e=2)

        def round_w2(copy, staged, g, columns):
            half = staged[:, g * PACK * PASS : (g + 1) * PACK * PASS]
            copy(
                out=half.rearrange("p (t m j) -> p m j t", t=PACK, j=PACK)[:, columns],
                in_=w2_raw[g].rearrange("p j (m t) -> p m j t", t=PACK)[:, columns],
            )

        def pool_round(out, in_):
            nc.gpsimd.tensor_scalar(out, in_, 1.0, 0.0, ALU.mult, ALU.add)

        def pool_copy(out, in_):
            order = "p m j t -> p m t j"
            pool_round(out.rearrange(order), in_.rearrange(order))

        def gather_before(before, t, start):
            nc.vector.tensor_copy(before, x_plane[t][:].indirect(offsets(idx3, start, before.shape[1])))

        def gather_change(change, before, t, start):
            picked = x_plane[t][:].indirect(offsets(idx2, start, HALF))
            nc.vector.tensor_tensor(change[:, t, :], picked, before, ALU.subtract)

        def round_rows(rounded, rows):
            nc.scalar.copy(
                out=rounded.rearrange("p (c i t) -> p c t i", i=4, t=PACK),
                in_=rows.rearrange("p t (c i) -> p c t i", i=4),
            )

        def pool_round_rows(rounded, rows):
            pool_round(rounded.rearrange("p (c t) -> p c t", t=PACK), rows.rearrange("p t c -> p c t"))

        def x_codes(tag):
            return keep.tile([P, CHUNK], U32, name="x_w", tag=f"x_w{tag}", align_bytes=64)[:]

        def quantize_x(x_bf, tag, x_w):
            x_s = keep.tile([P, CHUNK], U8, name="x_s", tag=f"x_s{tag}", align_bytes=64)
            nc.vector.quantize_mx(out=x_w.bitcast(E4M3), scales=x_s[:], in_=x_bf)
            return x_w, x_s

        def make_b(x, i, bank_pair, tag="b_bf", bufs=4):
            x_w, x_s = x
            tokens = slice(i * P, (i + 1) * P)
            b_bf = ring.tile([P, G, P, PACK], BF16, name="b_bf", tag=tag, bufs=bufs, align_bytes=64)
            for g in range(G):
                bank = banks[bank_pair[g]][:].rearrange("p (t n) -> p t n", t=PACK)
                for t in range(PACK):
                    cols = slice(g * PASS + t * P, g * PASS + (t + 1) * P)
                    nc.tensor.matmul_mx(
                        out=bank[:, t, :],
                        lhsT=w2_w[:, cols].bitcast(E4M3),
                        lhsT_scale=w2_s[:, cols],
                        rhs=x_w[:, tokens].bitcast(E4M3),
                        rhs_scale=x_s[:, tokens],
                        start=True,
                        stop=True,
                    )
                nc.scalar.copy(out=b_bf[:, g], in_=bank.rearrange("p t n -> p n t"))
            return b_bf

        def envelope_tile(name, width):
            return ring.tile([P, G, width, PACK], BF16, name=f"{name}_bf", tag=f"{name}{width}", align_bytes=64)[:]

        def envelope(env, i, op, a_woven, b_bf):
            nc.vector.tensor_tensor(
                env[:, :, i * P : (i + 1) * P, :].rearrange("p g n (u e) -> p g n u e", u=2),
                a_woven,
                b_bf[:].rearrange("p g n (u e) -> p g n u e", u=2),
                op,
            )

        def quantize_envelope(name, env):
            width = G * env.shape[2]
            env_w = ring.tile([P, width], U32, name=f"{name}_w", align_bytes=64, bufs=3)
            env_s = ring.tile([P, width], U8, name=f"{name}_s", align_bytes=64, bufs=3)
            nc.vector.quantize_mx(
                out=env_w[:].bitcast(E4M3), scales=env_s[:], in_=env.rearrange("p g n t -> p (g n t)")
            )
            return env_w, env_s

        def envelopes(c, lo):
            hi = envelope_tile("hi", CHUNK)
            for i in range(2):
                s = 2 * c + i
                envelope(hi, i, ALU.max, a_woven[s], b[s])
                envelope(lo, i, ALU.min, a_woven[s], b[s])
                a_woven.append(weave_a(s + 2))
            return hi, lo

        def project(target, weight, weight_s, env, row, first=0):
            env_w, env_s = env
            width = env_w.shape[1] // G
            for g in range(G):
                cols = slice(g * N + row * P, g * N + (row + 1) * P)
                tokens = slice(g * width + first, g * width + first + target.shape[1])
                nc.tensor.matmul_mx(
                    out=target,
                    lhsT=weight[:, cols].bitcast(E4M3),
                    lhsT_scale=weight_s[:, cols],
                    rhs=env_w[:, tokens].bitcast(E4M3),
                    rhs_scale=env_s[:, tokens],
                    start=(g == 0),
                    stop=(g == G - 1),
                )

        w3_flat = w3_w[:].rearrange("p g n -> p (g n)")
        out_rows = out.rearrange("(n p) j -> p n j", p=P)

        def rows_of(bank, count, width):
            return banks[bank][:, : count * width].rearrange("p (n j) -> p n j", n=count)

        def projections(hi, lo, bank_ids, pool_rows):
            y = ring.tile([P, 2, NT, CHUNK], F32, name="y", bufs=3)
            upper, mixed, lower = [rows_of(bank, 2, CHUNK) for bank in bank_ids]
            for row in range(2):
                project(upper[:, row, :], w3_flat, w3_s, hi, row)
            nc.scalar.copy(out=y[:, 0, :2, :], in_=upper)
            project(mixed[:, 0, :], w3_flat, w3_s, hi, 2)
            project(mixed[:, 1, :], w4_w, w4_s, lo, 2)
            kept = 2 if pool_rows == NT else 1
            nc.scalar.copy(out=y[:, :kept, 2, :], in_=mixed[:, :kept, :])
            for row in range(2):
                project(lower[:, row, :], w4_w, w4_s, lo, row)
            kept = min(pool_rows, 2)
            nc.scalar.copy(out=y[:, 1, :kept, :], in_=lower[:, :kept, :])
            return y, (lower[:, 0, :], lower[:, 1, :], mixed[:, 1, :])

        def pool_product(env, y, rows, start, queue=nc.sync):
            res = as_result(env)[:, : rows * CHUNK].rearrange("p (n j) -> p n j", n=rows)
            nc.gpsimd.tensor_tensor(res, y[:, 0, :rows, :], y[:, 1, :rows, :], ALU.mult)
            store(res, slice(0, rows), start, queue)

        def row_product(y, sums, row, start):
            res = ring.tile([P, 1, CHUNK], F32, name="res_row", bufs=3)
            nc.vector.tensor_tensor(res[:, 0, :], sums[row], y[:, 0, row, :], ALU.mult)
            store(res[:], slice(row, row + 1), start)

        def as_result(env):
            return env.rearrange("p g n t -> p (g n t)").bitcast(F32)

        def store(res, rows, start, queue=nc.sync):
            queue.dma_start(out=out_rows[:, rows, start : start + res.shape[2]], in_=res)

        nc.tensor.transpose(banks[0][:, :P], bias_rows[:], ident_f32[:])
        nc.scalar.copy(out=bias[:], in_=banks[0][:, :BLOCKS])
        v_s = keep.tile([P, S], U8, name="v_s", align_bytes=64)
        nc.vector.tensor_copy(v_s[:], tab_s[:].indirect(idx[:]))
        v_w = [keep.tile([P, HALF], U32, name=f"v_w{h}", align_bytes=64) for h in range(2)]
        a_rows = [keep.tile([P, BLOCKS, HALF], BF16, name=f"a_rows{h}") for h in range(2)]
        a_turned = [keep.tile([P, H // 2], F32, name=f"a_turned{s}", align_bytes=64) for s in range(S // P)]
        for h in range(2):
            nc.vector.tensor_copy(v_w[h][:], tab_w[:].bitcast(U32).indirect(offsets(idx, h * HALF, HALF)))
        for j in range(BLOCKS):
            make_a(0, j)
        for j in range(BLOCKS):
            make_a(1, j)
            if j % 2:
                turn_a(j // 2, banks[4 + j // 2])
        for s in range(4, 8):
            turn_a(s, banks[s])

        a_woven = [weave_a(s) for s in range(2)]

        w2_bf = keep.tile([P, PACK * H], BF16, name="w2_bf", align_bytes=64)

        def before_at(word):
            return w2_bf[:, PACK * word : PACK * word + S].bitcast(F32)

        round_w2(pool_copy, w2_bf, 0, slice(0, CUTS[0]))
        for t, word in ((3, PASS - P + CUTS[0]), (2, H - CHUNK)):
            early = ring.tile([P, HALF], F32, name="early")[:]
            late = before_at(word)
            gather_before(early, t, 0)
            gather_before(late, t, HALF)
            gather_change(change01, early, t, 0)
            gather_change(change23, late, t, HALF)
            if t == 3:
                round_w2(pool_copy, w2_bf, 0, slice(CUTS[0], CUTS[1]))
        round_w2(pool_copy, w2_bf, 1, slice(0, P // 2))
        round_w2(pool_copy, w2_bf, 1, slice(P // 2, P))
        before1 = keep.tile([P, S], F32, name="before1", align_bytes=64)[:]
        gather_before(before1, 1, 0)
        early = ring.tile([P, HALF], F32, name="early")[:]
        gather_before(early, 0, 0)
        gather_change(change01, before1[:, :HALF], 1, 0)
        gather_change(change01, early, 0, 0)
        round_w2(nc.scalar.copy, w2_bf, 0, slice(CUTS[1], P))
        x_bf = [change_late[:, t * HALF : (t + 1) * HALF].bitcast(BF16) for t in (1, 0)]
        w4_first = keep.tile([P, N * PACK], BF16, name="w4_first", align_bytes=64)[:]
        round_rows(w4_first, w4_raw[0])
        for c in range(2):
            round_rows(x_bf[c], change01[:, :, c * CHUNK : (c + 1) * CHUNK])
        w2_w = keep.tile([P, H], U32, name="w2_w", align_bytes=64)
        nc.vector.quantize_mx(out=w2_w[:].bitcast(E4M3), scales=w2_s[:], in_=w2_bf[:])
        late = before1[:, :HALF]
        gather_before(late, 0, HALF)
        w4_tail = w2_bf[:, : P * PACK]
        pool_round_rows(w4_tail, w4_raw[1][:, :, CHUNK:])
        x0 = quantize_x(x_bf[0], 0, x_codes(0))
        gather_change(change23, before1[:, HALF:], 1, HALF)
        x1 = quantize_x(x_bf[1], 1, x_codes(1))
        gather_change(change23, late, 0, HALF)
        b = [make_b(x0, 0, (0, 1)), make_b(x0, 1, (2, 3), "b_then_codes", 1)]
        stage = keep.tile([P, (G + 1) * CHUNK * PACK], BF16, name="stage", align_bytes=64)
        first_lo = stage[:, : G * CHUNK * PACK].rearrange("p (g n t) -> p g n t", g=G, t=PACK)
        x2_bf = stage[:, G * CHUNK * PACK :]
        x3_bf = stage[:, G * CHUNK * PACK - HALF : G * CHUNK * PACK + HALF]
        pool_round_rows(x2_bf, change23[:, :, :CHUNK])
        w4_head = a_turned[2][:].bitcast(BF16)
        b.extend([make_b(x1, 0, (4, 5)), make_b(x1, 1, (0, 1))])

        hi_bf, lo_bf = envelopes(0, first_lo)
        round_rows(w4_head, w4_raw[1][:, :, :CHUNK])
        codes = ring.tile([P, G * N + CHUNK], U32, name="codes", tag="b_then_codes", bufs=1, align_bytes=64)
        w4_w = codes[:, : G * N]
        x2 = quantize_x(x2_bf, 0, codes[:, G * N :])
        hi0 = quantize_envelope("hi", hi_bf)
        for staged, first in ((w4_first, 0), (w4_tail, N + CHUNK), (w4_head, N)):
            cols = slice(first, first + staged.shape[1] // PACK)
            nc.vector.quantize_mx(out=w4_w[:, cols].bitcast(E4M3), scales=w4_s[:, cols], in_=staged)
        lo0 = quantize_envelope("lo", lo_bf)
        pool_round_rows(x3_bf, change23[:, :, CHUNK:])
        b.append(make_b(x2, 0, (2, 3)))
        y0 = projections(hi0, lo0, (0, 1, 4), NT)[0]
        b.append(make_b(x2, 1, (0, 1)))

        hi_bf, lo_bf = envelopes(1, envelope_tile("lo", CHUNK))
        x3 = quantize_x(x3_bf, 1, x_codes(1))
        hi1, lo1 = quantize_envelope("hi", hi_bf), quantize_envelope("lo", lo_bf)
        pool_product(lo_bf, y0, NT, 0)
        b.append(make_b(x3, 0, (3, 4)))
        y1, sums1 = projections(hi1, lo1, (5, 0, 1), 2)
        b.append(make_b(x3, 1, (5, 2)))

        hi_bf, lo_bf = envelopes(2, envelope_tile("lo", CHUNK))
        hi2, lo2 = quantize_envelope("hi", hi_bf), quantize_envelope("lo", lo_bf)
        pool_product(lo_bf, y1, 2, CHUNK)
        y2, sums2 = projections(hi2, lo2, (3, 4, 1), 1)

        hi_bf = envelope_tile("hi", CHUNK)
        lo_bf = [envelope_tile("lo", P) for i in range(2)]
        row_product(y1, sums1, 2, CHUNK)
        for i in range(2):
            envelope(hi_bf, i, ALU.max, a_woven[6 + i], b[6 + i])
        envelope(lo_bf[0], 0, ALU.min, a_woven[6], b[6])
        hi3 = quantize_envelope("hi", hi_bf)
        envelope(lo_bf[1], 0, ALU.min, a_woven[7], b[7])
        y3 = []
        for i, bank in enumerate((5, 2)):
            sums = rows_of(bank, NT, P)
            for row in range(NT):
                project(sums[:, row, :], w3_flat, w3_s, hi3, row, i * P)
            y3.append(ring.tile([P, NT, P], F32, name="y3"))
            nc.scalar.copy(out=y3[i][:], in_=sums)
        lo3 = [quantize_envelope("lo", env) for env in lo_bf]
        pool_product(lo_bf[1], y2, 1, HALF, nc.scalar)
        for row in (1, 2):
            row_product(y2, sums2, row, HALF)
        for i, rows, bank in ((0, range(NT), 6), (1, range(0, 1), 0), (1, range(1, 2), 3), (1, range(2, 3), 7)):
            sums = rows_of(bank, len(rows), P)
            for n, row in enumerate(rows):
                project(sums[:, n, :], w4_w, w4_s, lo3[i], row)
            res = ring.tile([P, len(rows), P], F32, name="res", bufs=4)
            tiles = slice(rows[0], rows[-1] + 1)
            nc.vector.tensor_tensor(res[:], sums, y3[i][:, tiles, :], ALU.mult)
            store(res[:], tiles, S - CHUNK + i * P)
